import numpy as np
import ml_dtypes


def mxq(x, axis, fmt="e4m3"):
    dtype, down = {"e4m3": (ml_dtypes.float8_e4m3fn, 7), "e5m2": (ml_dtypes.float8_e5m2, 14)}[fmt]
    v = np.moveaxis(np.asarray(x, np.float32).astype(ml_dtypes.bfloat16).astype(np.float64), axis, -1)
    blocks = v.reshape(v.shape[:-1] + (-1, 32))
    amax = np.abs(blocks).max(-1, keepdims=True)
    byte = np.maximum(np.where(amax > 0, np.frexp(amax)[1] - 1 + 127, 0) - down, 1)
    scale = np.exp2(byte - 127.0)
    codes = (blocks / scale).astype(np.float32).astype(dtype).astype(np.float64)
    return np.moveaxis((codes * scale).reshape(v.shape), -1, axis)


WIDE = False


def mx_kscale(k):
    if not WIDE:
        return np.ones(k)
    levels = np.array([18, -18])
    if k % 512:
        return np.exp2(np.random.permutation(np.resize(levels, k // 32))).repeat(32)
    a = np.empty((k // 512, 16))
    for p in range(k // 512):
        a[p, :8] = np.random.permutation(np.resize(levels, 8))
        for g in range(8):
            far = levels[np.abs(levels - a[p, g]) >= 10]
            a[p, g + 8] = far[np.random.randint(len(far))]
    return np.exp2(a.ravel()).repeat(32)


def f64(x):
    return np.asarray(x).astype(np.float64)


def striped(idx):
    return np.tile(np.asarray(idx).reshape(-1, 16).T, (8, 1)).astype(np.uint16)


def unstriped(offs):
    return offs[:16].T.reshape(-1).astype(np.int64)

def planes(y):
    n, m = y.shape
    v = y.astype(np.float32).astype(ml_dtypes.bfloat16).astype(np.float64).reshape(n // 32, 32, m)
    top = np.abs(v).max(1)
    byte = np.clip(np.where(top > 0, np.frexp(top)[1] - 1 + 127 - 7, 1), 1, 254)
    codes = (v * np.exp2(127.0 - byte)[:, None, :]).reshape(n, m).astype(np.float32).astype(ml_dtypes.float8_e4m3fn).view(np.uint8)
    words = codes.reshape(n // 512, 128, 4, m).transpose(0, 1, 3, 2)
    return np.ascontiguousarray(words), np.ascontiguousarray(byte.astype(np.uint8).reshape(n // 512, 16, m))


def setup_inputs():
    n = np.random.standard_normal
    uni = np.random.uniform
    idx = np.random.permutation(2048)[:512]
    f_d = mx_kscale(512)
    f_f = mx_kscale(512)
    return {
        "kT": (n((512, 2048)) * f_d[:, None]).astype(np.float32),
        "vT": (n((512, 2048))).astype(np.float32),
        "W": (n((512, 512)) / np.sqrt(512) / f_d[:, None] * f_f[None, :]).astype(np.float32),
        "ts": np.tile(uni(0.75, 1.3, 2048), (128, 1)).astype(np.float32),
        "tk": np.tile(uni(0.75, 1.3, 2048), (128, 1)).astype(np.float32),
        "cf": (uni(0.75, 1.3, (512, 1)) / f_f[:, None]).astype(np.float32),
        "offs": striped(idx),
    }


def reference(kT, vT, W, ts, tk, cf, offs):
    idx = unstriped(offs)
    kT_i = f64(kT)[:, idx]
    v = f64(vT)[:, idx]
    ts_i = f64(ts)[:1][:, idx]
    tk_i = f64(tk)[:1][:, idx]
    u = mxq(f64(W), 0, "e4m3").T @ mxq(kT_i, 0, "e4m3")
    e = f64(cf) * ts_i * tk_i * (f64(cf) * tk_i * u - v)
    dk = mxq(f64(W), 1, "e4m3") @ mxq(e, 0, "e5m2")
    out_0 = np.zeros((512, 2048))
    out_0[:, idx] = dk
    return (out_0,) + planes(out_0)

@@ -1,0 +1,186 @@
+from contextlib import ExitStack
+
+import concourse.mybir as mybir
+from concourse.masks import make_identity
+
+F32 = mybir.dt.float32
+BF16 = mybir.dt.bfloat16
+I32 = mybir.dt.int32
+U32 = mybir.dt.uint32
+U16 = mybir.dt.uint16
+U8 = mybir.dt.uint8
+E4M3 = mybir.dt.float8_e4m3fn_x4
+E5M2 = mybir.dt.float8_e5m2_x4
+COPY = mybir.ActivationFunctionType.Copy
+MULT = mybir.AluOpType.mult
+SUB = mybir.AluOpType.subtract
+
+P = 128
+PACK = 4
+D = 512
+SLOTS = 512
+TOKENS = 2048
+CHUNK = 512
+
+FLOPS = 2 * 2 * D * D * SLOTS
+BYTES = 4 * (3 * D * TOKENS + D * D + 2 * TOKENS + D) + 2 * P * SLOTS // 16 + D * TOKENS + 16 * TOKENS
+
+
+def woven(tile):
+    return tile[:].rearrange("p (c i) t -> p c t i", i=4)
+
+
+def planes_walk(tile):
+    return tile[:].rearrange("p t (c i) -> p c t i", i=4)
+
+
+def quantize(nc, pool, name, grouped, fmt, tag=""):
+    codes = pool.tile([P, 512], U32, name=name + "_codes", tag=tag, align_bytes=64)
+    scales = pool.tile([P, 512], U8, name=name + "_scales", align_bytes=64)
+    nc.vector.quantize_mx(out=codes[:].bitcast(fmt), scales=scales[:], in_=grouped[:].rearrange("p c t -> p (c t)"))
+    return codes, scales
+
+
+def tile_attend_gttt_k_pl_kernel(tc, kT, vT, W, ts, tk, cf, offs, out_0, out_1, out_2):
+    nc = tc.nc
+    with ExitStack() as ctx:
+        sb = ctx.enter_context(tc.tile_pool(name="sb", bufs=1))
+        ps = ctx.enter_context(tc.psum_pool(name="ps", bufs=1))
+
+        def bank(b, name, shape):
+            return ps.tile(shape, F32, name=name, tag="bank%d" % b)
+
+        offsets = sb.tile([P, SLOTS // 16], U16, name="offsets")
+        nc.sync.dma_start(offsets[:], offs)
+        last = P - 1
+        tk_pool = sb.tile([P, TOKENS], F32, name="tk_pool")
+        ts_pool = sb.tile([P, TOKENS], F32, name="ts_pool")
+        cf_sb = sb.tile([P, PACK], F32, name="cf_sb")
+        nc.scalar.dma_start(tk_pool[last:P, :], tk[0:1, :])
+        nc.scalar.dma_start(ts_pool[last:P, :], ts[0:1, :])
+        nc.scalar.dma_start(cf_sb[:], cf.rearrange("(p j) o -> p (j o)", j=PACK))
+        w_raw = sb.tile([P, PACK, D], F32, name="w_raw")
+        nc.sync.dma_start(w_raw[:], W.rearrange("(p j) f -> p j f", j=PACK))
+        k_pool = [sb.tile([P, TOKENS], F32, name="k_pool%d" % j) for j in range(PACK)]
+        v_pool = [sb.tile([P, TOKENS], F32, name="v_pool%d" % j) for j in range(PACK)]
+        for j in range(PACK):
+            nc.sync.dma_start(k_pool[j][:], kT.rearrange("(p j) t -> p j t", j=PACK)[:, j, :])
+        for j in range(PACK):
+            nc.sync.dma_start(v_pool[j][:], vT.rearrange("(p j) t -> p j t", j=PACK)[:, j, :])
+
+        ident = sb.tile([P, P], F32, name="ident")
+        make_identity(nc, ident[:])
+
+        nc.vector.memset(tk_pool[0:last, :], 0.0)
+        nc.vector.memset(ts_pool[0:last, :], 0.0)
+        window = [sb.tile([P, TOKENS], F32, name="window%d" % j) for j in range(2)]
+        for j in range(2):
+            nc.vector.memset(window[j][:], 0.0)
+
+        w_d = sb.tile([P, D, PACK], BF16, name="w_d", tag="bf_a", align_bytes=64)
+        nc.scalar.activation(woven(w_d), planes_walk(w_raw), COPY)
+
+        w_f = sb.tile([P, D, PACK], BF16, name="w_f", tag="bf_b", align_bytes=64)
+        for j in range(PACK):
+            w_t = bank(j, "w_t%d" % j, [P, PACK, P])
+            for t in range(PACK):
+                nc.tensor.transpose(w_t[:, t, :], w_raw[:, j, t:D:PACK], ident[:])
+            nc.scalar.copy(w_f[:, P * j : P * (j + 1), :], w_t[:].rearrange("p t s -> p s t"))
+
+        tk_g = sb.tile([P, SLOTS], F32, name="tk_g")
+        ts_g = sb.tile([P, SLOTS], F32, name="ts_g")
+        nc.vector.tensor_copy(tk_g[:], tk_pool[:].indirect(offsets[:]))
+        nc.vector.tensor_copy(ts_g[:], ts_pool[:].indirect(offsets[:]))
+        tk_t = bank(4, "tk_t", [P, PACK, P])
+        ts_t = bank(5, "ts_t", [P, PACK, P])
+        for m in range(4):
+            nc.tensor.transpose(tk_t[:, m, :], tk_g[:, P * m : P * (m + 1)], ident[:])
+        for m in range(4):
+            nc.tensor.transpose(ts_t[:, m, :], ts_g[:, P * m : P * (m + 1)], ident[:])
+
+        k_bf = sb.tile([P, SLOTS, PACK], BF16, name="k_bf", tag="late_a", align_bytes=64)
+        nc.vector.tensor_copy(k_bf[:, :, 0], k_pool[0][:].indirect(offsets[:]))
+
+        tk_col = sb.tile([P, 4], F32, name="tk_col")
+        t1_col = sb.tile([P, 4], F32, name="t1_col")
+        t2_col = sb.tile([P, 4], F32, name="t2_col")
+        cf2 = sb.tile([P, PACK], F32, name="cf2")
+        nc.scalar.copy(tk_col[:], tk_t[:, :, last])
+        nc.vector.tensor_tensor(t1_col[:], ts_t[:, :, last], tk_col[:], MULT)
+        nc.vector.tensor_tensor(cf2[:], cf_sb[:], cf_sb[:], MULT)
+        wd_codes, wd_scales = quantize(nc, sb, "wd", w_d, E4M3)
+        nc.vector.tensor_tensor(t2_col[:], t1_col[:], tk_col[:], MULT)
+        t1_row = bank(6, "t1_row", [P, SLOTS])
+        for m in range(4):
+            nc.tensor.transpose(t1_row[:, P * m : P * (m + 1)], t1_col[:, m : m + 1].to_broadcast([P, P]), ident[:])
+        v_factor = [sb.tile([P, SLOTS], F32, name="v_factor%d" % t) for t in range(PACK)]
+        for t in range(PACK):
+            nc.scalar.activation(v_factor[t][:], t1_row[:], COPY, scale=cf_sb[:, t : t + 1])
+
+        nc.vector.tensor_copy(k_bf[:, :, 1], k_pool[1][:].indirect(offsets[:]))
+        wf_codes, wf_scales = quantize(nc, sb, "wf", w_f, E4M3)
+        for j in range(2, PACK):
+            nc.vector.tensor_copy(k_bf[:, :, j], k_pool[j][:].indirect(offsets[:]))
+        k_codes, k_scales = quantize(nc, sb, "k", k_bf, E4M3, "late_b")
+        v_term = [sb.tile([P, SLOTS], F32, name="v_term%d" % t) for t in range(PACK)]
+
+        u_back = [bank(4 + r, "u_back%d" % r, [P, SLOTS]) for r in range(PACK)]
+        for m in range(4):
+            cols = slice(P * m, P * (m + 1))
+            u_t = bank(m, "u_t%d" % m, [P, D])
+            nc.tensor.matmul_mx(u_t[:], lhsT=k_codes[:, cols].bitcast(E4M3), lhsT_scale=k_scales[:, cols],
+                                rhs=wd_codes[:].bitcast(E4M3), rhs_scale=wd_scales[:], start=True, stop=True)
+            u_s = sb.tile([P, PACK, P], F32, name="u_s%d" % m, tag="f32_%d" % m)
+            nc.scalar.activation(u_s[:], u_t[:].rearrange("p (s r) -> p r s", r=PACK), COPY, scale=t2_col[:, m : m + 1])
+            for r in range(PACK):
+                nc.tensor.transpose(u_back[r][:, cols], u_s[:, r, :], ident[:])
+
+        e_planes = sb.tile([P, PACK, SLOTS], BF16, name="e_planes", tag="bf_d", align_bytes=64)
+        for j, tag in ((2, "late_a"), (3, "late_b")):
+            window.append(sb.tile([P, TOKENS], F32, name="window%d" % j, tag=tag, align_bytes=64))
+            nc.gpsimd.memset(window[j][:], 0.0)
+        for t in range(PACK + 1):
+            if t < PACK:
+                nc.vector.tensor_tensor(v_term[t][:], v_pool[t][:].indirect(offsets[:]), v_factor[t][:], MULT)
+            if t > 0:
+                r = t - 1
+                nc.vector.scalar_tensor_tensor(e_planes[:, r, :], u_back[r][:], cf2[:, r : r + 1], v_term[r][:], MULT, SUB)
+        e_bf = sb.tile([P, SLOTS, PACK], BF16, name="e_bf", align_bytes=64)
+        cut = 352 // 4
+        nc.vector.tensor_copy(woven(e_bf)[:, :cut], planes_walk(e_planes)[:, :cut])
+        nc.scalar.copy(woven(e_bf)[:, cut:], planes_walk(e_planes)[:, cut:])
+        e_codes, e_scales = quantize(nc, sb, "e", e_bf, E5M2)
+
+        n_chunks = TOKENS // CHUNK
+        pairs = [sb.tile([P, 2, CHUNK, 2], BF16, name="pairs%d" % c, align_bytes=64) for c in range(n_chunks)]
+        dk_sb = []
+        for j in range(PACK):
+            cols = slice(P * j, P * (j + 1))
+            dk = bank(j, "dk%d" % j, [P, SLOTS])
+            nc.tensor.matmul_mx(dk[:], lhsT=wf_codes[:, cols].bitcast(E4M3), lhsT_scale=wf_scales[:, cols],
+                                rhs=e_codes[:].bitcast(E5M2), rhs_scale=e_scales[:], start=True, stop=True)
+            dk_sb.append(sb.tile([P, SLOTS], F32, name="dk_sb%d" % j, tag="f32_%d" % j))
+            nc.scalar.copy(dk_sb[j][:], dk[:])
+        for j in range(PACK):
+            nc.vector.tensor_copy(window[j][:].indirect(offsets[:]), dk_sb[j][:])
+            nc.sync.dma_start(out_0.rearrange("(p j) t -> p j t", j=PACK)[:, j, :], window[j][:])
+            for c in range(n_chunks):
+                nc.scalar.copy(pairs[c][:, j // 2, :, j % 2], window[j][:, CHUNK * c : CHUNK * (c + 1)])
+
+        words_out = out_1[0].rearrange("p c l -> p (c l)").bitcast(I32)
+        y_scales = sb.tile([P, TOKENS], U8, name="y_scales", align_bytes=64)
+        for c in range(n_chunks):
+            cols = slice(CHUNK * c, CHUNK * (c + 1))
+            y_bf = sb.tile([P, CHUNK, PACK], BF16, name="y_bf%d" % c, tag="bf_" + "abcd"[c], align_bytes=64)
+            y_words = y_bf[:].rearrange("p c t -> p (c t)").bitcast(F32).rearrange("p (c i u) -> p c u i", i=4, u=2)
+            pair_words = pairs[c][:].rearrange("p u c e -> p u (c e)").bitcast(F32).rearrange("p u (c i) -> p c u i", i=4)
+            if c == n_chunks - 1:
+                nc.scalar.copy(y_words, pair_words)
+            else:
+                nc.vector.tensor_copy(y_words, pair_words)
+            y_codes = sb.tile([P, CHUNK], U32, name="y_codes%d" % c, align_bytes=64)
+            nc.vector.quantize_mx(out=y_codes[:].bitcast(E4M3), scales=y_scales[:, cols], in_=y_bf[:].rearrange("p c t -> p (c t)"))
+            nc.sync.dma_start(words_out[:, cols], y_codes[:].bitcast(I32))
+        for q in range(4):
+            queue = nc.sync if q % 2 == 0 else nc.scalar
+            queue.dma_start(out_2[0].bitcast(I32)[4 * q : 4 * q + 4, :], y_scales[32 * q : 32 * q + 4, :].bitcast(I32))

@@ -51,7 +51,6 @@ def tile_attend_gttt_k_pl_kernel(tc, kT, vT, W, ts, tk, cf, offs, out_0, out_1, 
             return ps.tile(shape, F32, name=name, tag="bank%d" % b)
 
         offsets = sb.tile([P, SLOTS // 16], U16, name="offsets")
-        nc.sync.dma_start(offsets[:], offs)
         last = P - 1
         tk_pool = sb.tile([P, TOKENS], F32, name="tk_pool")
         ts_pool = sb.tile([P, TOKENS], F32, name="ts_pool")
@@ -61,6 +60,7 @@ def tile_attend_gttt_k_pl_kernel(tc, kT, vT, W, ts, tk, cf, offs, out_0, out_1, 
         nc.scalar.dma_start(cf_sb[:], cf.rearrange("(p j) o -> p (j o)", j=PACK))
         w_raw = sb.tile([P, PACK, D], F32, name="w_raw")
         nc.sync.dma_start(w_raw[:], W.rearrange("(p j) f -> p j f", j=PACK))
+        nc.sync.dma_start(offsets[:], offs)
         k_pool = [sb.tile([P, TOKENS], F32, name="k_pool%d" % j) for j in range(PACK)]
         v_pool = [sb.tile([P, TOKENS], F32, name="v_pool%d" % j) for j in range(PACK)]
         for j in range(PACK):
@@ -73,9 +73,8 @@ def tile_attend_gttt_k_pl_kernel(tc, kT, vT, W, ts, tk, cf, offs, out_0, out_1, 
 
         nc.vector.memset(tk_pool[0:last, :], 0.0)
         nc.vector.memset(ts_pool[0:last, :], 0.0)
-        window = [sb.tile([P, TOKENS], F32, name="window%d" % j) for j in range(2)]
-        for j in range(2):
-            nc.vector.memset(window[j][:], 0.0)
+        window = [sb.tile([P, TOKENS], F32, name="window0")]
+        nc.gpsimd.memset(window[0][:], 0.0)
 
         w_d = sb.tile([P, D, PACK], BF16, name="w_d", tag="bf_a", align_bytes=64)
         nc.scalar.activation(woven(w_d), planes_walk(w_raw), COPY)
@@ -108,7 +107,7 @@ def tile_attend_gttt_k_pl_kernel(tc, kT, vT, W, ts, tk, cf, offs, out_0, out_1, 
         nc.scalar.copy(tk_col[:], tk_t[:, :, last])
         nc.vector.tensor_tensor(t1_col[:], ts_t[:, :, last], tk_col[:], MULT)
         nc.vector.tensor_tensor(cf2[:], cf_sb[:], cf_sb[:], MULT)
-        wd_codes, wd_scales = quantize(nc, sb, "wd", w_d, E4M3)
+        wd_codes, wd_scales = quantize(nc, sb, "wd", w_d, E4M3, "late_c")
         nc.vector.tensor_tensor(t2_col[:], t1_col[:], tk_col[:], MULT)
         t1_row = bank(6, "t1_row", [P, SLOTS])
         for m in range(4):
@@ -122,33 +121,30 @@ def tile_attend_gttt_k_pl_kernel(tc, kT, vT, W, ts, tk, cf, offs, out_0, out_1, 
         for j in range(2, PACK):
             nc.vector.tensor_copy(k_bf[:, :, j], k_pool[j][:].indirect(offsets[:]))
         k_codes, k_scales = quantize(nc, sb, "k", k_bf, E4M3, "late_b")
-        v_term = [sb.tile([P, SLOTS], F32, name="v_term%d" % t) for t in range(PACK)]
+        v_term = sb.tile([P, PACK, SLOTS], F32, name="v_term")
 
-        u_back = [bank(4 + r, "u_back%d" % r, [P, SLOTS]) for r in range(PACK)]
+        u_s = []
         for m in range(4):
             cols = slice(P * m, P * (m + 1))
             u_t = bank(m, "u_t%d" % m, [P, D])
             nc.tensor.matmul_mx(u_t[:], lhsT=k_codes[:, cols].bitcast(E4M3), lhsT_scale=k_scales[:, cols],
                                 rhs=wd_codes[:].bitcast(E4M3), rhs_scale=wd_scales[:], start=True, stop=True)
-            u_s = sb.tile([P, PACK, P], F32, name="u_s%d" % m, tag="f32_%d" % m)
-            nc.scalar.activation(u_s[:], u_t[:].rearrange("p (s r) -> p r s", r=PACK), COPY, scale=t2_col[:, m : m + 1])
-            for r in range(PACK):
-                nc.tensor.transpose(u_back[r][:, cols], u_s[:, r, :], ident[:])
+            u_s.append(sb.tile([P, PACK, P], F32, name="u_s%d" % m, tag="f32_%d" % m))
+            nc.scalar.activation(u_s[m][:], u_t[:].rearrange("p (s r) -> p r s", r=PACK), COPY, scale=t2_col[:, m : m + 1])
+        u_term = sb.tile([P, PACK, SLOTS], F32, name="u_term")
+        for r in range(PACK):
+            u_back = bank(4 + r, "u_back%d" % r, [P, SLOTS])
+            for m in range(4):
+                nc.tensor.transpose(u_back[:, P * m : P * (m + 1)], u_s[m][:, r, :], ident[:])
+            nc.scalar.activation(u_term[:, r, :], u_back[:], COPY, scale=cf2[:, r : r + 1])
 
-        e_planes = sb.tile([P, PACK, SLOTS], BF16, name="e_planes", tag="bf_d", align_bytes=64)
-        for j, tag in ((2, "late_a"), (3, "late_b")):
+        for j, tag in ((1, "late_a"), (2, "late_b"), (3, "late_c")):
             window.append(sb.tile([P, TOKENS], F32, name="window%d" % j, tag=tag, align_bytes=64))
             nc.gpsimd.memset(window[j][:], 0.0)
-        for t in range(PACK + 1):
-            if t < PACK:
-                nc.vector.tensor_tensor(v_term[t][:], v_pool[t][:].indirect(offsets[:]), v_factor[t][:], MULT)
-            if t > 0:
-                r = t - 1
-                nc.vector.scalar_tensor_tensor(e_planes[:, r, :], u_back[r][:], cf2[:, r : r + 1], v_term[r][:], MULT, SUB)
+        for t in range(PACK):
+            nc.vector.tensor_tensor(v_term[:, t, :], v_pool[t][:].indirect(offsets[:]), v_factor[t][:], MULT)
         e_bf = sb.tile([P, SLOTS, PACK], BF16, name="e_bf", align_bytes=64)
-        cut = 352 // 4
-        nc.vector.tensor_copy(woven(e_bf)[:, :cut], planes_walk(e_planes)[:, :cut])
-        nc.scalar.copy(woven(e_bf)[:, cut:], planes_walk(e_planes)[:, cut:])
+        nc.vector.tensor_tensor(woven(e_bf), planes_walk(u_term), planes_walk(v_term), SUB)
         e_codes, e_scales = quantize(nc, sb, "e", e_bf, E5M2)
 
         n_chunks = TOKENS // CHUNK
@@ -164,23 +160,36 @@ def tile_attend_gttt_k_pl_kernel(tc, kT, vT, W, ts, tk, cf, offs, out_0, out_1, 
         for j in range(PACK):
             nc.vector.tensor_copy(window[j][:].indirect(offsets[:]), dk_sb[j][:])
             nc.sync.dma_start(out_0.rearrange("(p j) t -> p j t", j=PACK)[:, j, :], window[j][:])
-            for c in range(n_chunks):
+            for c in range(j // 2, n_chunks):
                 nc.scalar.copy(pairs[c][:, j // 2, :, j % 2], window[j][:, CHUNK * c : CHUNK * (c + 1)])
+        for j in (2, 3):
+            nc.vector.tensor_copy(pairs[0][:, 1, :, j % 2], window[j][:, :CHUNK])
 
         words_out = out_1[0].rearrange("p c l -> p (c l)").bitcast(I32)
         y_scales = sb.tile([P, TOKENS], U8, name="y_scales", align_bytes=64)
-        for c in range(n_chunks):
-            cols = slice(CHUNK * c, CHUNK * (c + 1))
-            y_bf = sb.tile([P, CHUNK, PACK], BF16, name="y_bf%d" % c, tag="bf_" + "abcd"[c], align_bytes=64)
-            y_words = y_bf[:].rearrange("p c t -> p (c t)").bitcast(F32).rearrange("p (c i u) -> p c u i", i=4, u=2)
+        y_bf = [sb.tile([P, CHUNK, PACK], BF16, name="y_bf%d" % c, tag="bf_" + "abcd"[c], align_bytes=64) for c in range(n_chunks)]
+        vector_groups = (128, 128, 64, 0)
+
+        def weave(c):
+            y_words = y_bf[c][:].rearrange("p c t -> p (c t)").bitcast(F32).rearrange("p (c i u) -> p c u i", i=4, u=2)
             pair_words = pairs[c][:].rearrange("p u c e -> p u (c e)").bitcast(F32).rearrange("p u (c i) -> p c u i", i=4)
-            if c == n_chunks - 1:
-                nc.scalar.copy(y_words, pair_words)
-            else:
-                nc.vector.tensor_copy(y_words, pair_words)
+            g = vector_groups[c]
+            if g > 0:
+                nc.vector.tensor_copy(y_words[:, :g], pair_words[:, :g])
+            if g < CHUNK // 4:
+                nc.scalar.copy(y_words[:, g:], pair_words[:, g:])
+
+        def hand_on(c):
+            cols = slice(CHUNK * c, CHUNK * (c + 1))
             y_codes = sb.tile([P, CHUNK], U32, name="y_codes%d" % c, align_bytes=64)
-            nc.vector.quantize_mx(out=y_codes[:].bitcast(E4M3), scales=y_scales[:, cols], in_=y_bf[:].rearrange("p c t -> p (c t)"))
+            nc.vector.quantize_mx(out=y_codes[:].bitcast(E4M3), scales=y_scales[:, cols], in_=y_bf[c][:].rearrange("p c t -> p (c t)"))
             nc.sync.dma_start(words_out[:, cols], y_codes[:].bitcast(I32))
+
+        for c in range(n_chunks + 1):
+            if c < n_chunks:
+                weave(c)
+            if c > 0:
+                hand_on(c - 1)
         for q in range(4):
             queue = nc.sync if q % 2 == 0 else nc.scalar
             queue.dma_start(out_2[0].bitcast(I32)[4 * q : 4 * q + 4, :], y_scales[32 * q : 32 * q + 4, :].bitcast(I32))

@@ -61,7 +61,7 @@ def tile_attend_gttt_k_pl_kernel(tc, kT, vT, W, ts, tk, cf, offs, out_0, out_1, 
         w_raw = sb.tile([P, PACK, D], F32, name="w_raw")
         nc.sync.dma_start(w_raw[:], W.rearrange("(p j) f -> p j f", j=PACK))
         nc.sync.dma_start(offsets[:], offs)
-        k_pool = [sb.tile([P, TOKENS], F32, name="k_pool%d" % j) for j in range(PACK)]
+        k_pool = [sb.tile([P, TOKENS], F32, name="k_pool%d" % j, tag="k_pool%d" % j, align_bytes=64) for j in range(PACK)]
         v_pool = [sb.tile([P, TOKENS], F32, name="v_pool%d" % j) for j in range(PACK)]
         for j in range(PACK):
             nc.sync.dma_start(k_pool[j][:], kT.rearrange("(p j) t -> p j t", j=PACK)[:, j, :])
@@ -76,15 +76,10 @@ def tile_attend_gttt_k_pl_kernel(tc, kT, vT, W, ts, tk, cf, offs, out_0, out_1, 
         window = [sb.tile([P, TOKENS], F32, name="window0")]
         nc.gpsimd.memset(window[0][:], 0.0)
 
-        w_d = sb.tile([P, D, PACK], BF16, name="w_d", tag="bf_a", align_bytes=64)
-        nc.scalar.activation(woven(w_d), planes_walk(w_raw), COPY)
-
-        w_f = sb.tile([P, D, PACK], BF16, name="w_f", tag="bf_b", align_bytes=64)
-        for j in range(PACK):
-            w_t = bank(j, "w_t%d" % j, [P, PACK, P])
-            for t in range(PACK):
-                nc.tensor.transpose(w_t[:, t, :], w_raw[:, j, t:D:PACK], ident[:])
-            nc.scalar.copy(w_f[:, P * j : P * (j + 1), :], w_t[:].rearrange("p t s -> p s t"))
+        w_d = sb.tile([P, D, PACK], BF16, name="w_d", align_bytes=64)
+        nc.scalar.activation(
+            w_d[:].rearrange("p (t m) j -> p m t j", t=PACK), w_raw[:].rearrange("p j (m t) -> p m t j", t=PACK), COPY
+        )
 
         tk_g = sb.tile([P, SLOTS], F32, name="tk_g")
         ts_g = sb.tile([P, SLOTS], F32, name="ts_g")
@@ -97,18 +92,30 @@ def tile_attend_gttt_k_pl_kernel(tc, kT, vT, W, ts, tk, cf, offs, out_0, out_1, 
         for m in range(4):
             nc.tensor.transpose(ts_t[:, m, :], ts_g[:, P * m : P * (m + 1)], ident[:])
 
-        k_bf = sb.tile([P, SLOTS, PACK], BF16, name="k_bf", tag="late_a", align_bytes=64)
-        nc.vector.tensor_copy(k_bf[:, :, 0], k_pool[0][:].indirect(offsets[:]))
-
         tk_col = sb.tile([P, 4], F32, name="tk_col")
+        ts_col = sb.tile([P, 4], F32, name="ts_col")
         t1_col = sb.tile([P, 4], F32, name="t1_col")
         t2_col = sb.tile([P, 4], F32, name="t2_col")
         cf2 = sb.tile([P, PACK], F32, name="cf2")
         nc.scalar.copy(tk_col[:], tk_t[:, :, last])
-        nc.vector.tensor_tensor(t1_col[:], ts_t[:, :, last], tk_col[:], MULT)
-        nc.vector.tensor_tensor(cf2[:], cf_sb[:], cf_sb[:], MULT)
+        nc.scalar.copy(ts_col[:], ts_t[:, :, last])
+        nc.gpsimd.tensor_tensor(cf2[:], cf_sb[:], cf_sb[:], MULT)
+        nc.gpsimd.tensor_tensor(t1_col[:], ts_col[:], tk_col[:], MULT)
+        nc.gpsimd.tensor_tensor(t2_col[:], t1_col[:], tk_col[:], MULT)
+
+        w_f = sb.tile([P, PACK, P, PACK], BF16, name="w_f", align_bytes=64)
+        w_words = w_d[:].rearrange("p c j -> p (c j)").bitcast(F32).rearrange("p (t m u) -> p t u m", t=PACK, u=2)
+        for u in range(2):
+            w_t = bank(u, "w_t%d" % u, [P, PACK, P])
+            for t in range(PACK):
+                nc.tensor.transpose(w_t[:, t, :], w_words[:, t, u, :], ident[:])
+            halves = w_t[:].rearrange("p t s -> p (t s)").bitcast(BF16).rearrange("p (t s e) -> p e s t", t=PACK, e=2)
+            nc.scalar.copy(w_f[:, 2 * u : 2 * u + 2, :, :], halves)
+
+        k_bf = sb.tile([P, SLOTS, PACK], BF16, name="k_bf", tag="late_a", align_bytes=64)
+        nc.vector.tensor_copy(k_bf[:, :, 0], k_pool[0][:].indirect(offsets[:]))
+
         wd_codes, wd_scales = quantize(nc, sb, "wd", w_d, E4M3, "late_c")
-        nc.vector.tensor_tensor(t2_col[:], t1_col[:], tk_col[:], MULT)
         t1_row = bank(6, "t1_row", [P, SLOTS])
         for m in range(4):
             nc.tensor.transpose(t1_row[:, P * m : P * (m + 1)], t1_col[:, m : m + 1].to_broadcast([P, P]), ident[:])
@@ -117,9 +124,9 @@ def tile_attend_gttt_k_pl_kernel(tc, kT, vT, W, ts, tk, cf, offs, out_0, out_1, 
             nc.scalar.activation(v_factor[t][:], t1_row[:], COPY, scale=cf_sb[:, t : t + 1])
 
         nc.vector.tensor_copy(k_bf[:, :, 1], k_pool[1][:].indirect(offsets[:]))
-        wf_codes, wf_scales = quantize(nc, sb, "wf", w_f, E4M3)
-        for j in range(2, PACK):
-            nc.vector.tensor_copy(k_bf[:, :, j], k_pool[j][:].indirect(offsets[:]))
+        nc.vector.tensor_copy(k_bf[:, :, 2], k_pool[2][:].indirect(offsets[:]))
+        wf_codes, wf_scales = quantize(nc, sb, "wf", w_f[:].rearrange("p j s t -> p (j s) t"), E4M3, "k_pool2")
+        nc.vector.tensor_copy(k_bf[:, :, 3], k_pool[3][:].indirect(offsets[:]))
         k_codes, k_scales = quantize(nc, sb, "k", k_bf, E4M3, "late_b")
         v_term = sb.tile([P, PACK, SLOTS], F32, name="v_term")
 
@@ -130,7 +137,7 @@ def tile_attend_gttt_k_pl_kernel(tc, kT, vT, W, ts, tk, cf, offs, out_0, out_1, 
             nc.tensor.matmul_mx(u_t[:], lhsT=k_codes[:, cols].bitcast(E4M3), lhsT_scale=k_scales[:, cols],
                                 rhs=wd_codes[:].bitcast(E4M3), rhs_scale=wd_scales[:], start=True, stop=True)
             u_s.append(sb.tile([P, PACK, P], F32, name="u_s%d" % m, tag="f32_%d" % m))
-            nc.scalar.activation(u_s[m][:], u_t[:].rearrange("p (s r) -> p r s", r=PACK), COPY, scale=t2_col[:, m : m + 1])
+            nc.scalar.activation(u_s[m][:].rearrange("p r s -> p (r s)"), u_t[:], COPY, scale=t2_col[:, m : m + 1])
         u_term = sb.tile([P, PACK, SLOTS], F32, name="u_term")
         for r in range(PACK):
             u_back = bank(4 + r, "u_back%d" % r, [P, SLOTS])
@@ -141,14 +148,27 @@ def tile_attend_gttt_k_pl_kernel(tc, kT, vT, W, ts, tk, cf, offs, out_0, out_1, 
         for j, tag in ((1, "late_a"), (2, "late_b"), (3, "late_c")):
             window.append(sb.tile([P, TOKENS], F32, name="window%d" % j, tag=tag, align_bytes=64))
             nc.gpsimd.memset(window[j][:], 0.0)
-        for t in range(PACK):
+        for t in range(PACK - 1):
             nc.vector.tensor_tensor(v_term[:, t, :], v_pool[t][:].indirect(offsets[:]), v_factor[t][:], MULT)
+        half = SLOTS // 2
+        t = PACK - 1
+        for h in range(2):
+            cols = slice(half * h, half * (h + 1))
+            listed = offsets[:, half // 16 * h : half // 16 * (h + 1)]
+            nc.vector.tensor_tensor(v_term[:, t, cols], v_pool[t][:].indirect(listed), v_factor[t][:, cols], MULT)
         e_bf = sb.tile([P, SLOTS, PACK], BF16, name="e_bf", align_bytes=64)
-        nc.vector.tensor_tensor(woven(e_bf), planes_walk(u_term), planes_walk(v_term), SUB)
-        e_codes, e_scales = quantize(nc, sb, "e", e_bf, E5M2)
+        for h in range(2):
+            groups = slice(half // 4 * h, half // 4 * (h + 1))
+            nc.vector.tensor_tensor(woven(e_bf)[:, groups], planes_walk(u_term)[:, groups], planes_walk(v_term)[:, groups], SUB)
+        e_codes = sb.tile([P, SLOTS], U32, name="e_codes", align_bytes=64)
+        e_scales = sb.tile([P, SLOTS], U8, name="e_scales", align_bytes=64)
+        for h in range(2):
+            cols = slice(half * h, half * (h + 1))
+            nc.vector.quantize_mx(out=e_codes[:, cols].bitcast(E5M2), scales=e_scales[:, cols], in_=e_bf[:, cols, :].rearrange("p c t -> p (c t)"))
 
-        n_chunks = TOKENS // CHUNK
-        pairs = [sb.tile([P, 2, CHUNK, 2], BF16, name="pairs%d" % c, align_bytes=64) for c in range(n_chunks)]
+        bounds = (0, 512, 1024, 1536, 1792, 2048)
+        chunks = [slice(a, b) for a, b in zip(bounds[:-1], bounds[1:])]
+        pairs = [sb.tile([P, 2, c.stop - c.start, 2], BF16, name="pairs%d" % c.start, align_bytes=64) for c in chunks]
         dk_sb = []
         for j in range(PACK):
             cols = slice(P * j, P * (j + 1))
@@ -160,36 +180,37 @@ def tile_attend_gttt_k_pl_kernel(tc, kT, vT, W, ts, tk, cf, offs, out_0, out_1, 
         for j in range(PACK):
             nc.vector.tensor_copy(window[j][:].indirect(offsets[:]), dk_sb[j][:])
             nc.sync.dma_start(out_0.rearrange("(p j) t -> p j t", j=PACK)[:, j, :], window[j][:])
-            for c in range(j // 2, n_chunks):
-                nc.scalar.copy(pairs[c][:, j // 2, :, j % 2], window[j][:, CHUNK * c : CHUNK * (c + 1)])
+            for c in range(j // 2, len(chunks)):
+                nc.scalar.copy(pairs[c][:, j // 2, :, j % 2], window[j][:, chunks[c]])
         for j in (2, 3):
-            nc.vector.tensor_copy(pairs[0][:, 1, :, j % 2], window[j][:, :CHUNK])
+            nc.vector.tensor_copy(pairs[0][:, 1, :, j % 2], window[j][:, chunks[0]])
 
         words_out = out_1[0].rearrange("p c l -> p (c l)").bitcast(I32)
         y_scales = sb.tile([P, TOKENS], U8, name="y_scales", align_bytes=64)
-        y_bf = [sb.tile([P, CHUNK, PACK], BF16, name="y_bf%d" % c, tag="bf_" + "abcd"[c], align_bytes=64) for c in range(n_chunks)]
-        vector_groups = (128, 128, 64, 0)
+        y_bf = [sb.tile([P, c.stop - c.start, PACK], BF16, name="y_bf%d" % c.start, align_bytes=64) for c in chunks]
+        vector_stop = 1408
 
         def weave(c):
             y_words = y_bf[c][:].rearrange("p c t -> p (c t)").bitcast(F32).rearrange("p (c i u) -> p c u i", i=4, u=2)
             pair_words = pairs[c][:].rearrange("p u c e -> p u (c e)").bitcast(F32).rearrange("p u (c i) -> p c u i", i=4)
-            g = vector_groups[c]
+            width = chunks[c].stop - chunks[c].start
+            g = min(max(vector_stop - chunks[c].start, 0), width) // 4
             if g > 0:
                 nc.vector.tensor_copy(y_words[:, :g], pair_words[:, :g])
-            if g < CHUNK // 4:
+            if g < width // 4:
                 nc.scalar.copy(y_words[:, g:], pair_words[:, g:])
 
         def hand_on(c):
-            cols = slice(CHUNK * c, CHUNK * (c + 1))
-            y_codes = sb.tile([P, CHUNK], U32, name="y_codes%d" % c, align_bytes=64)
+            cols = chunks[c]
+            y_codes = sb.tile([P, cols.stop - cols.start], U32, name="y_codes%d" % c, align_bytes=64)
             nc.vector.quantize_mx(out=y_codes[:].bitcast(E4M3), scales=y_scales[:, cols], in_=y_bf[c][:].rearrange("p c t -> p (c t)"))
             nc.sync.dma_start(words_out[:, cols], y_codes[:].bitcast(I32))
 
-        for c in range(n_chunks + 1):
-            if c < n_chunks:
+        for c in range(len(chunks) + 1):
+            if c < len(chunks):
                 weave(c)
             if c > 0:
                 hand_on(c - 1)
         for q in range(4):
-            queue = nc.sync if q % 2 == 0 else nc.scalar
+            queue = nc.sync if q == 3 else nc.scalar
             queue.dma_start(out_2[0].bitcast(I32)[4 * q : 4 * q + 4, :], y_scales[32 * q : 32 * q + 4, :].bitcast(I32))

@@ -16,29 +16,30 @@ MULT = mybir.AluOpType.mult
 SUB = mybir.AluOpType.subtract
 
 P = 128
-PACK = 4
+LANES = 4
 D = 512
 SLOTS = 512
 TOKENS = 2048
-CHUNK = 512
+SLOT_TILES = SLOTS // P
+HALF = SLOTS // 2
+RUN = 4
+PER_COLUMN = 16
+ROW = P - 1
+
+CHUNKS = [slice(0, 512), slice(512, 1024), slice(1024, 1536), slice(1536, 1792), slice(1792, 2048)]
+VECTOR_ROUNDS = 256
+VECTOR_WEAVES = 1408
 
 FLOPS = 2 * 2 * D * D * SLOTS
-BYTES = 4 * (3 * D * TOKENS + D * D + 2 * TOKENS + D) + 2 * P * SLOTS // 16 + D * TOKENS + 16 * TOKENS
+BYTES = 4 * (3 * D * TOKENS + D * D + 2 * TOKENS + D) + 2 * P * SLOTS // PER_COLUMN + D * TOKENS + D // 32 * TOKENS
 
 
-def woven(tile):
-    return tile[:].rearrange("p (c i) t -> p c t i", i=4)
+def half(h, per=1):
+    return slice(HALF // per * h, HALF // per * (h + 1))
 
 
-def planes_walk(tile):
-    return tile[:].rearrange("p t (c i) -> p c t i", i=4)
-
-
-def quantize(nc, pool, name, grouped, fmt, tag=""):
-    codes = pool.tile([P, 512], U32, name=name + "_codes", tag=tag, align_bytes=64)
-    scales = pool.tile([P, 512], U8, name=name + "_scales", align_bytes=64)
-    nc.vector.quantize_mx(out=codes[:].bitcast(fmt), scales=scales[:], in_=grouped[:].rearrange("p c t -> p (c t)"))
-    return codes, scales
+def quantize(nc, codes, scales, grouped, fmt):
+    nc.vector.quantize_mx(out=codes.bitcast(fmt), scales=scales, in_=grouped.rearrange("p c t -> p (c t)"))
 
 
 def tile_attend_gttt_k_pl_kernel(tc, kT, vT, W, ts, tk, cf, offs, out_0, out_1, out_2):
@@ -50,167 +51,180 @@ def tile_attend_gttt_k_pl_kernel(tc, kT, vT, W, ts, tk, cf, offs, out_0, out_1, 
         def bank(b, name, shape):
             return ps.tile(shape, F32, name=name, tag="bank%d" % b)
 
-        offsets = sb.tile([P, SLOTS // 16], U16, name="offsets")
-        last = P - 1
+        def operand(name, tag=""):
+            codes = sb.tile([P, 512], U32, name=name + "_codes", tag=tag, align_bytes=64)
+            scales = sb.tile([P, 512], U8, name=name + "_scales", align_bytes=64)
+            return codes, scales
+
+        offsets = sb.tile([P, SLOTS // PER_COLUMN], U16, name="offsets")
         tk_pool = sb.tile([P, TOKENS], F32, name="tk_pool")
         ts_pool = sb.tile([P, TOKENS], F32, name="ts_pool")
-        cf_sb = sb.tile([P, PACK], F32, name="cf_sb")
-        nc.scalar.dma_start(tk_pool[last:P, :], tk[0:1, :])
-        nc.scalar.dma_start(ts_pool[last:P, :], ts[0:1, :])
-        nc.scalar.dma_start(cf_sb[:], cf.rearrange("(p j) o -> p (j o)", j=PACK))
-        w_raw = sb.tile([P, PACK, D], F32, name="w_raw")
-        nc.sync.dma_start(w_raw[:], W.rearrange("(p j) f -> p j f", j=PACK))
+        cf_sb = sb.tile([P, LANES], F32, name="cf_sb")
+        nc.scalar.dma_start(tk_pool[ROW:P, :], tk[0:1, :])
+        nc.scalar.dma_start(ts_pool[ROW:P, :], ts[0:1, :])
+        nc.scalar.dma_start(cf_sb[:], cf.rearrange("(p t) o -> p (t o)", t=LANES))
+        w_raw = sb.tile([P, LANES, D], F32, name="w_raw")
+        nc.sync.dma_start(w_raw[:], W.rearrange("(p j) f -> p j f", j=LANES))
         nc.sync.dma_start(offsets[:], offs)
-        k_pool = [sb.tile([P, TOKENS], F32, name="k_pool%d" % j, tag="k_pool%d" % j, align_bytes=64) for j in range(PACK)]
-        v_pool = [sb.tile([P, TOKENS], F32, name="v_pool%d" % j) for j in range(PACK)]
-        for j in range(PACK):
-            nc.sync.dma_start(k_pool[j][:], kT.rearrange("(p j) t -> p j t", j=PACK)[:, j, :])
-        for j in range(PACK):
-            nc.sync.dma_start(v_pool[j][:], vT.rearrange("(p j) t -> p j t", j=PACK)[:, j, :])
+        k_pool = [sb.tile([P, TOKENS], F32, name="k_pool%d" % j, tag="k_pool%d" % j, align_bytes=64) for j in range(LANES)]
+        v_pool = [sb.tile([P, TOKENS], F32, name="v_pool%d" % t) for t in range(LANES)]
+        for j in range(LANES):
+            nc.sync.dma_start(k_pool[j][:], kT.rearrange("(p j) c -> p j c", j=LANES)[:, j, :])
+        for t in range(LANES):
+            nc.sync.dma_start(v_pool[t][:], vT.rearrange("(p t) c -> p t c", t=LANES)[:, t, :])
 
         ident = sb.tile([P, P], F32, name="ident")
         make_identity(nc, ident[:])
 
-        nc.vector.memset(tk_pool[0:last, :], 0.0)
-        nc.vector.memset(ts_pool[0:last, :], 0.0)
+        nc.vector.memset(tk_pool[0:ROW, :], 0.0)
+        nc.vector.memset(ts_pool[0:ROW, :], 0.0)
         window = [sb.tile([P, TOKENS], F32, name="window0")]
         nc.gpsimd.memset(window[0][:], 0.0)
 
-        w_d = sb.tile([P, D, PACK], BF16, name="w_d", align_bytes=64)
+        w_d = sb.tile([P, D, LANES], BF16, name="w_d", align_bytes=64)
         nc.scalar.activation(
-            w_d[:].rearrange("p (t m) j -> p m t j", t=PACK), w_raw[:].rearrange("p j (m t) -> p m t j", t=PACK), COPY
+            w_d[:].rearrange("p (t s) j -> p s t j", t=LANES), w_raw[:].rearrange("p j (s t) -> p s t j", t=LANES), COPY
         )
 
         tk_g = sb.tile([P, SLOTS], F32, name="tk_g")
         ts_g = sb.tile([P, SLOTS], F32, name="ts_g")
         nc.vector.tensor_copy(tk_g[:], tk_pool[:].indirect(offsets[:]))
         nc.vector.tensor_copy(ts_g[:], ts_pool[:].indirect(offsets[:]))
-        tk_t = bank(4, "tk_t", [P, PACK, P])
-        ts_t = bank(5, "ts_t", [P, PACK, P])
-        for m in range(4):
-            nc.tensor.transpose(tk_t[:, m, :], tk_g[:, P * m : P * (m + 1)], ident[:])
-        for m in range(4):
-            nc.tensor.transpose(ts_t[:, m, :], ts_g[:, P * m : P * (m + 1)], ident[:])
+        tk_turned = bank(4, "tk_turned", [P, SLOT_TILES, P])
+        ts_turned = bank(5, "ts_turned", [P, SLOT_TILES, P])
+        for m in range(SLOT_TILES):
+            nc.tensor.transpose(tk_turned[:, m, :], tk_g[:, P * m : P * (m + 1)], ident[:])
+        for m in range(SLOT_TILES):
+            nc.tensor.transpose(ts_turned[:, m, :], ts_g[:, P * m : P * (m + 1)], ident[:])
 
-        tk_col = sb.tile([P, 4], F32, name="tk_col")
-        ts_col = sb.tile([P, 4], F32, name="ts_col")
-        t1_col = sb.tile([P, 4], F32, name="t1_col")
-        t2_col = sb.tile([P, 4], F32, name="t2_col")
-        cf2 = sb.tile([P, PACK], F32, name="cf2")
-        nc.scalar.copy(tk_col[:], tk_t[:, :, last])
-        nc.scalar.copy(ts_col[:], ts_t[:, :, last])
+        tk_col = sb.tile([P, SLOT_TILES], F32, name="tk_col")
+        ts_col = sb.tile([P, SLOT_TILES], F32, name="ts_col")
+        tstk_col = sb.tile([P, SLOT_TILES], F32, name="tstk_col")
+        tstk2_col = sb.tile([P, SLOT_TILES], F32, name="tstk2_col")
+        cf2 = sb.tile([P, LANES], F32, name="cf2")
+        nc.scalar.copy(tk_col[:], tk_turned[:, :, ROW])
+        nc.scalar.copy(ts_col[:], ts_turned[:, :, ROW])
         nc.gpsimd.tensor_tensor(cf2[:], cf_sb[:], cf_sb[:], MULT)
-        nc.gpsimd.tensor_tensor(t1_col[:], ts_col[:], tk_col[:], MULT)
-        nc.gpsimd.tensor_tensor(t2_col[:], t1_col[:], tk_col[:], MULT)
+        nc.gpsimd.tensor_tensor(tstk_col[:], ts_col[:], tk_col[:], MULT)
+        nc.gpsimd.tensor_tensor(tstk2_col[:], tstk_col[:], tk_col[:], MULT)
 
-        w_f = sb.tile([P, PACK, P, PACK], BF16, name="w_f", align_bytes=64)
-        w_words = w_d[:].rearrange("p c j -> p (c j)").bitcast(F32).rearrange("p (t m u) -> p t u m", t=PACK, u=2)
+        w_f = sb.tile([P, LANES, P, LANES], BF16, name="w_f", align_bytes=64)
+        w_words = w_d[:].rearrange("p c j -> p (c j)").bitcast(F32).rearrange("p (t s u) -> p t u s", t=LANES, u=2)
         for u in range(2):
-            w_t = bank(u, "w_t%d" % u, [P, PACK, P])
-            for t in range(PACK):
-                nc.tensor.transpose(w_t[:, t, :], w_words[:, t, u, :], ident[:])
-            halves = w_t[:].rearrange("p t s -> p (t s)").bitcast(BF16).rearrange("p (t s e) -> p e s t", t=PACK, e=2)
-            nc.scalar.copy(w_f[:, 2 * u : 2 * u + 2, :, :], halves)
+            w_turned = bank(u, "w_turned%d" % u, [P, LANES, P])
+            for t in range(LANES):
+                nc.tensor.transpose(w_turned[:, t, :], w_words[:, t, u, :], ident[:])
+            unpacked = w_turned[:].rearrange("p t s -> p (t s)").bitcast(BF16).rearrange("p (t s i) -> p i s t", t=LANES, i=2)
+            nc.scalar.copy(w_f[:, 2 * u : 2 * u + 2, :, :], unpacked)
 
-        k_bf = sb.tile([P, SLOTS, PACK], BF16, name="k_bf", tag="late_a", align_bytes=64)
+        k_bf = sb.tile([P, SLOTS, LANES], BF16, name="k_bf", tag="then_window1", align_bytes=64)
         nc.vector.tensor_copy(k_bf[:, :, 0], k_pool[0][:].indirect(offsets[:]))
 
-        wd_codes, wd_scales = quantize(nc, sb, "wd", w_d, E4M3, "late_c")
-        t1_row = bank(6, "t1_row", [P, SLOTS])
-        for m in range(4):
-            nc.tensor.transpose(t1_row[:, P * m : P * (m + 1)], t1_col[:, m : m + 1].to_broadcast([P, P]), ident[:])
-        v_factor = [sb.tile([P, SLOTS], F32, name="v_factor%d" % t) for t in range(PACK)]
-        for t in range(PACK):
-            nc.scalar.activation(v_factor[t][:], t1_row[:], COPY, scale=cf_sb[:, t : t + 1])
+        wd_codes, wd_scales = operand("wd", "then_window3")
+        quantize(nc, wd_codes[:], wd_scales[:], w_d[:], E4M3)
+
+        tstk_row = bank(6, "tstk_row", [P, SLOTS])
+        for m in range(SLOT_TILES):
+            nc.tensor.transpose(tstk_row[:, P * m : P * (m + 1)], tstk_col[:, m : m + 1].to_broadcast([P, P]), ident[:])
+        v_factor = [sb.tile([P, SLOTS], F32, name="v_factor%d" % t) for t in range(LANES)]
+        for t in range(LANES):
+            nc.scalar.activation(v_factor[t][:], tstk_row[:], COPY, scale=cf_sb[:, t : t + 1])
 
         nc.vector.tensor_copy(k_bf[:, :, 1], k_pool[1][:].indirect(offsets[:]))
         nc.vector.tensor_copy(k_bf[:, :, 2], k_pool[2][:].indirect(offsets[:]))
-        wf_codes, wf_scales = quantize(nc, sb, "wf", w_f[:].rearrange("p j s t -> p (j s) t"), E4M3, "k_pool2")
-        nc.vector.tensor_copy(k_bf[:, :, 3], k_pool[3][:].indirect(offsets[:]))
-        k_codes, k_scales = quantize(nc, sb, "k", k_bf, E4M3, "late_b")
-        v_term = sb.tile([P, PACK, SLOTS], F32, name="v_term")
+        wf_codes, wf_scales = operand("wf", "k_pool2")
+        quantize(nc, wf_codes[:], wf_scales[:], w_f[:].rearrange("p j s t -> p (j s) t"), E4M3)
+        for h in range(2):
+            nc.vector.tensor_copy(k_bf[:, half(h), LANES - 1], k_pool[LANES - 1][:].indirect(offsets[:, half(h, PER_COLUMN)]))
+        k_codes, k_scales = operand("k", "then_window2")
+        for h in range(2):
+            quantize(nc, k_codes[:, half(h)], k_scales[:, half(h)], k_bf[:, half(h), :], E4M3)
+        v_term = sb.tile([P, LANES, SLOTS], F32, name="v_term")
 
-        u_s = []
-        for m in range(4):
+        u_scaled = []
+        for m in range(SLOT_TILES):
             cols = slice(P * m, P * (m + 1))
-            u_t = bank(m, "u_t%d" % m, [P, D])
-            nc.tensor.matmul_mx(u_t[:], lhsT=k_codes[:, cols].bitcast(E4M3), lhsT_scale=k_scales[:, cols],
-                                rhs=wd_codes[:].bitcast(E4M3), rhs_scale=wd_scales[:], start=True, stop=True)
-            u_s.append(sb.tile([P, PACK, P], F32, name="u_s%d" % m, tag="f32_%d" % m))
-            nc.scalar.activation(u_s[m][:].rearrange("p r s -> p (r s)"), u_t[:], COPY, scale=t2_col[:, m : m + 1])
-        u_term = sb.tile([P, PACK, SLOTS], F32, name="u_term")
-        for r in range(PACK):
-            u_back = bank(4 + r, "u_back%d" % r, [P, SLOTS])
-            for m in range(4):
-                nc.tensor.transpose(u_back[:, P * m : P * (m + 1)], u_s[m][:, r, :], ident[:])
-            nc.scalar.activation(u_term[:, r, :], u_back[:], COPY, scale=cf2[:, r : r + 1])
+            u_psum = bank(m, "u_psum%d" % m, [P, D])
+            nc.tensor.matmul_mx(
+                u_psum[:], lhsT=k_codes[:, cols].bitcast(E4M3), lhsT_scale=k_scales[:, cols],
+                rhs=wd_codes[:].bitcast(E4M3), rhs_scale=wd_scales[:], start=True, stop=True,
+            )
+            u_scaled.append(sb.tile([P, LANES, P], F32, name="u_scaled%d" % m, tag="from_psum%d" % m))
+            nc.scalar.activation(u_scaled[m][:].rearrange("p t s -> p (t s)"), u_psum[:], COPY, scale=tstk2_col[:, m : m + 1])
+        u_term = sb.tile([P, LANES, SLOTS], F32, name="u_term")
+        for t in range(LANES):
+            u_turned = bank(SLOT_TILES + t, "u_turned%d" % t, [P, SLOTS])
+            for m in range(SLOT_TILES):
+                nc.tensor.transpose(u_turned[:, P * m : P * (m + 1)], u_scaled[m][:, t, :], ident[:])
+            nc.scalar.activation(u_term[:, t, :], u_turned[:], COPY, scale=cf2[:, t : t + 1])
 
-        for j, tag in ((1, "late_a"), (2, "late_b"), (3, "late_c")):
-            window.append(sb.tile([P, TOKENS], F32, name="window%d" % j, tag=tag, align_bytes=64))
+        for j in range(1, LANES):
+            window.append(sb.tile([P, TOKENS], F32, name="window%d" % j, tag="then_window%d" % j, align_bytes=64))
             nc.gpsimd.memset(window[j][:], 0.0)
-        for t in range(PACK - 1):
-            nc.vector.tensor_tensor(v_term[:, t, :], v_pool[t][:].indirect(offsets[:]), v_factor[t][:], MULT)
-        half = SLOTS // 2
-        t = PACK - 1
-        for h in range(2):
-            cols = slice(half * h, half * (h + 1))
-            listed = offsets[:, half // 16 * h : half // 16 * (h + 1)]
-            nc.vector.tensor_tensor(v_term[:, t, cols], v_pool[t][:].indirect(listed), v_factor[t][:, cols], MULT)
-        e_bf = sb.tile([P, SLOTS, PACK], BF16, name="e_bf", align_bytes=64)
-        for h in range(2):
-            groups = slice(half // 4 * h, half // 4 * (h + 1))
-            nc.vector.tensor_tensor(woven(e_bf)[:, groups], planes_walk(u_term)[:, groups], planes_walk(v_term)[:, groups], SUB)
-        e_codes = sb.tile([P, SLOTS], U32, name="e_codes", align_bytes=64)
-        e_scales = sb.tile([P, SLOTS], U8, name="e_scales", align_bytes=64)
-        for h in range(2):
-            cols = slice(half * h, half * (h + 1))
-            nc.vector.quantize_mx(out=e_codes[:, cols].bitcast(E5M2), scales=e_scales[:, cols], in_=e_bf[:, cols, :].rearrange("p c t -> p (c t)"))
 
-        bounds = (0, 512, 1024, 1536, 1792, 2048)
-        chunks = [slice(a, b) for a, b in zip(bounds[:-1], bounds[1:])]
-        pairs = [sb.tile([P, 2, c.stop - c.start, 2], BF16, name="pairs%d" % c.start, align_bytes=64) for c in chunks]
+        for t in range(LANES - 1):
+            nc.vector.tensor_tensor(v_term[:, t, :], v_pool[t][:].indirect(offsets[:]), v_factor[t][:], MULT)
+        for h in range(2):
+            listed = v_pool[LANES - 1][:].indirect(offsets[:, half(h, PER_COLUMN)])
+            nc.vector.tensor_tensor(v_term[:, LANES - 1, half(h)], listed, v_factor[LANES - 1][:, half(h)], MULT)
+        e_bf = sb.tile([P, SLOTS, LANES], BF16, name="e_bf", align_bytes=64)
+        e_walk = e_bf[:].rearrange("p (c i) t -> p c t i", i=RUN)
+        u_walk = u_term[:].rearrange("p t (c i) -> p c t i", i=RUN)
+        v_walk = v_term[:].rearrange("p t (c i) -> p c t i", i=RUN)
+        for h in range(2):
+            nc.vector.tensor_tensor(e_walk[:, half(h, RUN)], u_walk[:, half(h, RUN)], v_walk[:, half(h, RUN)], SUB)
+        e_codes, e_scales = operand("e")
+        for h in range(2):
+            quantize(nc, e_codes[:, half(h)], e_scales[:, half(h)], e_bf[:, half(h), :], E5M2)
+
+        pairs = [sb.tile([P, 2, c.stop - c.start, 2], BF16, name="pairs%d" % c.start, align_bytes=64) for c in CHUNKS]
         dk_sb = []
-        for j in range(PACK):
+        for j in range(LANES):
             cols = slice(P * j, P * (j + 1))
-            dk = bank(j, "dk%d" % j, [P, SLOTS])
-            nc.tensor.matmul_mx(dk[:], lhsT=wf_codes[:, cols].bitcast(E4M3), lhsT_scale=wf_scales[:, cols],
-                                rhs=e_codes[:].bitcast(E5M2), rhs_scale=e_scales[:], start=True, stop=True)
-            dk_sb.append(sb.tile([P, SLOTS], F32, name="dk_sb%d" % j, tag="f32_%d" % j))
-            nc.scalar.copy(dk_sb[j][:], dk[:])
-        for j in range(PACK):
+            dk_psum = bank(j, "dk_psum%d" % j, [P, SLOTS])
+            nc.tensor.matmul_mx(
+                dk_psum[:], lhsT=wf_codes[:, cols].bitcast(E4M3), lhsT_scale=wf_scales[:, cols],
+                rhs=e_codes[:].bitcast(E5M2), rhs_scale=e_scales[:], start=True, stop=True,
+            )
+            dk_sb.append(sb.tile([P, SLOTS], F32, name="dk_sb%d" % j, tag="from_psum%d" % j))
+            nc.scalar.copy(dk_sb[j][:], dk_psum[:])
+        for j in range(LANES):
             nc.vector.tensor_copy(window[j][:].indirect(offsets[:]), dk_sb[j][:])
-            nc.sync.dma_start(out_0.rearrange("(p j) t -> p j t", j=PACK)[:, j, :], window[j][:])
-            for c in range(j // 2, len(chunks)):
-                nc.scalar.copy(pairs[c][:, j // 2, :, j % 2], window[j][:, chunks[c]])
+            nc.sync.dma_start(out_0.rearrange("(p j) c -> p j c", j=LANES)[:, j, :], window[j][:])
+            for c, cols in enumerate(CHUNKS):
+                skip = max(VECTOR_ROUNDS - cols.start, 0) if j >= 2 else 0
+                nc.scalar.copy(pairs[c][:, j // 2, skip:, j % 2], window[j][:, cols.start + skip : cols.stop])
         for j in (2, 3):
-            nc.vector.tensor_copy(pairs[0][:, 1, :, j % 2], window[j][:, chunks[0]])
+            nc.vector.tensor_copy(pairs[0][:, 1, :VECTOR_ROUNDS, j % 2], window[j][:, :VECTOR_ROUNDS])
 
         words_out = out_1[0].rearrange("p c l -> p (c l)").bitcast(I32)
-        y_scales = sb.tile([P, TOKENS], U8, name="y_scales", align_bytes=64)
-        y_bf = [sb.tile([P, c.stop - c.start, PACK], BF16, name="y_bf%d" % c.start, align_bytes=64) for c in chunks]
-        vector_stop = 1408
+        y_scales = sb.tile([P, TOKENS // 2], U8, name="y_scales", align_bytes=64)
+        y_bf = [sb.tile([P, c.stop - c.start, LANES], BF16, name="y_bf%d" % c.start, align_bytes=64) for c in CHUNKS]
 
         def weave(c):
-            y_words = y_bf[c][:].rearrange("p c t -> p (c t)").bitcast(F32).rearrange("p (c i u) -> p c u i", i=4, u=2)
-            pair_words = pairs[c][:].rearrange("p u c e -> p u (c e)").bitcast(F32).rearrange("p u (c i) -> p c u i", i=4)
-            width = chunks[c].stop - chunks[c].start
-            g = min(max(vector_stop - chunks[c].start, 0), width) // 4
-            if g > 0:
-                nc.vector.tensor_copy(y_words[:, :g], pair_words[:, :g])
-            if g < width // 4:
-                nc.scalar.copy(y_words[:, g:], pair_words[:, g:])
+            y_words = y_bf[c][:].rearrange("p c t -> p (c t)").bitcast(F32).rearrange("p (c i u) -> p c u i", i=RUN, u=2)
+            pair_words = pairs[c][:].rearrange("p u c e -> p u (c e)").bitcast(F32).rearrange("p u (c i) -> p c u i", i=RUN)
+            width = CHUNKS[c].stop - CHUNKS[c].start
+            cut = min(max(VECTOR_WEAVES - CHUNKS[c].start, 0), width) // RUN
+            if cut > 0:
+                nc.vector.tensor_copy(y_words[:, :cut], pair_words[:, :cut])
+            if cut < width // RUN:
+                nc.scalar.copy(y_words[:, cut:], pair_words[:, cut:])
 
         def hand_on(c):
-            cols = chunks[c]
-            y_codes = sb.tile([P, cols.stop - cols.start], U32, name="y_codes%d" % c, align_bytes=64)
-            nc.vector.quantize_mx(out=y_codes[:].bitcast(E4M3), scales=y_scales[:, cols], in_=y_bf[c][:].rearrange("p c t -> p (c t)"))
+            cols = CHUNKS[c]
+            width = cols.stop - cols.start
+            y_codes = sb.tile([P, width], U32, name="y_codes%d" % c, align_bytes=64)
+            g, first = divmod(cols.start, TOKENS // 2)
+            quantize(nc, y_codes[:], y_scales[4 * g : P, first : first + width], y_bf[c][:], E4M3)
             nc.sync.dma_start(words_out[:, cols], y_codes[:].bitcast(I32))
 
-        for c in range(len(chunks) + 1):
-            if c < len(chunks):
+        for c in range(len(CHUNKS) + 1):
+            if c < len(CHUNKS):
                 weave(c)
             if c > 0:
                 hand_on(c - 1)
         for q in range(4):
             queue = nc.sync if q == 3 else nc.scalar
-            queue.dma_start(out_2[0].bitcast(I32)[4 * q : 4 * q + 4, :], y_scales[32 * q : 32 * q + 4, :].bitcast(I32))
+            rows = out_2[0].bitcast(I32)[4 * q : 4 * q + 4, :].rearrange("r (g x) -> g r x", g=2)
+            queue.dma_start(rows, y_scales[32 * q : 32 * q + 8, :].bitcast(I32))

@@ -46,6 +46,7 @@ def tile_attend_gttt_k_pl_kernel(tc, kT, vT, W, ts, tk, cf, offs, out_0, out_1, 
     nc = tc.nc
     with ExitStack() as ctx:
         sb = ctx.enter_context(tc.tile_pool(name="sb", bufs=1))
+        ring = ctx.enter_context(tc.tile_pool(name="ring", bufs=2))
         ps = ctx.enter_context(tc.psum_pool(name="ps", bufs=1))
 
         def bank(b, name, shape):
@@ -126,7 +127,7 @@ def tile_attend_gttt_k_pl_kernel(tc, kT, vT, W, ts, tk, cf, offs, out_0, out_1, 
         tstk_row = bank(6, "tstk_row", [P, SLOTS])
         for m in range(SLOT_TILES):
             nc.tensor.transpose(tstk_row[:, P * m : P * (m + 1)], tstk_col[:, m : m + 1].to_broadcast([P, P]), ident[:])
-        v_factor = [sb.tile([P, SLOTS], F32, name="v_factor%d" % t) for t in range(LANES)]
+        v_factor = [sb.tile([P, SLOTS], F32, name="v_factor%d" % t, tag="v_factor%d" % t) for t in range(LANES)]
         for t in range(LANES):
             nc.scalar.activation(v_factor[t][:], tstk_row[:], COPY, scale=cf_sb[:, t : t + 1])
 
@@ -139,7 +140,6 @@ def tile_attend_gttt_k_pl_kernel(tc, kT, vT, W, ts, tk, cf, offs, out_0, out_1, 
         k_codes, k_scales = operand("k", "then_window2")
         for h in range(2):
             quantize(nc, k_codes[:, half(h)], k_scales[:, half(h)], k_bf[:, half(h), :], E4M3)
-        v_term = sb.tile([P, LANES, SLOTS], F32, name="v_term")
 
         u_scaled = []
         for m in range(SLOT_TILES):
@@ -151,45 +151,77 @@ def tile_attend_gttt_k_pl_kernel(tc, kT, vT, W, ts, tk, cf, offs, out_0, out_1, 
             )
             u_scaled.append(sb.tile([P, LANES, P], F32, name="u_scaled%d" % m, tag="from_psum%d" % m))
             nc.scalar.activation(u_scaled[m][:].rearrange("p t s -> p (t s)"), u_psum[:], COPY, scale=tstk2_col[:, m : m + 1])
-        u_term = sb.tile([P, LANES, SLOTS], F32, name="u_term")
+        u_turned = []
         for t in range(LANES):
-            u_turned = bank(SLOT_TILES + t, "u_turned%d" % t, [P, SLOTS])
+            u_turned.append(bank(SLOT_TILES + t, "u_turned%d" % t, [P, SLOTS]))
             for m in range(SLOT_TILES):
-                nc.tensor.transpose(u_turned[:, P * m : P * (m + 1)], u_scaled[m][:, t, :], ident[:])
-            nc.scalar.activation(u_term[:, t, :], u_turned[:], COPY, scale=cf2[:, t : t + 1])
+                nc.tensor.transpose(u_turned[t][:, P * m : P * (m + 1)], u_scaled[m][:, t, :], ident[:])
 
         for j in range(1, LANES):
             window.append(sb.tile([P, TOKENS], F32, name="window%d" % j, tag="then_window%d" % j, align_bytes=64))
             nc.gpsimd.memset(window[j][:], 0.0)
 
-        for t in range(LANES - 1):
-            nc.vector.tensor_tensor(v_term[:, t, :], v_pool[t][:].indirect(offsets[:]), v_factor[t][:], MULT)
-        for h in range(2):
-            listed = v_pool[LANES - 1][:].indirect(offsets[:, half(h, PER_COLUMN)])
-            nc.vector.tensor_tensor(v_term[:, LANES - 1, half(h)], listed, v_factor[LANES - 1][:, half(h)], MULT)
         e_bf = sb.tile([P, SLOTS, LANES], BF16, name="e_bf", align_bytes=64)
-        e_walk = e_bf[:].rearrange("p (c i) t -> p c t i", i=RUN)
-        u_walk = u_term[:].rearrange("p t (c i) -> p c t i", i=RUN)
-        v_walk = v_term[:].rearrange("p t (c i) -> p c t i", i=RUN)
-        for h in range(2):
-            nc.vector.tensor_tensor(e_walk[:, half(h, RUN)], u_walk[:, half(h, RUN)], v_walk[:, half(h, RUN)], SUB)
-        e_codes, e_scales = operand("e")
-        for h in range(2):
-            quantize(nc, e_codes[:, half(h)], e_scales[:, half(h)], e_bf[:, half(h), :], E5M2)
+        e_low = sb.tile([P, 2, SLOTS], BF16, name="e_low", tag="v_factor1")
+        e_high = sb.tile([P, 2, SLOTS], BF16, name="e_high")
+
+        def look_up_v(t, first, count):
+            listed = v_pool[t][:].indirect(offsets[:, first // PER_COLUMN : (first + count) // PER_COLUMN])
+            v_term = ring.tile([P, count], F32, name="v_term", tag="v_term%d" % count)
+            nc.vector.tensor_tensor(v_term[:], listed, v_factor[t][:, first : first + count], MULT)
+            return v_term
+
+        def combine(t, first, count, v_term):
+            cols = slice(first, first + count)
+            plane = (e_low, e_high)[t // 2][:, t % 2, cols]
+            nc.vector.scalar_tensor_tensor(plane, u_turned[t][:, cols], cf2[:, t : t + 1], v_term[:], MULT, SUB)
+
+        def lay_lanes(u, first, count):
+            cols = slice(first, first + count)
+            nc.scalar.copy(e_bf[:, cols, 2 * u : 2 * u + 2], (e_low, e_high)[u][:, :, cols].rearrange("p i c -> p c i"))
+
+        v_terms = [look_up_v(0, 0, SLOTS), look_up_v(1, 0, SLOTS)]
+        combine(0, 0, SLOTS, v_terms[0])
+        combine(1, 0, SLOTS, v_terms[1])
+        lay_lanes(0, 0, SLOTS)
+        combine(2, 0, SLOTS, look_up_v(2, 0, SLOTS))
+        e_codes = sb.tile([P, HALF + SLOTS], U32, name="e_codes", align_bytes=64)
+        e_scales = sb.tile([P, HALF + SLOTS], U8, name="e_scales", align_bytes=64)
+        nc.vector.memset(e_codes[:, :HALF], 0)
+        nc.vector.memset(e_scales[:, :HALF], 0)
+        v_terms = [look_up_v(3, 0, P)]
+        for m in range(SLOT_TILES):
+            if m + 1 < SLOT_TILES:
+                v_terms.append(look_up_v(3, P * (m + 1), P))
+            combine(3, P * m, P, v_terms[m])
+            lay_lanes(1, P * m, P)
+            if m % 2 == 1:
+                h = m // 2
+                cols = slice(HALF * (h + 1), HALF * (h + 2))
+                quantize(nc, e_codes[:, cols], e_scales[:, cols], e_bf[:, half(h), :], E5M2)
 
         pairs = [sb.tile([P, 2, c.stop - c.start, 2], BF16, name="pairs%d" % c.start, align_bytes=64) for c in CHUNKS]
-        dk_sb = []
-        for j in range(LANES):
+
+        def dk_pass(j, b, first):
             cols = slice(P * j, P * (j + 1))
-            dk_psum = bank(j, "dk_psum%d" % j, [P, SLOTS])
+            dk_psum = bank(b, "dk_psum%d" % b, [P, SLOTS])
             nc.tensor.matmul_mx(
                 dk_psum[:], lhsT=wf_codes[:, cols].bitcast(E4M3), lhsT_scale=wf_scales[:, cols],
-                rhs=e_codes[:].bitcast(E5M2), rhs_scale=e_scales[:], start=True, stop=True,
+                rhs=e_codes[:, first : first + SLOTS].bitcast(E5M2), rhs_scale=e_scales[:, first : first + SLOTS], start=True, stop=True,
             )
-            dk_sb.append(sb.tile([P, SLOTS], F32, name="dk_sb%d" % j, tag="from_psum%d" % j))
-            nc.scalar.copy(dk_sb[j][:], dk_psum[:])
+            return dk_psum
+
+        dk_sb = [sb.tile([P, SLOTS], F32, name="dk_sb%d" % j, tag="from_psum%d" % j) for j in range(LANES)]
+        nc.scalar.copy(dk_sb[0][:, half(0)], dk_pass(0, 0, 0)[:, half(1)])
+        nc.scalar.copy(dk_sb[0][:, half(1)], dk_pass(0, 1, HALF)[:, half(1)])
+        for j in range(1, LANES):
+            nc.scalar.copy(dk_sb[j][:], dk_pass(j, j + 1, HALF)[:])
         for j in range(LANES):
-            nc.vector.tensor_copy(window[j][:].indirect(offsets[:]), dk_sb[j][:])
+            if j == 0:
+                for h in range(2):
+                    nc.vector.tensor_copy(window[j][:].indirect(offsets[:, half(h, PER_COLUMN)]), dk_sb[j][:, half(h)])
+            else:
+                nc.vector.tensor_copy(window[j][:].indirect(offsets[:]), dk_sb[j][:])
             nc.sync.dma_start(out_0.rearrange("(p j) c -> p j c", j=LANES)[:, j, :], window[j][:])
             for c, cols in enumerate(CHUNKS):
                 skip = max(VECTOR_ROUNDS - cols.start, 0) if j >= 2 else 0

@@ -58,7 +58,7 @@ def tile_attend_gttt_k_pl_kernel(tc, kT, vT, W, ts, tk, cf, offs, out_0, out_1, 
             return codes, scales
 
         offsets = sb.tile([P, SLOTS // PER_COLUMN], U16, name="offsets")
-        tk_pool = sb.tile([P, TOKENS], F32, name="tk_pool")
+        tk_pool = sb.tile([P, TOKENS], F32, name="tk_pool", tag="then_window0", align_bytes=64)
         ts_pool = sb.tile([P, TOKENS], F32, name="ts_pool")
         cf_sb = sb.tile([P, LANES], F32, name="cf_sb")
         nc.scalar.dma_start(tk_pool[ROW:P, :], tk[0:1, :])
@@ -68,7 +68,7 @@ def tile_attend_gttt_k_pl_kernel(tc, kT, vT, W, ts, tk, cf, offs, out_0, out_1, 
         nc.sync.dma_start(w_raw[:], W.rearrange("(p j) f -> p j f", j=LANES))
         nc.sync.dma_start(offsets[:], offs)
         k_pool = [sb.tile([P, TOKENS], F32, name="k_pool%d" % j, tag="k_pool%d" % j, align_bytes=64) for j in range(LANES)]
-        v_pool = [sb.tile([P, TOKENS], F32, name="v_pool%d" % t) for t in range(LANES)]
+        v_pool = [sb.tile([P, TOKENS], F32, name="v_pool%d" % t, tag="v_pool%d" % t) for t in range(LANES)]
         for j in range(LANES):
             nc.sync.dma_start(k_pool[j][:], kT.rearrange("(p j) c -> p j c", j=LANES)[:, j, :])
         for t in range(LANES):
@@ -79,10 +79,8 @@ def tile_attend_gttt_k_pl_kernel(tc, kT, vT, W, ts, tk, cf, offs, out_0, out_1, 
 
         nc.vector.memset(tk_pool[0:ROW, :], 0.0)
         nc.vector.memset(ts_pool[0:ROW, :], 0.0)
-        window = [sb.tile([P, TOKENS], F32, name="window0")]
-        nc.gpsimd.memset(window[0][:], 0.0)
 
-        w_d = sb.tile([P, D, LANES], BF16, name="w_d", align_bytes=64)
+        w_d = sb.tile([P, D, LANES], BF16, name="w_d", tag="then_window1", align_bytes=64)
         nc.scalar.activation(
             w_d[:].rearrange("p (t s) j -> p s t j", t=LANES), w_raw[:].rearrange("p j (s t) -> p s t j", t=LANES), COPY
         )
@@ -91,6 +89,8 @@ def tile_attend_gttt_k_pl_kernel(tc, kT, vT, W, ts, tk, cf, offs, out_0, out_1, 
         ts_g = sb.tile([P, SLOTS], F32, name="ts_g")
         nc.vector.tensor_copy(tk_g[:], tk_pool[:].indirect(offsets[:]))
         nc.vector.tensor_copy(ts_g[:], ts_pool[:].indirect(offsets[:]))
+        window = [sb.tile([P, TOKENS], F32, name="window0", tag="then_window0", align_bytes=64)]
+        nc.gpsimd.memset(window[0][:], 0.0)
         tk_turned = bank(4, "tk_turned", [P, SLOT_TILES, P])
         ts_turned = bank(5, "ts_turned", [P, SLOT_TILES, P])
         for m in range(SLOT_TILES):
@@ -119,7 +119,8 @@ def tile_attend_gttt_k_pl_kernel(tc, kT, vT, W, ts, tk, cf, offs, out_0, out_1, 
             nc.scalar.copy(w_f[:, 2 * u : 2 * u + 2, :, :], unpacked)
 
         k_bf = sb.tile([P, SLOTS, LANES], BF16, name="k_bf", tag="then_window1", align_bytes=64)
-        nc.vector.tensor_copy(k_bf[:, :, 0], k_pool[0][:].indirect(offsets[:]))
+        k_low = sb.tile([P, 2, SLOTS], BF16, name="k_low", tag="k_low")
+        nc.vector.tensor_copy(k_low[:, 0, :], k_pool[0][:].indirect(offsets[:]))
 
         wd_codes, wd_scales = operand("wd", "then_window3")
         quantize(nc, wd_codes[:], wd_scales[:], w_d[:], E4M3)
@@ -127,11 +128,12 @@ def tile_attend_gttt_k_pl_kernel(tc, kT, vT, W, ts, tk, cf, offs, out_0, out_1, 
         tstk_row = bank(6, "tstk_row", [P, SLOTS])
         for m in range(SLOT_TILES):
             nc.tensor.transpose(tstk_row[:, P * m : P * (m + 1)], tstk_col[:, m : m + 1].to_broadcast([P, P]), ident[:])
-        v_factor = [sb.tile([P, SLOTS], F32, name="v_factor%d" % t, tag="v_factor%d" % t) for t in range(LANES)]
+        nc.vector.tensor_copy(k_low[:, 1, :], k_pool[1][:].indirect(offsets[:]))
+        nc.scalar.copy(k_bf[:, :, 0:2], k_low[:].rearrange("p i c -> p c i"))
+        v_factors = sb.tile([P, LANES, SLOTS], F32, name="v_factors", tag="k_low")
+        v_factor = [v_factors[:, t, :] for t in range(LANES)]
         for t in range(LANES):
-            nc.scalar.activation(v_factor[t][:], tstk_row[:], COPY, scale=cf_sb[:, t : t + 1])
-
-        nc.vector.tensor_copy(k_bf[:, :, 1], k_pool[1][:].indirect(offsets[:]))
+            nc.scalar.activation(v_factor[t], tstk_row[:], COPY, scale=cf_sb[:, t : t + 1])
         nc.vector.tensor_copy(k_bf[:, :, 2], k_pool[2][:].indirect(offsets[:]))
         wf_codes, wf_scales = operand("wf", "k_pool2")
         quantize(nc, wf_codes[:], wf_scales[:], w_f[:].rearrange("p j s t -> p (j s) t"), E4M3)
@@ -162,7 +164,7 @@ def tile_attend_gttt_k_pl_kernel(tc, kT, vT, W, ts, tk, cf, offs, out_0, out_1, 
             nc.gpsimd.memset(window[j][:], 0.0)
 
         e_bf = sb.tile([P, SLOTS, LANES], BF16, name="e_bf", align_bytes=64)
-        e_low = sb.tile([P, 2, SLOTS], BF16, name="e_low", tag="v_factor1")
+        e_low = sb.tile([P, 2, SLOTS], BF16, name="e_low", tag="v_pool1")
         e_high = sb.tile([P, 2, SLOTS], BF16, name="e_high")
 
         def look_up_v(t, first, count):

@@ -153,54 +153,44 @@ def tile_attend_gttt_k_pl_kernel(tc, kT, vT, W, ts, tk, cf, offs, out_0, out_1, 
             )
             u_scaled.append(sb.tile([P, LANES, P], F32, name="u_scaled%d" % m, tag="from_psum%d" % m))
             nc.scalar.activation(u_scaled[m][:].rearrange("p t s -> p (t s)"), u_psum[:], COPY, scale=tstk2_col[:, m : m + 1])
-        u_turned = []
+        u_term = sb.tile([P, LANES, SLOTS], F32, name="u_term")
         for t in range(LANES):
-            u_turned.append(bank(SLOT_TILES + t, "u_turned%d" % t, [P, SLOTS]))
+            u_turned = bank(SLOT_TILES + t, "u_turned%d" % t, [P, SLOTS])
             for m in range(SLOT_TILES):
-                nc.tensor.transpose(u_turned[t][:, P * m : P * (m + 1)], u_scaled[m][:, t, :], ident[:])
+                nc.tensor.transpose(u_turned[:, P * m : P * (m + 1)], u_scaled[m][:, t, :], ident[:])
+            nc.scalar.activation(u_term[:, t, :], u_turned[:], COPY, scale=cf2[:, t : t + 1])
 
         for j in range(1, LANES):
             window.append(sb.tile([P, TOKENS], F32, name="window%d" % j, tag="then_window%d" % j, align_bytes=64))
             nc.gpsimd.memset(window[j][:], 0.0)
 
-        e_bf = sb.tile([P, SLOTS, LANES], BF16, name="e_bf", align_bytes=64)
-        e_low = sb.tile([P, 2, SLOTS], BF16, name="e_low", tag="v_pool1")
-        e_high = sb.tile([P, 2, SLOTS], BF16, name="e_high")
-
-        def look_up_v(t, first, count):
-            listed = v_pool[t][:].indirect(offsets[:, first // PER_COLUMN : (first + count) // PER_COLUMN])
-            v_term = ring.tile([P, count], F32, name="v_term", tag="v_term%d" % count)
-            nc.vector.tensor_tensor(v_term[:], listed, v_factor[t][:, first : first + count], MULT)
-            return v_term
-
-        def combine(t, first, count, v_term):
-            cols = slice(first, first + count)
-            plane = (e_low, e_high)[t // 2][:, t % 2, cols]
-            nc.vector.scalar_tensor_tensor(plane, u_turned[t][:, cols], cf2[:, t : t + 1], v_term[:], MULT, SUB)
-
-        def lay_lanes(u, first, count):
-            cols = slice(first, first + count)
-            nc.scalar.copy(e_bf[:, cols, 2 * u : 2 * u + 2], (e_low, e_high)[u][:, :, cols].rearrange("p i c -> p c i"))
-
-        v_terms = [look_up_v(0, 0, SLOTS), look_up_v(1, 0, SLOTS)]
-        combine(0, 0, SLOTS, v_terms[0])
-        combine(1, 0, SLOTS, v_terms[1])
-        lay_lanes(0, 0, SLOTS)
-        combine(2, 0, SLOTS, look_up_v(2, 0, SLOTS))
+        v_term = sb.tile([P, LANES, SLOTS], F32, name="v_term")
         e_codes = sb.tile([P, HALF + SLOTS], U32, name="e_codes", align_bytes=64)
         e_scales = sb.tile([P, HALF + SLOTS], U8, name="e_scales", align_bytes=64)
         nc.vector.memset(e_codes[:, :HALF], 0)
         nc.vector.memset(e_scales[:, :HALF], 0)
-        v_terms = [look_up_v(3, 0, P)]
-        for m in range(SLOT_TILES):
-            if m + 1 < SLOT_TILES:
-                v_terms.append(look_up_v(3, P * (m + 1), P))
-            combine(3, P * m, P, v_terms[m])
-            lay_lanes(1, P * m, P)
-            if m % 2 == 1:
-                h = m // 2
-                cols = slice(HALF * (h + 1), HALF * (h + 2))
-                quantize(nc, e_codes[:, cols], e_scales[:, cols], e_bf[:, half(h), :], E5M2)
+
+        def look_up_v(t, first, count):
+            listed = v_pool[t][:].indirect(offsets[:, first // PER_COLUMN : (first + count) // PER_COLUMN])
+            nc.vector.tensor_tensor(v_term[:, t, first : first + count], listed, v_factor[t][:, first : first + count], MULT)
+
+        def subtract(m):
+            cols = slice(P // RUN * m, P // RUN * (m + 1))
+            e_bf = ring.tile([P, P, LANES], BF16, name="e_bf", align_bytes=64)
+            u_walk = u_term[:].rearrange("p t (c i) -> p c t i", i=RUN)
+            v_walk = v_term[:].rearrange("p t (c i) -> p c t i", i=RUN)
+            nc.vector.tensor_tensor(e_bf[:].rearrange("p (c i) t -> p c t i", i=RUN), u_walk[:, cols], v_walk[:, cols], SUB)
+            return e_bf
+
+        for t in range(LANES - 1):
+            look_up_v(t, 0, SLOTS)
+        for h in range(2):
+            look_up_v(LANES - 1, HALF * h, HALF)
+        for h in range(2):
+            e_tiles = [(m, subtract(m)) for m in (2 * h, 2 * h + 1)]
+            for m, e_bf in e_tiles:
+                cols = slice(HALF + P * m, HALF + P * (m + 1))
+                quantize(nc, e_codes[:, cols], e_scales[:, cols], e_bf[:], E5M2)
 
         pairs = [sb.tile([P, 2, c.stop - c.start, 2], BF16, name="pairs%d" % c.start, align_bytes=64) for c in CHUNKS]
 
@@ -214,7 +204,9 @@ def tile_attend_gttt_k_pl_kernel(tc, kT, vT, W, ts, tk, cf, offs, out_0, out_1, 
             return dk_psum
 
         dk_sb = [sb.tile([P, SLOTS], F32, name="dk_sb%d" % j, tag="from_psum%d" % j) for j in range(LANES)]
-        nc.scalar.copy(dk_sb[0][:, half(0)], dk_pass(0, 0, 0)[:, half(1)])
+        early = dk_pass(0, 0, 0)
+        nc.scalar.copy(dk_sb[0][:, : HALF - 32], early[:, HALF : SLOTS - 32])
+        nc.vector.tensor_copy(dk_sb[0][:, HALF - 32 : HALF], early[:, SLOTS - 32 :])
         nc.scalar.copy(dk_sb[0][:, half(1)], dk_pass(0, 1, HALF)[:, half(1)])
         for j in range(1, LANES):
             nc.scalar.copy(dk_sb[j][:], dk_pass(j, j + 1, HALF)[:])

@@ -26,9 +26,8 @@ RUN = 4
 PER_COLUMN = 16
 ROW = P - 1
 
-CHUNKS = [slice(0, 512), slice(512, 1024), slice(1024, 1536), slice(1536, 1792), slice(1792, 2048)]
-VECTOR_ROUNDS = 256
-VECTOR_WEAVES = 1408
+CHUNKS = [slice(0, SLOTS), slice(512, 1024), slice(1024, 1536), slice(1536, 1792), slice(1792, 2048)]
+VECTOR_WEAVES = 1280
 
 FLOPS = 2 * 2 * D * D * SLOTS
 BYTES = 4 * (3 * D * TOKENS + D * D + 2 * TOKENS + D) + 2 * P * SLOTS // PER_COLUMN + D * TOKENS + D // 32 * TOKENS
@@ -52,7 +51,7 @@ def tile_attend_gttt_k_pl_kernel(tc, kT, vT, W, ts, tk, cf, offs, out_0, out_1, 
         def bank(b, name, shape):
             return ps.tile(shape, F32, name=name, tag="bank%d" % b)
 
-        def operand(name, tag=""):
+        def operand(name, tag):
             codes = sb.tile([P, 512], U32, name=name + "_codes", tag=tag, align_bytes=64)
             scales = sb.tile([P, 512], U8, name=name + "_scales", align_bytes=64)
             return codes, scales
@@ -130,10 +129,9 @@ def tile_attend_gttt_k_pl_kernel(tc, kT, vT, W, ts, tk, cf, offs, out_0, out_1, 
             nc.tensor.transpose(tstk_row[:, P * m : P * (m + 1)], tstk_col[:, m : m + 1].to_broadcast([P, P]), ident[:])
         nc.vector.tensor_copy(k_low[:, 1, :], k_pool[1][:].indirect(offsets[:]))
         nc.scalar.copy(k_bf[:, :, 0:2], k_low[:].rearrange("p i c -> p c i"))
-        v_factors = sb.tile([P, LANES, SLOTS], F32, name="v_factors", tag="k_low")
-        v_factor = [v_factors[:, t, :] for t in range(LANES)]
+        v_factor = sb.tile([P, LANES, SLOTS], F32, name="v_factor", tag="k_low")
         for t in range(LANES):
-            nc.scalar.activation(v_factor[t], tstk_row[:], COPY, scale=cf_sb[:, t : t + 1])
+            nc.scalar.activation(v_factor[:, t, :], tstk_row[:], COPY, scale=cf_sb[:, t : t + 1])
         nc.vector.tensor_copy(k_bf[:, :, 2], k_pool[2][:].indirect(offsets[:]))
         wf_codes, wf_scales = operand("wf", "k_pool2")
         quantize(nc, wf_codes[:], wf_scales[:], w_f[:].rearrange("p j s t -> p (j s) t"), E4M3)
@@ -171,15 +169,16 @@ def tile_attend_gttt_k_pl_kernel(tc, kT, vT, W, ts, tk, cf, offs, out_0, out_1, 
         nc.vector.memset(e_scales[:, :HALF], 0)
 
         def look_up_v(t, first, count):
+            slots = slice(first, first + count)
             listed = v_pool[t][:].indirect(offsets[:, first // PER_COLUMN : (first + count) // PER_COLUMN])
-            nc.vector.tensor_tensor(v_term[:, t, first : first + count], listed, v_factor[t][:, first : first + count], MULT)
+            nc.vector.tensor_tensor(v_term[:, t, slots], listed, v_factor[:, t, slots], MULT)
 
         def subtract(m):
-            cols = slice(P // RUN * m, P // RUN * (m + 1))
+            runs = slice(P // RUN * m, P // RUN * (m + 1))
             e_bf = ring.tile([P, P, LANES], BF16, name="e_bf", align_bytes=64)
             u_walk = u_term[:].rearrange("p t (c i) -> p c t i", i=RUN)
             v_walk = v_term[:].rearrange("p t (c i) -> p c t i", i=RUN)
-            nc.vector.tensor_tensor(e_bf[:].rearrange("p (c i) t -> p c t i", i=RUN), u_walk[:, cols], v_walk[:, cols], SUB)
+            nc.vector.tensor_tensor(e_bf[:].rearrange("p (c i) t -> p c t i", i=RUN), u_walk[:, runs], v_walk[:, runs], SUB)
             return e_bf
 
         for t in range(LANES - 1):
@@ -196,17 +195,16 @@ def tile_attend_gttt_k_pl_kernel(tc, kT, vT, W, ts, tk, cf, offs, out_0, out_1, 
 
         def dk_pass(j, b, first):
             cols = slice(P * j, P * (j + 1))
+            moving = slice(first, first + SLOTS)
             dk_psum = bank(b, "dk_psum%d" % b, [P, SLOTS])
             nc.tensor.matmul_mx(
                 dk_psum[:], lhsT=wf_codes[:, cols].bitcast(E4M3), lhsT_scale=wf_scales[:, cols],
-                rhs=e_codes[:, first : first + SLOTS].bitcast(E5M2), rhs_scale=e_scales[:, first : first + SLOTS], start=True, stop=True,
+                rhs=e_codes[:, moving].bitcast(E5M2), rhs_scale=e_scales[:, moving], start=True, stop=True,
             )
             return dk_psum
 
         dk_sb = [sb.tile([P, SLOTS], F32, name="dk_sb%d" % j, tag="from_psum%d" % j) for j in range(LANES)]
-        early = dk_pass(0, 0, 0)
-        nc.scalar.copy(dk_sb[0][:, : HALF - 32], early[:, HALF : SLOTS - 32])
-        nc.vector.tensor_copy(dk_sb[0][:, HALF - 32 : HALF], early[:, SLOTS - 32 :])
+        nc.vector.tensor_copy(dk_sb[0][:, half(0)], dk_pass(0, 0, 0)[:, half(1)])
         nc.scalar.copy(dk_sb[0][:, half(1)], dk_pass(0, 1, HALF)[:, half(1)])
         for j in range(1, LANES):
             nc.scalar.copy(dk_sb[j][:], dk_pass(j, j + 1, HALF)[:])
@@ -218,10 +216,12 @@ def tile_attend_gttt_k_pl_kernel(tc, kT, vT, W, ts, tk, cf, offs, out_0, out_1, 
                 nc.vector.tensor_copy(window[j][:].indirect(offsets[:]), dk_sb[j][:])
             nc.sync.dma_start(out_0.rearrange("(p j) c -> p j c", j=LANES)[:, j, :], window[j][:])
             for c, cols in enumerate(CHUNKS):
-                skip = max(VECTOR_ROUNDS - cols.start, 0) if j >= 2 else 0
-                nc.scalar.copy(pairs[c][:, j // 2, skip:, j % 2], window[j][:, cols.start + skip : cols.stop])
-        for j in (2, 3):
-            nc.vector.tensor_copy(pairs[0][:, 1, :VECTOR_ROUNDS, j % 2], window[j][:, :VECTOR_ROUNDS])
+                if c == 0 and j == 2:
+                    nc.scalar.copy(pairs[c][:, 1], window[j][:, cols].unsqueeze(2).to_broadcast([P, cols.stop, 2]))
+                elif c > 0 or j < 2:
+                    nc.scalar.copy(pairs[c][:, j // 2, :, j % 2], window[j][:, cols])
+        for h in range(2):
+            nc.vector.tensor_copy(pairs[0][:, 1, half(h), 1], window[LANES - 1][:, half(h)])
 
         words_out = out_1[0].rearrange("p c l -> p (c l)").bitcast(I32)
         y_scales = sb.tile([P, TOKENS // 2], U8, name="y_scales", align_bytes=64)
@@ -232,7 +232,10 @@ def tile_attend_gttt_k_pl_kernel(tc, kT, vT, W, ts, tk, cf, offs, out_0, out_1, 
             pair_words = pairs[c][:].rearrange("p u c e -> p u (c e)").bitcast(F32).rearrange("p u (c i) -> p c u i", i=RUN)
             width = CHUNKS[c].stop - CHUNKS[c].start
             cut = min(max(VECTOR_WEAVES - CHUNKS[c].start, 0), width) // RUN
-            if cut > 0:
+            if c == 0:
+                for h in range(2):
+                    nc.vector.tensor_copy(y_words[:, half(h, RUN)], pair_words[:, half(h, RUN)])
+            elif cut > 0:
                 nc.vector.tensor_copy(y_words[:, :cut], pair_words[:, :cut])
             if cut < width // RUN:
                 nc.scalar.copy(y_words[:, cut:], pair_words[:, cut:])

@@ -67,7 +67,7 @@ def tile_attend_gttt_k_pl_kernel(tc, kT, vT, W, ts, tk, cf, offs, out_0, out_1, 
         nc.sync.dma_start(w_raw[:], W.rearrange("(p j) f -> p j f", j=LANES))
         nc.sync.dma_start(offsets[:], offs)
         k_pool = [sb.tile([P, TOKENS], F32, name="k_pool%d" % j, tag="k_pool%d" % j, align_bytes=64) for j in range(LANES)]
-        v_pool = [sb.tile([P, TOKENS], F32, name="v_pool%d" % t, tag="v_pool%d" % t) for t in range(LANES)]
+        v_pool = [sb.tile([P, TOKENS], F32, name="v_pool%d" % t, tag="v_pool%d" % t, align_bytes=64) for t in range(LANES)]
         for j in range(LANES):
             nc.sync.dma_start(k_pool[j][:], kT.rearrange("(p j) c -> p j c", j=LANES)[:, j, :])
         for t in range(LANES):
@@ -162,34 +162,66 @@ def tile_attend_gttt_k_pl_kernel(tc, kT, vT, W, ts, tk, cf, offs, out_0, out_1, 
             window.append(sb.tile([P, TOKENS], F32, name="window%d" % j, tag="then_window%d" % j, align_bytes=64))
             nc.gpsimd.memset(window[j][:], 0.0)
 
-        v_term = sb.tile([P, LANES, SLOTS], F32, name="v_term")
         e_codes = sb.tile([P, HALF + SLOTS], U32, name="e_codes", align_bytes=64)
         e_scales = sb.tile([P, HALF + SLOTS], U8, name="e_scales", align_bytes=64)
         nc.vector.memset(e_codes[:, :HALF], 0)
         nc.vector.memset(e_scales[:, :HALF], 0)
 
-        def look_up_v(t, first, count):
-            slots = slice(first, first + count)
-            listed = v_pool[t][:].indirect(offsets[:, first // PER_COLUMN : (first + count) // PER_COLUMN])
-            nc.vector.tensor_tensor(v_term[:, t, slots], listed, v_factor[:, t, slots], MULT)
+        v_term = sb.tile([P, 7, HALF], F32, name="v_term")
+        v_row = {(0, 0): 5, (0, 1): 6, (0, 2): 0, (0, 3): 4, (1, 0): 1, (1, 1): 2, (1, 2): 3, (1, 3): 4}
 
-        def subtract(m):
-            runs = slice(P // RUN * m, P // RUN * (m + 1))
+        def look_up_v(t, first, count):
+            h, within = divmod(first, HALF)
+            listed = v_pool[t][:].indirect(offsets[:, first // PER_COLUMN : (first + count) // PER_COLUMN])
+            nc.vector.tensor_tensor(
+                v_term[:, v_row[h, t], within : within + count], listed, v_factor[:, t, first : first + count], MULT
+            )
+
+        def walk(planes, m):
+            return planes[:, :, P * m : P * (m + 1)].rearrange("p t (c i) -> p c t i", i=RUN)
+
+        e_pairs = sb.tile([P, 2, 2, P, 2], BF16, name="e_pairs", tag="v_pool2", align_bytes=64)
+
+        def subtract_pair(m, u):
+            first, second = v_row[0, 2 * u], v_row[0, 2 * u + 1]
+            rows = v_term[:, first : second + 1 : second - first, :]
+            out = e_pairs[:, m, u].rearrange("p (c i) t -> p c t i", i=RUN)
+            nc.vector.tensor_tensor(out, walk(u_term[:, 2 * u : 2 * u + 2, :], m), walk(rows, m), SUB)
+
+        def weave_e(m):
             e_bf = ring.tile([P, P, LANES], BF16, name="e_bf", align_bytes=64)
-            u_walk = u_term[:].rearrange("p t (c i) -> p c t i", i=RUN)
-            v_walk = v_term[:].rearrange("p t (c i) -> p c t i", i=RUN)
-            nc.vector.tensor_tensor(e_bf[:].rearrange("p (c i) t -> p c t i", i=RUN), u_walk[:, runs], v_walk[:, runs], SUB)
+            e_words = e_bf[:].rearrange("p c t -> p (c t)").bitcast(F32).rearrange("p (c i u) -> p c u i", i=RUN, u=2)
+            pair_words = e_pairs[:, m].rearrange("p u c e -> p u (c e)").bitcast(F32).rearrange("p u (c i) -> p c u i", i=RUN)
+            nc.scalar.copy(e_words, pair_words)
             return e_bf
 
+        def subtract(m):
+            e_bf = ring.tile([P, P, LANES], BF16, name="e_bf", align_bytes=64)
+            out = e_bf[:].rearrange("p (c i) t -> p c t i", i=RUN)
+            nc.vector.tensor_tensor(out, walk(u_term[:], m), walk(v_term[:, 1:5, :], m - 2), SUB)
+            return e_bf
+
+        def quantize_e(m, e_bf):
+            cols = slice(HALF + P * m, HALF + P * (m + 1))
+            quantize(nc, e_codes[:, cols], e_scales[:, cols], e_bf[:], E5M2)
+
         for t in range(LANES - 1):
-            look_up_v(t, 0, SLOTS)
-        for h in range(2):
-            look_up_v(LANES - 1, HALF * h, HALF)
-        for h in range(2):
-            e_tiles = [(m, subtract(m)) for m in (2 * h, 2 * h + 1)]
-            for m, e_bf in e_tiles:
-                cols = slice(HALF + P * m, HALF + P * (m + 1))
-                quantize(nc, e_codes[:, cols], e_scales[:, cols], e_bf[:], E5M2)
+            for h in range(2):
+                look_up_v(t, HALF * h, HALF)
+        for m in range(2):
+            subtract_pair(m, 0)
+        for m in range(2):
+            look_up_v(LANES - 1, P * m, P)
+        for m in range(2):
+            subtract_pair(m, 1)
+        for m in range(2, 4):
+            look_up_v(LANES - 1, P * m, P)
+        e_tiles = [weave_e(m) for m in range(2)]
+        for m in range(2):
+            quantize_e(m, e_tiles[m])
+        e_tiles = [subtract(m) for m in range(2, 4)]
+        for m in range(2, 4):
+            quantize_e(m, e_tiles[m - 2])
 
         pairs = [sb.tile([P, 2, c.stop - c.start, 2], BF16, name="pairs%d" % c.start, align_bytes=64) for c in CHUNKS]
 

@@ -14,6 +14,7 @@ E5M2 = mybir.dt.float8_e5m2_x4
 COPY = mybir.ActivationFunctionType.Copy
 MULT = mybir.AluOpType.mult
 SUB = mybir.AluOpType.subtract
+ADD = mybir.AluOpType.add
 
 P = 128
 LANES = 4
@@ -22,6 +23,7 @@ SLOTS = 512
 TOKENS = 2048
 SLOT_TILES = SLOTS // P
 HALF = SLOTS // 2
+PAD = SLOTS - P
 RUN = 4
 PER_COLUMN = 16
 ROW = P - 1
@@ -45,7 +47,6 @@ def tile_attend_gttt_k_pl_kernel(tc, kT, vT, W, ts, tk, cf, offs, out_0, out_1, 
     nc = tc.nc
     with ExitStack() as ctx:
         sb = ctx.enter_context(tc.tile_pool(name="sb", bufs=1))
-        ring = ctx.enter_context(tc.tile_pool(name="ring", bufs=2))
         ps = ctx.enter_context(tc.psum_pool(name="ps", bufs=1))
 
         def bank(b, name, shape):
@@ -162,66 +163,71 @@ def tile_attend_gttt_k_pl_kernel(tc, kT, vT, W, ts, tk, cf, offs, out_0, out_1, 
             window.append(sb.tile([P, TOKENS], F32, name="window%d" % j, tag="then_window%d" % j, align_bytes=64))
             nc.gpsimd.memset(window[j][:], 0.0)
 
-        e_codes = sb.tile([P, HALF + SLOTS], U32, name="e_codes", align_bytes=64)
-        e_scales = sb.tile([P, HALF + SLOTS], U8, name="e_scales", align_bytes=64)
-        nc.vector.memset(e_codes[:, :HALF], 0)
-        nc.vector.memset(e_scales[:, :HALF], 0)
+        e_codes = sb.tile([P, PAD + SLOTS], U32, name="e_codes", align_bytes=64)
+        e_scales = sb.tile([P, PAD + SLOTS], U8, name="e_scales", align_bytes=64)
+        zeros = sb.tile([P, P], F32, name="zeros")
+        nc.vector.memset(e_codes[:, :PAD], 0)
+        nc.vector.memset(e_scales[:, :PAD], 0)
+        nc.vector.memset(zeros[:], 0.0)
 
-        v_term = sb.tile([P, 7, HALF], F32, name="v_term")
-        v_row = {(0, 0): 5, (0, 1): 6, (0, 2): 0, (0, 3): 4, (1, 0): 1, (1, 1): 2, (1, 2): 3, (1, 3): 4}
+        v_term = sb.tile([P, LANES * SLOT_TILES, P], F32, name="v_term")
 
-        def look_up_v(t, first, count):
-            h, within = divmod(first, HALF)
-            listed = v_pool[t][:].indirect(offsets[:, first // PER_COLUMN : (first + count) // PER_COLUMN])
-            nc.vector.tensor_tensor(
-                v_term[:, v_row[h, t], within : within + count], listed, v_factor[:, t, first : first + count], MULT
-            )
+        def v_row(t, m):
+            return SLOT_TILES * t + (m if t < LANES - 1 else {0: 0, 1: 3, 2: 0, 3: 3}[m])
 
-        def walk(planes, m):
-            return planes[:, :, P * m : P * (m + 1)].rearrange("p t (c i) -> p c t i", i=RUN)
+        def look_up_v(t, m, tiles):
+            first, last = P * m, P * (m + tiles)
+            listed = v_pool[t][:].indirect(offsets[:, first // PER_COLUMN : last // PER_COLUMN])
+            rows = v_term[:, v_row(t, m) : v_row(t, m) + tiles, :].rearrange("p m s -> p (m s)")
+            nc.vector.tensor_tensor(rows, listed, v_factor[:, t, first:last], MULT)
+
+        def walk(planes):
+            return planes.rearrange("p t (c i) -> p c t i", i=RUN)
+
+        def two_rows(tile, first, second):
+            return tile[:, first : second + 1 : second - first]
 
         e_pairs = sb.tile([P, 2, 2, P, 2], BF16, name="e_pairs", tag="v_pool2", align_bytes=64)
 
         def subtract_pair(m, u):
-            first, second = v_row[0, 2 * u], v_row[0, 2 * u + 1]
-            rows = v_term[:, first : second + 1 : second - first, :]
-            out = e_pairs[:, m, u].rearrange("p (c i) t -> p c t i", i=RUN)
-            nc.vector.tensor_tensor(out, walk(u_term[:, 2 * u : 2 * u + 2, :], m), walk(rows, m), SUB)
+            out = e_pairs[:, m - 1, u].rearrange("p (c i) t -> p c t i", i=RUN)
+            u_rows = u_term[:, 2 * u : 2 * u + 2, P * m : P * (m + 1)]
+            nc.vector.tensor_tensor(out, walk(u_rows), walk(two_rows(v_term, v_row(2 * u, m), v_row(2 * u + 1, m))), SUB)
 
         def weave_e(m):
-            e_bf = ring.tile([P, P, LANES], BF16, name="e_bf", align_bytes=64)
+            e_bf = sb.tile([P, P, LANES], BF16, name="e_bf%d" % m, align_bytes=64)
             e_words = e_bf[:].rearrange("p c t -> p (c t)").bitcast(F32).rearrange("p (c i u) -> p c u i", i=RUN, u=2)
-            pair_words = e_pairs[:, m].rearrange("p u c e -> p u (c e)").bitcast(F32).rearrange("p u (c i) -> p c u i", i=RUN)
-            nc.scalar.copy(e_words, pair_words)
-            return e_bf
+            nc.scalar.copy(e_words, walk(e_pairs[:, m - 1].rearrange("p r c e -> p r (c e)").bitcast(F32)))
+            return e_bf[:]
 
-        def subtract(m):
-            e_bf = ring.tile([P, P, LANES], BF16, name="e_bf", align_bytes=64)
-            out = e_bf[:].rearrange("p (c i) t -> p c t i", i=RUN)
-            nc.vector.tensor_tensor(out, walk(u_term[:], m), walk(v_term[:, 1:5, :], m - 2), SUB)
-            return e_bf
+        def subtract(m, e_bf):
+            out = e_bf.rearrange("p (c i) t -> p c t i", i=RUN)
+            v_rows = v_term[:, m : LANES * SLOT_TILES : SLOT_TILES, :]
+            nc.vector.tensor_tensor(out, walk(u_term[:, :, P * m : P * (m + 1)]), walk(v_rows), SUB)
 
         def quantize_e(m, e_bf):
-            cols = slice(HALF + P * m, HALF + P * (m + 1))
-            quantize(nc, e_codes[:, cols], e_scales[:, cols], e_bf[:], E5M2)
+            cols = slice(PAD + P * m, PAD + P * (m + 1))
+            quantize(nc, e_codes[:, cols], e_scales[:, cols], e_bf, E5M2)
 
         for t in range(LANES - 1):
-            for h in range(2):
-                look_up_v(t, HALF * h, HALF)
-        for m in range(2):
+            look_up_v(t, 0, SLOT_TILES)
+        for m in (1, 2):
             subtract_pair(m, 0)
         for m in range(2):
-            look_up_v(LANES - 1, P * m, P)
-        for m in range(2):
-            subtract_pair(m, 1)
+            look_up_v(LANES - 1, m, 1)
+        e_first = sb.tile([P, P, LANES], BF16, name="e_first", align_bytes=64)
+        subtract(0, e_first[:])
+        subtract_pair(1, 1)
+        quantize_e(0, e_first[:])
         for m in range(2, 4):
-            look_up_v(LANES - 1, P * m, P)
-        e_tiles = [weave_e(m) for m in range(2)]
-        for m in range(2):
-            quantize_e(m, e_tiles[m])
-        e_tiles = [subtract(m) for m in range(2, 4)]
-        for m in range(2, 4):
-            quantize_e(m, e_tiles[m - 2])
+            look_up_v(LANES - 1, m, 1)
+        subtract_pair(2, 1)
+        quantize_e(1, weave_e(1))
+        e_last = e_pairs[:, 0].rearrange("p u c e -> p (u c e)").rearrange("p (c t) -> p c t", t=LANES)
+        subtract(3, e_last)
+        e_third = weave_e(2)
+        quantize_e(3, e_last)
+        quantize_e(2, e_third)
 
         pairs = [sb.tile([P, 2, c.stop - c.start, 2], BF16, name="pairs%d" % c.start, align_bytes=64) for c in CHUNKS]
 
@@ -236,27 +242,33 @@ def tile_attend_gttt_k_pl_kernel(tc, kT, vT, W, ts, tk, cf, offs, out_0, out_1, 
             return dk_psum
 
         dk_sb = [sb.tile([P, SLOTS], F32, name="dk_sb%d" % j, tag="from_psum%d" % j) for j in range(LANES)]
-        nc.vector.tensor_copy(dk_sb[0][:, half(0)], dk_pass(0, 0, 0)[:, half(1)])
-        nc.scalar.copy(dk_sb[0][:, half(1)], dk_pass(0, 1, HALF)[:, half(1)])
-        for j in range(1, LANES):
-            nc.scalar.copy(dk_sb[j][:], dk_pass(j, j + 1, HALF)[:])
+        early = [P, HALF]
+        for j in range(2):
+            nc.scalar.copy(dk_sb[j][:, : early[j]], dk_pass(j, j, early[j] - P)[:, SLOTS - early[j] :])
         for j in range(LANES):
-            if j == 0:
-                for h in range(2):
-                    nc.vector.tensor_copy(window[j][:].indirect(offsets[:, half(h, PER_COLUMN)]), dk_sb[j][:, half(h)])
-            else:
-                nc.vector.tensor_copy(window[j][:].indirect(offsets[:]), dk_sb[j][:])
+            first = early[j] if j < 2 else 0
+            nc.scalar.copy(dk_sb[j][:, first:], dk_pass(j, j + 2, PAD)[:, first:])
+        nc.vector.tensor_tensor(window[0][:].indirect(offsets[:, : P // PER_COLUMN]), dk_sb[0][:, :P], zeros[:], ADD)
+        nc.vector.tensor_copy(window[1][:].indirect(offsets[:, half(0, PER_COLUMN)]), dk_sb[1][:, half(0)])
+        for j in range(LANES):
+            first = early[j] if j < 2 else 0
+            nc.vector.tensor_copy(window[j][:].indirect(offsets[:, first // PER_COLUMN :]), dk_sb[j][:, first:])
             nc.sync.dma_start(out_0.rearrange("(p j) c -> p j c", j=LANES)[:, j, :], window[j][:])
             for c, cols in enumerate(CHUNKS):
+                both = window[j][:, cols].unsqueeze(2).to_broadcast([P, cols.stop - cols.start, 2])
                 if c == 0 and j == 2:
-                    nc.scalar.copy(pairs[c][:, 1], window[j][:, cols].unsqueeze(2).to_broadcast([P, cols.stop, 2]))
+                    nc.scalar.copy(pairs[c][:, 1], both)
+                elif c >= 3 and j == 2:
+                    nc.gpsimd.tensor_scalar(pairs[c][:, 1], both, 1.0, 0.0, MULT, ADD)
+                elif c >= 3 and j < 2:
+                    nc.gpsimd.tensor_scalar(pairs[c][:, 0, :, j], window[j][:, cols], 1.0, 0.0, MULT, ADD)
                 elif c > 0 or j < 2:
                     nc.scalar.copy(pairs[c][:, j // 2, :, j % 2], window[j][:, cols])
         for h in range(2):
             nc.vector.tensor_copy(pairs[0][:, 1, half(h), 1], window[LANES - 1][:, half(h)])
 
         words_out = out_1[0].rearrange("p c l -> p (c l)").bitcast(I32)
-        y_scales = sb.tile([P, TOKENS // 2], U8, name="y_scales", align_bytes=64)
+        y_scales = sb.tile([P, TOKENS // 4], U8, name="y_scales", align_bytes=64)
         y_bf = [sb.tile([P, c.stop - c.start, LANES], BF16, name="y_bf%d" % c.start, align_bytes=64) for c in CHUNKS]
 
         def weave(c):
@@ -276,7 +288,7 @@ def tile_attend_gttt_k_pl_kernel(tc, kT, vT, W, ts, tk, cf, offs, out_0, out_1, 
             cols = CHUNKS[c]
             width = cols.stop - cols.start
             y_codes = sb.tile([P, width], U32, name="y_codes%d" % c, align_bytes=64)
-            g, first = divmod(cols.start, TOKENS // 2)
+            g, first = divmod(cols.start, TOKENS // 4)
             quantize(nc, y_codes[:], y_scales[4 * g : P, first : first + width], y_bf[c][:], E4M3)
             nc.sync.dma_start(words_out[:, cols], y_codes[:].bitcast(I32))
 
@@ -286,6 +298,6 @@ def tile_attend_gttt_k_pl_kernel(tc, kT, vT, W, ts, tk, cf, offs, out_0, out_1, 
             if c > 0:
                 hand_on(c - 1)
         for q in range(4):
-            queue = nc.sync if q == 3 else nc.scalar
-            rows = out_2[0].bitcast(I32)[4 * q : 4 * q + 4, :].rearrange("r (g x) -> g r x", g=2)
-            queue.dma_start(rows, y_scales[32 * q : 32 * q + 8, :].bitcast(I32))
+            queue = nc.sync
+            rows = out_2[0].bitcast(I32)[4 * q : 4 * q + 4, :].rearrange("r (g x) -> g r x", g=4)
+            queue.dma_start(rows, y_scales[32 * q : 32 * q + 16, :].bitcast(I32))

@@ -29,7 +29,7 @@ PER_COLUMN = 16
 ROW = P - 1
 
 CHUNKS = [slice(0, SLOTS), slice(512, 1024), slice(1024, 1536), slice(1536, 1792), slice(1792, 2048)]
-VECTOR_WEAVES = 1280
+VECTOR_WEAVES = 1536
 
 FLOPS = 2 * 2 * D * D * SLOTS
 BYTES = 4 * (3 * D * TOKENS + D * D + 2 * TOKENS + D) + 2 * P * SLOTS // PER_COLUMN + D * TOKENS + D // 32 * TOKENS
@@ -243,8 +243,8 @@ def tile_attend_gttt_k_pl_kernel(tc, kT, vT, W, ts, tk, cf, offs, out_0, out_1, 
 
         dk_sb = [sb.tile([P, SLOTS], F32, name="dk_sb%d" % j, tag="from_psum%d" % j) for j in range(LANES)]
         early = [P, HALF]
-        for j in range(2):
-            nc.scalar.copy(dk_sb[j][:, : early[j]], dk_pass(j, j, early[j] - P)[:, SLOTS - early[j] :])
+        nc.vector.tensor_copy(dk_sb[0][:, :P], dk_pass(0, 0, 0)[:, PAD:])
+        nc.scalar.copy(dk_sb[1][:, :HALF], dk_pass(1, 1, P)[:, HALF:])
         for j in range(LANES):
             first = early[j] if j < 2 else 0
             nc.scalar.copy(dk_sb[j][:, first:], dk_pass(j, j + 2, PAD)[:, first:])
@@ -258,8 +258,6 @@ def tile_attend_gttt_k_pl_kernel(tc, kT, vT, W, ts, tk, cf, offs, out_0, out_1, 
                 both = window[j][:, cols].unsqueeze(2).to_broadcast([P, cols.stop - cols.start, 2])
                 if c == 0 and j == 2:
                     nc.scalar.copy(pairs[c][:, 1], both)
-                elif c >= 3 and j == 2:
-                    nc.gpsimd.tensor_scalar(pairs[c][:, 1], both, 1.0, 0.0, MULT, ADD)
                 elif c >= 3 and j < 2:
                     nc.gpsimd.tensor_scalar(pairs[c][:, 0, :, j], window[j][:, cols], 1.0, 0.0, MULT, ADD)
                 elif c > 0 or j < 2:
@@ -271,32 +269,31 @@ def tile_attend_gttt_k_pl_kernel(tc, kT, vT, W, ts, tk, cf, offs, out_0, out_1, 
         y_scales = sb.tile([P, TOKENS // 4], U8, name="y_scales", align_bytes=64)
         y_bf = [sb.tile([P, c.stop - c.start, LANES], BF16, name="y_bf%d" % c.start, align_bytes=64) for c in CHUNKS]
 
+        def pieces(c):
+            return [slice(first, first + HALF) for first in range(0, CHUNKS[c].stop - CHUNKS[c].start, HALF)]
+
         def weave(c):
             y_words = y_bf[c][:].rearrange("p c t -> p (c t)").bitcast(F32).rearrange("p (c i u) -> p c u i", i=RUN, u=2)
             pair_words = pairs[c][:].rearrange("p u c e -> p u (c e)").bitcast(F32).rearrange("p u (c i) -> p c u i", i=RUN)
-            width = CHUNKS[c].stop - CHUNKS[c].start
-            cut = min(max(VECTOR_WEAVES - CHUNKS[c].start, 0), width) // RUN
-            if c == 0:
-                for h in range(2):
-                    nc.vector.tensor_copy(y_words[:, half(h, RUN)], pair_words[:, half(h, RUN)])
-            elif cut > 0:
-                nc.vector.tensor_copy(y_words[:, :cut], pair_words[:, :cut])
-            if cut < width // RUN:
-                nc.scalar.copy(y_words[:, cut:], pair_words[:, cut:])
+            for piece in pieces(c):
+                runs = slice(piece.start // RUN, piece.stop // RUN)
+                if CHUNKS[c].start < VECTOR_WEAVES:
+                    nc.vector.tensor_copy(y_words[:, runs], pair_words[:, runs])
+                else:
+                    nc.scalar.copy(y_words[:, runs], pair_words[:, runs])
 
         def hand_on(c):
             cols = CHUNKS[c]
-            width = cols.stop - cols.start
-            y_codes = sb.tile([P, width], U32, name="y_codes%d" % c, align_bytes=64)
+            y_codes = sb.tile([P, cols.stop - cols.start], U32, name="y_codes%d" % c, align_bytes=64)
             g, first = divmod(cols.start, TOKENS // 4)
-            quantize(nc, y_codes[:], y_scales[4 * g : P, first : first + width], y_bf[c][:], E4M3)
+            for piece in pieces(c):
+                scales = y_scales[4 * g : P, first + piece.start : first + piece.stop]
+                quantize(nc, y_codes[:, piece], scales, y_bf[c][:, piece, :], E4M3)
             nc.sync.dma_start(words_out[:, cols], y_codes[:].bitcast(I32))
 
-        for c in range(len(CHUNKS) + 1):
-            if c < len(CHUNKS):
-                weave(c)
-            if c > 0:
-                hand_on(c - 1)
+        for c in range(len(CHUNKS)):
+            weave(c)
+            hand_on(c)
         for q in range(4):
             queue = nc.sync
             rows = out_2[0].bitcast(I32)[4 * q : 4 * q + 4, :].rearrange("r (g x) -> g r x", g=4)

@@ -29,6 +29,7 @@ PER_COLUMN = 16
 ROW = P - 1
 
 CHUNKS = [slice(0, SLOTS), slice(512, 1024), slice(1024, 1536), slice(1536, 1792), slice(1792, 2048)]
+STORES = [slice(0, 768), slice(768, 1280), slice(1280, 1792), slice(1792, 2048)]
 VECTOR_WEAVES = 1536
 
 FLOPS = 2 * 2 * D * D * SLOTS
@@ -142,22 +143,25 @@ def tile_attend_gttt_k_pl_kernel(tc, kT, vT, W, ts, tk, cf, offs, out_0, out_1, 
         for h in range(2):
             quantize(nc, k_codes[:, half(h)], k_scales[:, half(h)], k_bf[:, half(h), :], E4M3)
 
-        u_scaled = []
-        for m in range(SLOT_TILES):
+        u_scaled = {}
+        for m in (1, 2, 0, 3):
             cols = slice(P * m, P * (m + 1))
             u_psum = bank(m, "u_psum%d" % m, [P, D])
             nc.tensor.matmul_mx(
                 u_psum[:], lhsT=k_codes[:, cols].bitcast(E4M3), lhsT_scale=k_scales[:, cols],
                 rhs=wd_codes[:].bitcast(E4M3), rhs_scale=wd_scales[:], start=True, stop=True,
             )
-            u_scaled.append(sb.tile([P, LANES, P], F32, name="u_scaled%d" % m, tag="from_psum%d" % m))
+            u_scaled[m] = sb.tile([P, LANES, P], F32, name="u_scaled%d" % m, tag="from_psum%d" % m)
             nc.scalar.activation(u_scaled[m][:].rearrange("p t s -> p (t s)"), u_psum[:], COPY, scale=tstk2_col[:, m : m + 1])
-        u_term = sb.tile([P, LANES, SLOTS], F32, name="u_term")
-        for t in range(LANES):
-            u_turned = bank(SLOT_TILES + t, "u_turned%d" % t, [P, SLOTS])
-            for m in range(SLOT_TILES):
-                nc.tensor.transpose(u_turned[:, P * m : P * (m + 1)], u_scaled[m][:, t, :], ident[:])
-            nc.scalar.activation(u_term[:, t, :], u_turned[:], COPY, scale=cf2[:, t : t + 1])
+        u_term = sb.tile([P, LANES, SLOT_TILES, P], F32, name="u_term")
+        for b, (u, tiles) in enumerate([(0, slice(1, 3)), (0, slice(0, 4, 3)), (1, slice(0, 4, 3)), (1, slice(1, 3))]):
+            u_turned = bank(SLOT_TILES + b, "u_turned%d" % b, [P, 2, 2, P])
+            for i in range(2):
+                for n, m in enumerate(range(SLOT_TILES)[tiles]):
+                    nc.tensor.transpose(u_turned[:, i, n, :], u_scaled[m][:, 2 * u + i, :], ident[:])
+            for i in range(2):
+                t = 2 * u + i
+                nc.scalar.activation(u_term[:, t, tiles, :], u_turned[:, i], COPY, scale=cf2[:, t : t + 1])
 
         for j in range(1, LANES):
             window.append(sb.tile([P, TOKENS], F32, name="window%d" % j, tag="then_window%d" % j, align_bytes=64))
@@ -191,7 +195,7 @@ def tile_attend_gttt_k_pl_kernel(tc, kT, vT, W, ts, tk, cf, offs, out_0, out_1, 
 
         def subtract_pair(m, u):
             out = e_pairs[:, m - 1, u].rearrange("p (c i) t -> p c t i", i=RUN)
-            u_rows = u_term[:, 2 * u : 2 * u + 2, P * m : P * (m + 1)]
+            u_rows = u_term[:, 2 * u : 2 * u + 2, m, :]
             nc.vector.tensor_tensor(out, walk(u_rows), walk(two_rows(v_term, v_row(2 * u, m), v_row(2 * u + 1, m))), SUB)
 
         def weave_e(m):
@@ -203,7 +207,7 @@ def tile_attend_gttt_k_pl_kernel(tc, kT, vT, W, ts, tk, cf, offs, out_0, out_1, 
         def subtract(m, e_bf):
             out = e_bf.rearrange("p (c i) t -> p c t i", i=RUN)
             v_rows = v_term[:, m : LANES * SLOT_TILES : SLOT_TILES, :]
-            nc.vector.tensor_tensor(out, walk(u_term[:, :, P * m : P * (m + 1)]), walk(v_rows), SUB)
+            nc.vector.tensor_tensor(out, walk(u_term[:, :, m, :]), walk(v_rows), SUB)
 
         def quantize_e(m, e_bf):
             cols = slice(PAD + P * m, PAD + P * (m + 1))
@@ -255,9 +259,10 @@ def tile_attend_gttt_k_pl_kernel(tc, kT, vT, W, ts, tk, cf, offs, out_0, out_1, 
             nc.vector.tensor_copy(window[j][:].indirect(offsets[:, first // PER_COLUMN :]), dk_sb[j][:, first:])
             nc.sync.dma_start(out_0.rearrange("(p j) c -> p j c", j=LANES)[:, j, :], window[j][:])
             for c, cols in enumerate(CHUNKS):
-                both = window[j][:, cols].unsqueeze(2).to_broadcast([P, cols.stop - cols.start, 2])
                 if c == 0 and j == 2:
-                    nc.scalar.copy(pairs[c][:, 1], both)
+                    nc.scalar.copy(pairs[c][:, 1, :, 0], window[j][:, cols])
+                    ends = slice(HALF - 1, SLOTS, HALF)
+                    nc.scalar.copy(pairs[c][:, 1, ends, :], window[j][:, ends].unsqueeze(2).to_broadcast([P, 2, 2]))
                 elif c >= 3 and j < 2:
                     nc.gpsimd.tensor_scalar(pairs[c][:, 0, :, j], window[j][:, cols], 1.0, 0.0, MULT, ADD)
                 elif c > 0 or j < 2:
@@ -267,6 +272,7 @@ def tile_attend_gttt_k_pl_kernel(tc, kT, vT, W, ts, tk, cf, offs, out_0, out_1, 
 
         words_out = out_1[0].rearrange("p c l -> p (c l)").bitcast(I32)
         y_scales = sb.tile([P, TOKENS // 4], U8, name="y_scales", align_bytes=64)
+        y_codes = sb.tile([P, TOKENS], U32, name="y_codes", align_bytes=64)
         y_bf = [sb.tile([P, c.stop - c.start, LANES], BF16, name="y_bf%d" % c.start, align_bytes=64) for c in CHUNKS]
 
         def pieces(c):
@@ -284,12 +290,14 @@ def tile_attend_gttt_k_pl_kernel(tc, kT, vT, W, ts, tk, cf, offs, out_0, out_1, 
 
         def hand_on(c):
             cols = CHUNKS[c]
-            y_codes = sb.tile([P, cols.stop - cols.start], U32, name="y_codes%d" % c, align_bytes=64)
             g, first = divmod(cols.start, TOKENS // 4)
             for piece in pieces(c):
                 scales = y_scales[4 * g : P, first + piece.start : first + piece.stop]
-                quantize(nc, y_codes[:, piece], scales, y_bf[c][:, piece, :], E4M3)
-            nc.sync.dma_start(words_out[:, cols], y_codes[:].bitcast(I32))
+                done = cols.start + piece.stop
+                quantize(nc, y_codes[:, done - HALF : done], scales, y_bf[c][:, piece, :], E4M3)
+                for store in STORES:
+                    if store.stop == done:
+                        nc.sync.dma_start(words_out[:, store], y_codes[:, store].bitcast(I32))
 
         for c in range(len(CHUNKS)):
             weave(c)

@@ -28,9 +28,13 @@ RUN = 4
 PER_COLUMN = 16
 ROW = P - 1
 
+GROUPS = 4
+GROUP = TOKENS // GROUPS
+
 CHUNKS = [slice(0, SLOTS), slice(512, 1024), slice(1024, 1536), slice(1536, 1792), slice(1792, 2048)]
 STORES = [slice(0, 768), slice(768, 1280), slice(1280, 1792), slice(1792, 2048)]
 VECTOR_WEAVES = 1536
+SCALAR_ROUNDS = 1536
 
 FLOPS = 2 * 2 * D * D * SLOTS
 BYTES = 4 * (3 * D * TOKENS + D * D + 2 * TOKENS + D) + 2 * P * SLOTS // PER_COLUMN + D * TOKENS + D // 32 * TOKENS
@@ -143,6 +147,7 @@ def tile_attend_gttt_k_pl_kernel(tc, kT, vT, W, ts, tk, cf, offs, out_0, out_1, 
         for h in range(2):
             quantize(nc, k_codes[:, half(h)], k_scales[:, half(h)], k_bf[:, half(h), :], E4M3)
 
+        inner, outer = slice(1, 3), slice(0, SLOT_TILES, 3)
         u_scaled = {}
         for m in (1, 2, 0, 3):
             cols = slice(P * m, P * (m + 1))
@@ -154,7 +159,7 @@ def tile_attend_gttt_k_pl_kernel(tc, kT, vT, W, ts, tk, cf, offs, out_0, out_1, 
             u_scaled[m] = sb.tile([P, LANES, P], F32, name="u_scaled%d" % m, tag="from_psum%d" % m)
             nc.scalar.activation(u_scaled[m][:].rearrange("p t s -> p (t s)"), u_psum[:], COPY, scale=tstk2_col[:, m : m + 1])
         u_term = sb.tile([P, LANES, SLOT_TILES, P], F32, name="u_term")
-        for b, (u, tiles) in enumerate([(0, slice(1, 3)), (0, slice(0, 4, 3)), (1, slice(0, 4, 3)), (1, slice(1, 3))]):
+        for b, (u, tiles) in enumerate([(0, inner), (0, outer), (1, outer), (1, inner)]):
             u_turned = bank(SLOT_TILES + b, "u_turned%d" % b, [P, 2, 2, P])
             for i in range(2):
                 for n, m in enumerate(range(SLOT_TILES)[tiles]):
@@ -177,7 +182,7 @@ def tile_attend_gttt_k_pl_kernel(tc, kT, vT, W, ts, tk, cf, offs, out_0, out_1, 
         v_term = sb.tile([P, LANES * SLOT_TILES, P], F32, name="v_term")
 
         def v_row(t, m):
-            return SLOT_TILES * t + (m if t < LANES - 1 else {0: 0, 1: 3, 2: 0, 3: 3}[m])
+            return SLOT_TILES * t + (m if t < LANES - 1 else 3 * (m % 2))
 
         def look_up_v(t, m, tiles):
             first, last = P * m, P * (m + tiles)
@@ -188,15 +193,13 @@ def tile_attend_gttt_k_pl_kernel(tc, kT, vT, W, ts, tk, cf, offs, out_0, out_1, 
         def walk(planes):
             return planes.rearrange("p t (c i) -> p c t i", i=RUN)
 
-        def two_rows(tile, first, second):
-            return tile[:, first : second + 1 : second - first]
-
         e_pairs = sb.tile([P, 2, 2, P, 2], BF16, name="e_pairs", tag="v_pool2", align_bytes=64)
 
         def subtract_pair(m, u):
             out = e_pairs[:, m - 1, u].rearrange("p (c i) t -> p c t i", i=RUN)
-            u_rows = u_term[:, 2 * u : 2 * u + 2, m, :]
-            nc.vector.tensor_tensor(out, walk(u_rows), walk(two_rows(v_term, v_row(2 * u, m), v_row(2 * u + 1, m))), SUB)
+            low, high = v_row(2 * u, m), v_row(2 * u + 1, m)
+            v_rows = v_term[:, low : high + 1 : high - low]
+            nc.vector.tensor_tensor(out, walk(u_term[:, 2 * u : 2 * u + 2, m, :]), walk(v_rows), SUB)
 
         def weave_e(m):
             e_bf = sb.tile([P, P, LANES], BF16, name="e_bf%d" % m, align_bytes=64)
@@ -223,7 +226,7 @@ def tile_attend_gttt_k_pl_kernel(tc, kT, vT, W, ts, tk, cf, offs, out_0, out_1, 
         subtract(0, e_first[:])
         subtract_pair(1, 1)
         quantize_e(0, e_first[:])
-        for m in range(2, 4):
+        for m in range(2, SLOT_TILES):
             look_up_v(LANES - 1, m, 1)
         subtract_pair(2, 1)
         quantize_e(1, weave_e(1))
@@ -233,7 +236,8 @@ def tile_attend_gttt_k_pl_kernel(tc, kT, vT, W, ts, tk, cf, offs, out_0, out_1, 
         quantize_e(3, e_last)
         quantize_e(2, e_third)
 
-        pairs = [sb.tile([P, 2, c.stop - c.start, 2], BF16, name="pairs%d" % c.start, align_bytes=64) for c in CHUNKS]
+        pairs = {c: sb.tile([P, 2, CHUNKS[c].stop - CHUNKS[c].start, 2], BF16, name="pairs%d" % c, align_bytes=64) for c in range(1, len(CHUNKS))}
+        y_bf = [sb.tile([P, c.stop - c.start, LANES], BF16, name="y_bf%d" % c.start, align_bytes=64) for c in CHUNKS]
 
         def dk_pass(j, b, first):
             cols = slice(P * j, P * (j + 1))
@@ -246,34 +250,31 @@ def tile_attend_gttt_k_pl_kernel(tc, kT, vT, W, ts, tk, cf, offs, out_0, out_1, 
             return dk_psum
 
         dk_sb = [sb.tile([P, SLOTS], F32, name="dk_sb%d" % j, tag="from_psum%d" % j) for j in range(LANES)]
-        early = [P, HALF]
+        early = [P, HALF, 0, 0]
         nc.vector.tensor_copy(dk_sb[0][:, :P], dk_pass(0, 0, 0)[:, PAD:])
         nc.scalar.copy(dk_sb[1][:, :HALF], dk_pass(1, 1, P)[:, HALF:])
         for j in range(LANES):
-            first = early[j] if j < 2 else 0
-            nc.scalar.copy(dk_sb[j][:, first:], dk_pass(j, j + 2, PAD)[:, first:])
+            nc.scalar.copy(dk_sb[j][:, early[j] :], dk_pass(j, j + 2, PAD)[:, early[j] :])
         nc.vector.tensor_tensor(window[0][:].indirect(offsets[:, : P // PER_COLUMN]), dk_sb[0][:, :P], zeros[:], ADD)
         nc.vector.tensor_copy(window[1][:].indirect(offsets[:, half(0, PER_COLUMN)]), dk_sb[1][:, half(0)])
         for j in range(LANES):
-            first = early[j] if j < 2 else 0
-            nc.vector.tensor_copy(window[j][:].indirect(offsets[:, first // PER_COLUMN :]), dk_sb[j][:, first:])
+            nc.vector.tensor_copy(window[j][:].indirect(offsets[:, early[j] // PER_COLUMN :]), dk_sb[j][:, early[j] :])
             nc.sync.dma_start(out_0.rearrange("(p j) c -> p j c", j=LANES)[:, j, :], window[j][:])
             for c, cols in enumerate(CHUNKS):
-                if c == 0 and j == 2:
-                    nc.scalar.copy(pairs[c][:, 1, :, 0], window[j][:, cols])
-                    ends = slice(HALF - 1, SLOTS, HALF)
-                    nc.scalar.copy(pairs[c][:, 1, ends, :], window[j][:, ends].unsqueeze(2).to_broadcast([P, 2, 2]))
-                elif c >= 3 and j < 2:
-                    nc.gpsimd.tensor_scalar(pairs[c][:, 0, :, j], window[j][:, cols], 1.0, 0.0, MULT, ADD)
-                elif c > 0 or j < 2:
+                if c > 0:
                     nc.scalar.copy(pairs[c][:, j // 2, :, j % 2], window[j][:, cols])
+                elif j < LANES - 1:
+                    nc.gpsimd.tensor_scalar(y_bf[c][:, :, j], window[j][:, cols], 1.0, 0.0, MULT, ADD)
+                if j == 2 and c == 0:
+                    ends = slice(HALF - 1, SLOTS, HALF)
+                    both = window[j][:, ends].unsqueeze(2).to_broadcast([P, 2, 2])
+                    nc.gpsimd.tensor_scalar(y_bf[c][:, ends, 2:], both, 1.0, 0.0, MULT, ADD)
         for h in range(2):
-            nc.vector.tensor_copy(pairs[0][:, 1, half(h), 1], window[LANES - 1][:, half(h)])
+            nc.vector.tensor_copy(y_bf[0][:, half(h), LANES - 1], window[LANES - 1][:, half(h)])
 
         words_out = out_1[0].rearrange("p c l -> p (c l)").bitcast(I32)
-        y_scales = sb.tile([P, TOKENS // 4], U8, name="y_scales", align_bytes=64)
+        y_scales = sb.tile([P, GROUP], U8, name="y_scales", align_bytes=64)
         y_codes = sb.tile([P, TOKENS], U32, name="y_codes", align_bytes=64)
-        y_bf = [sb.tile([P, c.stop - c.start, LANES], BF16, name="y_bf%d" % c.start, align_bytes=64) for c in CHUNKS]
 
         def pieces(c):
             return [slice(first, first + HALF) for first in range(0, CHUNKS[c].stop - CHUNKS[c].start, HALF)]
@@ -290,7 +291,7 @@ def tile_attend_gttt_k_pl_kernel(tc, kT, vT, W, ts, tk, cf, offs, out_0, out_1, 
 
         def hand_on(c):
             cols = CHUNKS[c]
-            g, first = divmod(cols.start, TOKENS // 4)
+            g, first = divmod(cols.start, GROUP)
             for piece in pieces(c):
                 scales = y_scales[4 * g : P, first + piece.start : first + piece.stop]
                 done = cols.start + piece.stop
@@ -300,9 +301,10 @@ def tile_attend_gttt_k_pl_kernel(tc, kT, vT, W, ts, tk, cf, offs, out_0, out_1, 
                         nc.sync.dma_start(words_out[:, store], y_codes[:, store].bitcast(I32))
 
         for c in range(len(CHUNKS)):
-            weave(c)
+            if c > 0:
+                weave(c)
             hand_on(c)
         for q in range(4):
-            queue = nc.sync
-            rows = out_2[0].bitcast(I32)[4 * q : 4 * q + 4, :].rearrange("r (g x) -> g r x", g=4)
+            rows = out_2[0].bitcast(I32)[4 * q : 4 * q + 4, :].rearrange("r (g x) -> g r x", g=GROUPS)
+            queue = nc.scalar if q < 2 else nc.sync
             queue.dma_start(rows, y_scales[32 * q : 32 * q + 16, :].bitcast(I32))

@@ -31,7 +31,7 @@ ROW = P - 1
 GROUPS = 4
 GROUP = TOKENS // GROUPS
 
-CHUNKS = [slice(0, SLOTS), slice(512, 1024), slice(1024, 1536), slice(1536, 1792), slice(1792, 2048)]
+CHUNKS = [slice(0, 512), slice(512, 1024), slice(1024, 1536), slice(1536, 1792), slice(1792, 2048)]
 STORES = [slice(0, 768), slice(768, 1280), slice(1280, 1792), slice(1792, 2048)]
 VECTOR_WEAVES = 1536
 SCALAR_ROUNDS = 1536
@@ -53,6 +53,7 @@ def tile_attend_gttt_k_pl_kernel(tc, kT, vT, W, ts, tk, cf, offs, out_0, out_1, 
     with ExitStack() as ctx:
         sb = ctx.enter_context(tc.tile_pool(name="sb", bufs=1))
         ps = ctx.enter_context(tc.psum_pool(name="ps", bufs=1))
+        placed = ctx.enter_context(tc.tile_pool(name="placed", bufs=1))
 
         def bank(b, name, shape):
             return ps.tile(shape, F32, name=name, tag="bank%d" % b)
@@ -73,7 +74,7 @@ def tile_attend_gttt_k_pl_kernel(tc, kT, vT, W, ts, tk, cf, offs, out_0, out_1, 
         nc.sync.dma_start(w_raw[:], W.rearrange("(p j) f -> p j f", j=LANES))
         nc.sync.dma_start(offsets[:], offs)
         k_pool = [sb.tile([P, TOKENS], F32, name="k_pool%d" % j, tag="k_pool%d" % j, align_bytes=64) for j in range(LANES)]
-        v_pool = [sb.tile([P, TOKENS], F32, name="v_pool%d" % t, tag="v_pool%d" % t, align_bytes=64) for t in range(LANES)]
+        v_pool = [placed.tile([P, TOKENS], F32, name="v_pool%d" % t, offset=4 * TOKENS * t, align_bytes=64) for t in range(LANES)]
         for j in range(LANES):
             nc.sync.dma_start(k_pool[j][:], kT.rearrange("(p j) c -> p j c", j=LANES)[:, j, :])
         for t in range(LANES):
@@ -147,9 +148,9 @@ def tile_attend_gttt_k_pl_kernel(tc, kT, vT, W, ts, tk, cf, offs, out_0, out_1, 
         for h in range(2):
             quantize(nc, k_codes[:, half(h)], k_scales[:, half(h)], k_bf[:, half(h), :], E4M3)
 
-        inner, outer = slice(1, 3), slice(0, SLOT_TILES, 3)
+        inner, outer = slice(0, 2), slice(2, SLOT_TILES)
         u_scaled = {}
-        for m in (1, 2, 0, 3):
+        for m in range(SLOT_TILES):
             cols = slice(P * m, P * (m + 1))
             u_psum = bank(m, "u_psum%d" % m, [P, D])
             nc.tensor.matmul_mx(
@@ -159,7 +160,7 @@ def tile_attend_gttt_k_pl_kernel(tc, kT, vT, W, ts, tk, cf, offs, out_0, out_1, 
             u_scaled[m] = sb.tile([P, LANES, P], F32, name="u_scaled%d" % m, tag="from_psum%d" % m)
             nc.scalar.activation(u_scaled[m][:].rearrange("p t s -> p (t s)"), u_psum[:], COPY, scale=tstk2_col[:, m : m + 1])
         u_term = sb.tile([P, LANES, SLOT_TILES, P], F32, name="u_term")
-        for b, (u, tiles) in enumerate([(0, inner), (0, outer), (1, outer), (1, inner)]):
+        for b, (u, tiles) in enumerate([(0, inner), (1, inner), (0, outer), (1, outer)]):
             u_turned = bank(SLOT_TILES + b, "u_turned%d" % b, [P, 2, 2, P])
             for i in range(2):
                 for n, m in enumerate(range(SLOT_TILES)[tiles]):
@@ -172,40 +173,31 @@ def tile_attend_gttt_k_pl_kernel(tc, kT, vT, W, ts, tk, cf, offs, out_0, out_1, 
             window.append(sb.tile([P, TOKENS], F32, name="window%d" % j, tag="then_window%d" % j, align_bytes=64))
             nc.gpsimd.memset(window[j][:], 0.0)
 
-        e_codes = sb.tile([P, PAD + SLOTS], U32, name="e_codes", align_bytes=64)
-        e_scales = sb.tile([P, PAD + SLOTS], U8, name="e_scales", align_bytes=64)
-        zeros = sb.tile([P, P], F32, name="zeros")
-        nc.vector.memset(e_codes[:, :PAD], 0)
-        nc.vector.memset(e_scales[:, :PAD], 0)
-        nc.vector.memset(zeros[:], 0.0)
+        e_codes = sb.tile([P, SLOTS], U32, name="e_codes", align_bytes=64)
+        e_scales = sb.tile([P, SLOTS], U8, name="e_scales", align_bytes=64)
 
-        v_term = sb.tile([P, LANES * SLOT_TILES, P], F32, name="v_term")
-
-        def v_row(t, m):
-            return SLOT_TILES * t + (m if t < LANES - 1 else 3 * (m % 2))
+        v_term = sb.tile([P, LANES * SLOT_TILES, P], F32, name="v_term", align_bytes=64)
 
         def look_up_v(t, m, tiles):
             first, last = P * m, P * (m + tiles)
             listed = v_pool[t][:].indirect(offsets[:, first // PER_COLUMN : last // PER_COLUMN])
-            rows = v_term[:, v_row(t, m) : v_row(t, m) + tiles, :].rearrange("p m s -> p (m s)")
+            rows = v_term[:, SLOT_TILES * t + m : SLOT_TILES * t + m + tiles, :].rearrange("p m s -> p (m s)")
             nc.vector.tensor_tensor(rows, listed, v_factor[:, t, first:last], MULT)
 
         def walk(planes):
             return planes.rearrange("p t (c i) -> p c t i", i=RUN)
 
-        e_pairs = sb.tile([P, 2, 2, P, 2], BF16, name="e_pairs", tag="v_pool2", align_bytes=64)
+        e_pairs = placed.tile([P, 2, 2, P, 2], BF16, name="e_pairs", offset=4 * TOKENS * 2, align_bytes=64)
 
         def subtract_pair(m, u):
-            out = e_pairs[:, m - 1, u].rearrange("p (c i) t -> p c t i", i=RUN)
-            low, high = v_row(2 * u, m), v_row(2 * u + 1, m)
-            v_rows = v_term[:, low : high + 1 : high - low]
+            out = e_pairs[:, m, u].rearrange("p (c i) t -> p c t i", i=RUN)
+            low = SLOT_TILES * 2 * u + m
+            v_rows = v_term[:, low : low + SLOT_TILES + 1 : SLOT_TILES]
             nc.vector.tensor_tensor(out, walk(u_term[:, 2 * u : 2 * u + 2, m, :]), walk(v_rows), SUB)
 
-        def weave_e(m):
-            e_bf = sb.tile([P, P, LANES], BF16, name="e_bf%d" % m, align_bytes=64)
-            e_words = e_bf[:].rearrange("p c t -> p (c t)").bitcast(F32).rearrange("p (c i u) -> p c u i", i=RUN, u=2)
-            nc.scalar.copy(e_words, walk(e_pairs[:, m - 1].rearrange("p r c e -> p r (c e)").bitcast(F32)))
-            return e_bf[:]
+        def weave_e(m, e_bf):
+            e_words = e_bf.rearrange("p c t -> p (c t)").bitcast(F32).rearrange("p (c i u) -> p c u i", i=RUN, u=2)
+            nc.vector.tensor_copy(e_words, walk(e_pairs[:, m].rearrange("p r c e -> p r (c e)").bitcast(F32)))
 
         def subtract(m, e_bf):
             out = e_bf.rearrange("p (c i) t -> p c t i", i=RUN)
@@ -213,64 +205,84 @@ def tile_attend_gttt_k_pl_kernel(tc, kT, vT, W, ts, tk, cf, offs, out_0, out_1, 
             nc.vector.tensor_tensor(out, walk(u_term[:, :, m, :]), walk(v_rows), SUB)
 
         def quantize_e(m, e_bf):
-            cols = slice(PAD + P * m, PAD + P * (m + 1))
+            cols = slice(P * m, P * (m + 1))
             quantize(nc, e_codes[:, cols], e_scales[:, cols], e_bf, E5M2)
 
         for t in range(LANES - 1):
             look_up_v(t, 0, SLOT_TILES)
-        for m in (1, 2):
+        for m in range(2):
             subtract_pair(m, 0)
         for m in range(2):
             look_up_v(LANES - 1, m, 1)
-        e_first = sb.tile([P, P, LANES], BF16, name="e_first", align_bytes=64)
-        subtract(0, e_first[:])
-        subtract_pair(1, 1)
-        quantize_e(0, e_first[:])
+        e_bf = [v_term[:, LANES * SLOT_TILES - 2 :, :].rearrange("p m s -> p (m s)").bitcast(BF16).rearrange("p (c t) -> p c t", t=LANES)]
+        for m in range(1, SLOT_TILES):
+            e_bf.append(sb.tile([P, P, LANES], BF16, name="e_bf%d" % m, tag="e_bf%d" % m, align_bytes=64)[:])
+        for m in range(2):
+            subtract_pair(m, 1)
+        for m in range(2):
+            weave_e(m, e_bf[m])
+        for m in range(2):
+            quantize_e(m, e_bf[m])
         for m in range(2, SLOT_TILES):
             look_up_v(LANES - 1, m, 1)
-        subtract_pair(2, 1)
-        quantize_e(1, weave_e(1))
-        e_last = e_pairs[:, 0].rearrange("p u c e -> p (u c e)").rearrange("p (c t) -> p c t", t=LANES)
-        subtract(3, e_last)
-        e_third = weave_e(2)
-        quantize_e(3, e_last)
-        quantize_e(2, e_third)
+        for m in range(2, SLOT_TILES):
+            subtract(m, e_bf[m])
+        for m in range(2, SLOT_TILES):
+            quantize_e(m, e_bf[m])
 
-        pairs = {c: sb.tile([P, 2, CHUNKS[c].stop - CHUNKS[c].start, 2], BF16, name="pairs%d" % c, align_bytes=64) for c in range(1, len(CHUNKS))}
-        y_bf = [sb.tile([P, c.stop - c.start, LANES], BF16, name="y_bf%d" % c.start, align_bytes=64) for c in CHUNKS]
-
-        def dk_pass(j, b, first):
-            cols = slice(P * j, P * (j + 1))
-            moving = slice(first, first + SLOTS)
-            dk_psum = bank(b, "dk_psum%d" % b, [P, SLOTS])
-            nc.tensor.matmul_mx(
-                dk_psum[:], lhsT=wf_codes[:, cols].bitcast(E4M3), lhsT_scale=wf_scales[:, cols],
-                rhs=e_codes[:, moving].bitcast(E5M2), rhs_scale=e_scales[:, moving], start=True, stop=True,
-            )
+        def dk_passes(b, h, planes):
+            dk_psum = bank(b, "dk_psum%d" % b, [P, len(planes), HALF])
+            for n, j in enumerate(planes):
+                cols = slice(P * j, P * (j + 1))
+                nc.tensor.matmul_mx(
+                    dk_psum[:, n, :], lhsT=wf_codes[:, cols].bitcast(E4M3), lhsT_scale=wf_scales[:, cols],
+                    rhs=e_codes[:, half(h)].bitcast(E5M2), rhs_scale=e_scales[:, half(h)], start=True, stop=True,
+                )
             return dk_psum
 
-        dk_sb = [sb.tile([P, SLOTS], F32, name="dk_sb%d" % j, tag="from_psum%d" % j) for j in range(LANES)]
-        early = [P, HALF, 0, 0]
-        nc.vector.tensor_copy(dk_sb[0][:, :P], dk_pass(0, 0, 0)[:, PAD:])
-        nc.scalar.copy(dk_sb[1][:, :HALF], dk_pass(1, 1, P)[:, HALF:])
-        for j in range(LANES):
-            nc.scalar.copy(dk_sb[j][:, early[j] :], dk_pass(j, j + 2, PAD)[:, early[j] :])
-        nc.vector.tensor_tensor(window[0][:].indirect(offsets[:, : P // PER_COLUMN]), dk_sb[0][:, :P], zeros[:], ADD)
-        nc.vector.tensor_copy(window[1][:].indirect(offsets[:, half(0, PER_COLUMN)]), dk_sb[1][:, half(0)])
-        for j in range(LANES):
-            nc.vector.tensor_copy(window[j][:].indirect(offsets[:, early[j] // PER_COLUMN :]), dk_sb[j][:, early[j] :])
+        groups = [(0, (0,)), (0, (1,)), (0, (2, 3)), (1, (0,)), (1, (1,)), (1, (2, 3))]
+        dk_psum = [dk_passes(b, h, planes) for b, (h, planes) in enumerate(groups)]
+        dk_first = sb.tile([P, 1, HALF], F32, name="dk_first", tag="from_psum0")
+        dk_low = sb.tile([P, LANES - 1, HALF], F32, name="dk_low", tag="e_bf3", align_bytes=64)
+        dk_high = sb.tile([P, LANES, HALF], F32, name="dk_high")
+        dk_sb = [dk_first[:], dk_low[:, 0:1], dk_low[:, 1:3], dk_high[:, 0:1], dk_high[:, 1:2], dk_high[:, 2:4]]
+        dk = {(j, h): dk_sb[b][:, n, :] for b, (h, planes) in enumerate(groups) for n, j in enumerate(planes)}
+
+        def listed(j, h):
+            return window[j][:].indirect(offsets[:, half(h, PER_COLUMN)])
+
+        def store(j):
             nc.sync.dma_start(out_0.rearrange("(p j) c -> p j c", j=LANES)[:, j, :], window[j][:])
+
+        nc.scalar.copy(dk_sb[0], dk_psum[0][:])
+        nc.scalar.activation(listed(0, 0), dk[0, 0], COPY)
+        for b in range(1, 5):
+            nc.vector.tensor_copy(dk_sb[b], dk_psum[b][:])
+        nc.vector.tensor_copy(listed(0, 1), dk[0, 1])
+        store(0)
+        nc.scalar.activation(listed(1, 0), dk[1, 0], COPY)
+        nc.vector.tensor_copy(dk_sb[5], dk_psum[5][:])
+        nc.vector.tensor_copy(listed(1, 1), dk[1, 1])
+        store(1)
+        for j in range(2, LANES):
+            for h in range(2):
+                nc.scalar.activation(listed(j, h), dk[j, h], COPY)
+            store(j)
+
+        pairs = [sb.tile([P, 2, c.stop - c.start, 2], BF16, name="pairs%d" % c.start, align_bytes=64) for c in CHUNKS]
+        y_bf = [sb.tile([P, c.stop - c.start, LANES], BF16, name="y_bf%d" % c.start, align_bytes=64) for c in CHUNKS]
+        for j in range(LANES - 1):
             for c, cols in enumerate(CHUNKS):
-                if c > 0:
-                    nc.scalar.copy(pairs[c][:, j // 2, :, j % 2], window[j][:, cols])
-                elif j < LANES - 1:
-                    nc.gpsimd.tensor_scalar(y_bf[c][:, :, j], window[j][:, cols], 1.0, 0.0, MULT, ADD)
-                if j == 2 and c == 0:
-                    ends = slice(HALF - 1, SLOTS, HALF)
-                    both = window[j][:, ends].unsqueeze(2).to_broadcast([P, 2, 2])
-                    nc.gpsimd.tensor_scalar(y_bf[c][:, ends, 2:], both, 1.0, 0.0, MULT, ADD)
+                nc.vector.tensor_copy(pairs[c][:, j // 2, :, j % 2], window[j][:, cols])
+                if j == 2 and c > 0:
+                    last = slice(cols.stop - 1, cols.stop)
+                    both = window[j][:, last].unsqueeze(2).to_broadcast([P, 1, 2])
+                    nc.vector.tensor_copy(pairs[c][:, 1, cols.stop - cols.start - 1 :, :], both)
         for h in range(2):
-            nc.vector.tensor_copy(y_bf[0][:, half(h), LANES - 1], window[LANES - 1][:, half(h)])
+            nc.vector.tensor_copy(pairs[0][:, 1, half(h), 1], window[LANES - 1][:, half(h)])
+        for c, cols in enumerate(CHUNKS):
+            if c > 0:
+                nc.scalar.copy(pairs[c][:, 1, :, 1], window[LANES - 1][:, cols])
 
         words_out = out_1[0].rearrange("p c l -> p (c l)").bitcast(I32)
         y_scales = sb.tile([P, GROUP], U8, name="y_scales", align_bytes=64)
@@ -301,8 +313,7 @@ def tile_attend_gttt_k_pl_kernel(tc, kT, vT, W, ts, tk, cf, offs, out_0, out_1, 
                         nc.sync.dma_start(words_out[:, store], y_codes[:, store].bitcast(I32))
 
         for c in range(len(CHUNKS)):
-            if c > 0:
-                weave(c)
+            weave(c)
             hand_on(c)
         for q in range(4):
             rows = out_2[0].bitcast(I32)[4 * q : 4 * q + 4, :].rearrange("r (g x) -> g r x", g=GROUPS)

@@ -31,9 +31,9 @@ ROW = P - 1
 GROUPS = 4
 GROUP = TOKENS // GROUPS
 
-CHUNKS = [slice(0, 512), slice(512, 1024), slice(1024, 1536), slice(1536, 1792), slice(1792, 2048)]
-STORES = [slice(0, 768), slice(768, 1280), slice(1280, 1792), slice(1792, 2048)]
-VECTOR_WEAVES = 1536
+CHUNKS = [slice(0, 1024), slice(1024, 2048)]
+STORES = [slice(0, 1024), slice(1024, 1536), slice(1536, 2048)]
+VECTOR_WEAVES = 1280
 SCALAR_ROUNDS = 1536
 
 FLOPS = 2 * 2 * D * D * SLOTS
@@ -160,7 +160,7 @@ def tile_attend_gttt_k_pl_kernel(tc, kT, vT, W, ts, tk, cf, offs, out_0, out_1, 
             u_scaled[m] = sb.tile([P, LANES, P], F32, name="u_scaled%d" % m, tag="from_psum%d" % m)
             nc.scalar.activation(u_scaled[m][:].rearrange("p t s -> p (t s)"), u_psum[:], COPY, scale=tstk2_col[:, m : m + 1])
         u_term = sb.tile([P, LANES, SLOT_TILES, P], F32, name="u_term")
-        for b, (u, tiles) in enumerate([(0, inner), (1, inner), (0, outer), (1, outer)]):
+        for b, (u, tiles) in enumerate([(0, inner), (0, outer), (1, inner), (1, outer)]):
             u_turned = bank(SLOT_TILES + b, "u_turned%d" % b, [P, 2, 2, P])
             for i in range(2):
                 for n, m in enumerate(range(SLOT_TILES)[tiles]):
@@ -176,59 +176,66 @@ def tile_attend_gttt_k_pl_kernel(tc, kT, vT, W, ts, tk, cf, offs, out_0, out_1, 
         e_codes = sb.tile([P, SLOTS], U32, name="e_codes", align_bytes=64)
         e_scales = sb.tile([P, SLOTS], U8, name="e_scales", align_bytes=64)
 
-        v_term = sb.tile([P, LANES * SLOT_TILES, P], F32, name="v_term", align_bytes=64)
+        v_term = sb.tile([P, LANES, SLOTS], F32, name="v_term", align_bytes=64)
+        u_flat = u_term[:].rearrange("p t m s -> p t (m s)")
 
-        def look_up_v(t, m, tiles):
-            first, last = P * m, P * (m + tiles)
-            listed = v_pool[t][:].indirect(offsets[:, first // PER_COLUMN : last // PER_COLUMN])
-            rows = v_term[:, SLOT_TILES * t + m : SLOT_TILES * t + m + tiles, :].rearrange("p m s -> p (m s)")
-            nc.vector.tensor_tensor(rows, listed, v_factor[:, t, first:last], MULT)
+        def slot_tile(m):
+            return slice(P * m, P * (m + 1))
+
+        def listed_v(t, cols):
+            return v_pool[t][:].indirect(offsets[:, cols.start // PER_COLUMN : cols.stop // PER_COLUMN])
+
+        def look_up_v(t, cols):
+            nc.vector.tensor_tensor(v_term[:, t, cols], listed_v(t, cols), v_factor[:, t, cols], MULT)
 
         def walk(planes):
             return planes.rearrange("p t (c i) -> p c t i", i=RUN)
 
-        e_pairs = placed.tile([P, 2, 2, P, 2], BF16, name="e_pairs", offset=4 * TOKENS * 2, align_bytes=64)
+        e_pairs = [
+            placed.tile([P, 2, HALF, 2], BF16, name="e_pairs%d" % h, offset=4 * TOKENS * (h + 1), align_bytes=64) for h in range(2)
+        ]
 
-        def subtract_pair(m, u):
-            out = e_pairs[:, m, u].rearrange("p (c i) t -> p c t i", i=RUN)
-            low = SLOT_TILES * 2 * u + m
-            v_rows = v_term[:, low : low + SLOT_TILES + 1 : SLOT_TILES]
-            nc.vector.tensor_tensor(out, walk(u_term[:, 2 * u : 2 * u + 2, m, :]), walk(v_rows), SUB)
+        def subtract_pair(u, cols):
+            h, first = divmod(cols.start, HALF)
+            out = e_pairs[h][:, u, first : first + cols.stop - cols.start].rearrange("p (c i) t -> p c t i", i=RUN)
+            planes = slice(2 * u, 2 * u + 2)
+            nc.vector.tensor_tensor(out, walk(u_flat[:, planes, cols]), walk(v_term[:, planes, cols]), SUB)
 
-        def weave_e(m, e_bf):
-            e_words = e_bf.rearrange("p c t -> p (c t)").bitcast(F32).rearrange("p (c i u) -> p c u i", i=RUN, u=2)
-            nc.vector.tensor_copy(e_words, walk(e_pairs[:, m].rearrange("p r c e -> p r (c e)").bitcast(F32)))
+        def weave_e(m):
+            e_words = e_bf[m].rearrange("p c t -> p (c t)").bitcast(F32).rearrange("p (c i u) -> p c u i", i=RUN, u=2)
+            pair_words = e_pairs[m // 2][:].rearrange("p u c e -> p u (c e)").bitcast(F32)
+            nc.vector.tensor_copy(e_words, walk(pair_words[:, :, slot_tile(m % 2)]))
 
-        def subtract(m, e_bf):
-            out = e_bf.rearrange("p (c i) t -> p c t i", i=RUN)
-            v_rows = v_term[:, m : LANES * SLOT_TILES : SLOT_TILES, :]
-            nc.vector.tensor_tensor(out, walk(u_term[:, :, m, :]), walk(v_rows), SUB)
+        def quantize_e(m):
+            quantize(nc, e_codes[:, slot_tile(m)], e_scales[:, slot_tile(m)], e_bf[m], E5M2)
 
-        def quantize_e(m, e_bf):
-            cols = slice(P * m, P * (m + 1))
-            quantize(nc, e_codes[:, cols], e_scales[:, cols], e_bf, E5M2)
-
-        for t in range(LANES - 1):
-            look_up_v(t, 0, SLOT_TILES)
+        whole = slice(0, SLOTS)
+        look_up_v(0, whole)
+        look_up_v(1, whole)
+        subtract_pair(0, half(0))
+        look_up_v(2, whole)
+        subtract_pair(0, half(1))
         for m in range(2):
-            subtract_pair(m, 0)
-        for m in range(2):
-            look_up_v(LANES - 1, m, 1)
-        e_bf = [v_term[:, LANES * SLOT_TILES - 2 :, :].rearrange("p m s -> p (m s)").bitcast(BF16).rearrange("p (c t) -> p c t", t=LANES)]
+            look_up_v(LANES - 1, slot_tile(m))
+        v_plain = sb.tile([P, SLOTS], F32, name="v_plain")
+        nc.scalar.activation(v_plain[:, half(1)], listed_v(LANES - 1, half(1)), COPY)
+
+        def scale_v(cols):
+            nc.vector.tensor_tensor(v_term[:, LANES - 1, cols], v_plain[:, cols], v_factor[:, LANES - 1, cols], MULT)
+
+        e_bf = [e_pairs[1][:, 1].rearrange("p c e -> p (c e)").rearrange("p (c t) -> p c t", t=LANES)]
         for m in range(1, SLOT_TILES):
             e_bf.append(sb.tile([P, P, LANES], BF16, name="e_bf%d" % m, tag="e_bf%d" % m, align_bytes=64)[:])
-        for m in range(2):
-            subtract_pair(m, 1)
-        for m in range(2):
-            weave_e(m, e_bf[m])
-        for m in range(2):
-            quantize_e(m, e_bf[m])
-        for m in range(2, SLOT_TILES):
-            look_up_v(LANES - 1, m, 1)
-        for m in range(2, SLOT_TILES):
-            subtract(m, e_bf[m])
-        for m in range(2, SLOT_TILES):
-            quantize_e(m, e_bf[m])
+        for h in range(2):
+            tiles = range(2 * h, 2 * h + 2)
+            if h:
+                scale_v(half(1))
+            for m in tiles:
+                subtract_pair(1, slot_tile(m))
+            for m in tiles:
+                weave_e(m)
+            for m in tiles:
+                quantize_e(m)
 
         def dk_passes(b, h, planes):
             dk_psum = bank(b, "dk_psum%d" % b, [P, len(planes), HALF])
@@ -240,12 +247,19 @@ def tile_attend_gttt_k_pl_kernel(tc, kT, vT, W, ts, tk, cf, offs, out_0, out_1, 
                 )
             return dk_psum
 
-        groups = [(0, (0,)), (0, (1,)), (0, (2, 3)), (1, (0,)), (1, (1,)), (1, (2, 3))]
-        dk_psum = [dk_passes(b, h, planes) for b, (h, planes) in enumerate(groups)]
+        groups = [(0, (0,)), (0, (1,)), (0, (2, 3)), (1, (0,)), (1, (1,)), (1, (2,)), (1, (3,))]
+        first_psum = [bank(7 * m, "first_psum%d" % m, [P, P]) for m in range(2)]
+        for m in range(2):
+            nc.tensor.matmul_mx(
+                first_psum[m][:], lhsT=wf_codes[:, :P].bitcast(E4M3), lhsT_scale=wf_scales[:, :P],
+                rhs=e_codes[:, slot_tile(m)].bitcast(E5M2), rhs_scale=e_scales[:, slot_tile(m)], start=True, stop=True,
+            )
+        dk_psum = [dk_passes(b, h, planes) if b else None for b, (h, planes) in enumerate(groups)]
         dk_first = sb.tile([P, 1, HALF], F32, name="dk_first", tag="from_psum0")
         dk_low = sb.tile([P, LANES - 1, HALF], F32, name="dk_low", tag="e_bf3", align_bytes=64)
-        dk_high = sb.tile([P, LANES, HALF], F32, name="dk_high")
-        dk_sb = [dk_first[:], dk_low[:, 0:1], dk_low[:, 1:3], dk_high[:, 0:1], dk_high[:, 1:2], dk_high[:, 2:4]]
+        dk_high = sb.tile([P, LANES - 1, HALF], F32, name="dk_high")
+        dk_last = placed.tile([P, 1, HALF], F32, name="dk_last", offset=0, align_bytes=64)
+        dk_sb = [dk_first[:], dk_low[:, 0:1], dk_low[:, 1:3], dk_high[:, 0:1], dk_high[:, 1:2], dk_last[:], dk_high[:, 2:3]]
         dk = {(j, h): dk_sb[b][:, n, :] for b, (h, planes) in enumerate(groups) for n, j in enumerate(planes)}
 
         def listed(j, h):
@@ -254,67 +268,67 @@ def tile_attend_gttt_k_pl_kernel(tc, kT, vT, W, ts, tk, cf, offs, out_0, out_1, 
         def store(j):
             nc.sync.dma_start(out_0.rearrange("(p j) c -> p j c", j=LANES)[:, j, :], window[j][:])
 
-        nc.scalar.copy(dk_sb[0], dk_psum[0][:])
+        for m in range(2):
+            nc.scalar.copy(dk_first[:, 0, slot_tile(m)], first_psum[m][:])
         nc.scalar.activation(listed(0, 0), dk[0, 0], COPY)
-        for b in range(1, 5):
+        for b in (1, 3, 2, 4):
             nc.vector.tensor_copy(dk_sb[b], dk_psum[b][:])
-        nc.vector.tensor_copy(listed(0, 1), dk[0, 1])
-        store(0)
-        nc.scalar.activation(listed(1, 0), dk[1, 0], COPY)
-        nc.vector.tensor_copy(dk_sb[5], dk_psum[5][:])
-        nc.vector.tensor_copy(listed(1, 1), dk[1, 1])
-        store(1)
-        for j in range(2, LANES):
-            for h in range(2):
-                nc.scalar.activation(listed(j, h), dk[j, h], COPY)
+        for j in range(LANES):
+            if j == LANES - 1:
+                nc.scalar.copy(dk_sb[6], dk_psum[6][:])
+            if j > 0:
+                nc.scalar.activation(listed(j, 0), dk[j, 0], COPY)
+            if j < LANES - 1:
+                nc.vector.tensor_copy(listed(j, 1), dk[j, 1])
+            else:
+                nc.scalar.activation(listed(j, 1), dk[j, 1], COPY)
+            if j == 0:
+                nc.vector.tensor_copy(dk_sb[5], dk_psum[5][:])
             store(j)
 
-        pairs = [sb.tile([P, 2, c.stop - c.start, 2], BF16, name="pairs%d" % c.start, align_bytes=64) for c in CHUNKS]
-        y_bf = [sb.tile([P, c.stop - c.start, LANES], BF16, name="y_bf%d" % c.start, align_bytes=64) for c in CHUNKS]
-        for j in range(LANES - 1):
+        pairs = [
+            placed.tile([P, 2, c.stop - c.start, 2], BF16, name="pairs%d" % c.start, offset=24 * c.start, align_bytes=64)
+            for c in CHUNKS
+        ]
+        for j in range(LANES):
             for c, cols in enumerate(CHUNKS):
-                nc.vector.tensor_copy(pairs[c][:, j // 2, :, j % 2], window[j][:, cols])
-                if j == 2 and c > 0:
-                    last = slice(cols.stop - 1, cols.stop)
-                    both = window[j][:, last].unsqueeze(2).to_broadcast([P, 1, 2])
-                    nc.vector.tensor_copy(pairs[c][:, 1, cols.stop - cols.start - 1 :, :], both)
-        for h in range(2):
-            nc.vector.tensor_copy(pairs[0][:, 1, half(h), 1], window[LANES - 1][:, half(h)])
-        for c, cols in enumerate(CHUNKS):
-            if c > 0:
-                nc.scalar.copy(pairs[c][:, 1, :, 1], window[LANES - 1][:, cols])
+                rounded, plane = pairs[c][:, j // 2, :, j % 2], window[j][:, cols]
+                if j < 2 and c == 1:
+                    nc.gpsimd.tensor_scalar(rounded, plane, 1.0, 0.0, MULT, ADD)
+                elif j < 2 or c == 0:
+                    nc.vector.tensor_copy(rounded, plane)
+        for c, cols in enumerate(CHUNKS[1:], 1):
+            for j in range(2, LANES):
+                nc.scalar.copy(pairs[c][:, j // 2, :, j % 2], window[j][:, cols])
 
         words_out = out_1[0].rearrange("p c l -> p (c l)").bitcast(I32)
         y_scales = sb.tile([P, GROUP], U8, name="y_scales", align_bytes=64)
         y_codes = sb.tile([P, TOKENS], U32, name="y_codes", align_bytes=64)
+        y_bf = [sb.tile([P, HALF, LANES], BF16, name="y_bf%d" % b, align_bytes=64) for b in range(TOKENS // HALF)]
 
-        def pieces(c):
-            return [slice(first, first + HALF) for first in range(0, CHUNKS[c].stop - CHUNKS[c].start, HALF)]
+        def weave(b):
+            c = max(n for n, cols in enumerate(CHUNKS) if cols.start <= HALF * b)
+            first = HALF * b - CHUNKS[c].start
+            y_words = y_bf[b][:].rearrange("p c t -> p (c t)").bitcast(F32).rearrange("p (c i u) -> p c u i", i=RUN, u=2)
+            pair_words = walk(pairs[c][:].rearrange("p u c e -> p u (c e)").bitcast(F32)[:, :, first : first + HALF])
+            if HALF * b < VECTOR_WEAVES:
+                nc.vector.tensor_copy(y_words, pair_words)
+            else:
+                nc.scalar.copy(y_words, pair_words)
 
-        def weave(c):
-            y_words = y_bf[c][:].rearrange("p c t -> p (c t)").bitcast(F32).rearrange("p (c i u) -> p c u i", i=RUN, u=2)
-            pair_words = pairs[c][:].rearrange("p u c e -> p u (c e)").bitcast(F32).rearrange("p u (c i) -> p c u i", i=RUN)
-            for piece in pieces(c):
-                runs = slice(piece.start // RUN, piece.stop // RUN)
-                if CHUNKS[c].start < VECTOR_WEAVES:
-                    nc.vector.tensor_copy(y_words[:, runs], pair_words[:, runs])
-                else:
-                    nc.scalar.copy(y_words[:, runs], pair_words[:, runs])
+        def hand_on(b):
+            g, first = divmod(HALF * b, GROUP)
+            done = HALF * (b + 1)
+            quantize(nc, y_codes[:, done - HALF : done], y_scales[4 * g : P, first : first + HALF], y_bf[b][:], E4M3)
+            for store in STORES:
+                if store.stop == done:
+                    nc.sync.dma_start(words_out[:, store], y_codes[:, store].bitcast(I32))
 
-        def hand_on(c):
-            cols = CHUNKS[c]
-            g, first = divmod(cols.start, GROUP)
-            for piece in pieces(c):
-                scales = y_scales[4 * g : P, first + piece.start : first + piece.stop]
-                done = cols.start + piece.stop
-                quantize(nc, y_codes[:, done - HALF : done], scales, y_bf[c][:, piece, :], E4M3)
-                for store in STORES:
-                    if store.stop == done:
-                        nc.sync.dma_start(words_out[:, store], y_codes[:, store].bitcast(I32))
-
-        for c in range(len(CHUNKS)):
-            weave(c)
-            hand_on(c)
+        for g in range(GROUPS):
+            for b in (2 * g, 2 * g + 1):
+                weave(b)
+            for b in (2 * g, 2 * g + 1):
+                hand_on(b)
         for q in range(4):
             rows = out_2[0].bitcast(I32)[4 * q : 4 * q + 4, :].rearrange("r (g x) -> g r x", g=GROUPS)
             queue = nc.scalar if q < 2 else nc.sync

@@ -31,9 +31,9 @@ ROW = P - 1
 GROUPS = 4
 GROUP = TOKENS // GROUPS
 
-CHUNKS = [slice(0, 1024), slice(1024, 2048)]
+CHUNKS = [slice(0, 512), slice(512, 1024), slice(1024, 1536), slice(1536, 2048)]
 STORES = [slice(0, 1024), slice(1024, 1536), slice(1536, 2048)]
-VECTOR_WEAVES = 1280
+VECTOR_WEAVES = 1536
 SCALAR_ROUNDS = 1536
 
 FLOPS = 2 * 2 * D * D * SLOTS
@@ -247,7 +247,7 @@ def tile_attend_gttt_k_pl_kernel(tc, kT, vT, W, ts, tk, cf, offs, out_0, out_1, 
                 )
             return dk_psum
 
-        groups = [(0, (0,)), (0, (1,)), (0, (2, 3)), (1, (0,)), (1, (1,)), (1, (2,)), (1, (3,))]
+        groups = [(0, (0,)), (0, (1,)), (0, (2, 3)), (1, (0,)), (1, (1,)), (1, (2, 3))]
         first_psum = [bank(7 * m, "first_psum%d" % m, [P, P]) for m in range(2)]
         for m in range(2):
             nc.tensor.matmul_mx(
@@ -257,9 +257,8 @@ def tile_attend_gttt_k_pl_kernel(tc, kT, vT, W, ts, tk, cf, offs, out_0, out_1, 
         dk_psum = [dk_passes(b, h, planes) if b else None for b, (h, planes) in enumerate(groups)]
         dk_first = sb.tile([P, 1, HALF], F32, name="dk_first", tag="from_psum0")
         dk_low = sb.tile([P, LANES - 1, HALF], F32, name="dk_low", tag="e_bf3", align_bytes=64)
-        dk_high = sb.tile([P, LANES - 1, HALF], F32, name="dk_high")
-        dk_last = placed.tile([P, 1, HALF], F32, name="dk_last", offset=0, align_bytes=64)
-        dk_sb = [dk_first[:], dk_low[:, 0:1], dk_low[:, 1:3], dk_high[:, 0:1], dk_high[:, 1:2], dk_last[:], dk_high[:, 2:3]]
+        dk_high = sb.tile([P, LANES, HALF], F32, name="dk_high")
+        dk_sb = [dk_first[:], dk_low[:, 0:1], dk_low[:, 1:3], dk_high[:, 0:1], dk_high[:, 1:2], dk_high[:, 2:4]]
         dk = {(j, h): dk_sb[b][:, n, :] for b, (h, planes) in enumerate(groups) for n, j in enumerate(planes)}
 
         def listed(j, h):
@@ -273,33 +272,32 @@ def tile_attend_gttt_k_pl_kernel(tc, kT, vT, W, ts, tk, cf, offs, out_0, out_1, 
         nc.scalar.activation(listed(0, 0), dk[0, 0], COPY)
         for b in (1, 3, 2, 4):
             nc.vector.tensor_copy(dk_sb[b], dk_psum[b][:])
-        for j in range(LANES):
+        nc.vector.tensor_copy(listed(0, 1), dk[0, 1])
+        store(0)
+        for j in range(1, LANES):
             if j == LANES - 1:
-                nc.scalar.copy(dk_sb[6], dk_psum[6][:])
-            if j > 0:
-                nc.scalar.activation(listed(j, 0), dk[j, 0], COPY)
-            if j < LANES - 1:
-                nc.vector.tensor_copy(listed(j, 1), dk[j, 1])
-            else:
-                nc.scalar.activation(listed(j, 1), dk[j, 1], COPY)
-            if j == 0:
-                nc.vector.tensor_copy(dk_sb[5], dk_psum[5][:])
+                nc.scalar.copy(dk_sb[5], dk_psum[5][:])
+            nc.scalar.activation(listed(j, 0), dk[j, 0], COPY)
+        nc.vector.tensor_copy(listed(1, 1), dk[1, 1])
+        store(1)
+        for j in range(2, LANES):
+            nc.scalar.activation(listed(j, 1), dk[j, 1], COPY)
             store(j)
 
-        pairs = [
-            placed.tile([P, 2, c.stop - c.start, 2], BF16, name="pairs%d" % c.start, offset=24 * c.start, align_bytes=64)
-            for c in CHUNKS
-        ]
-        for j in range(LANES):
+        pairs = [sb.tile([P, 2, c.stop - c.start, 2], BF16, name="pairs%d" % c.start, align_bytes=64) for c in CHUNKS]
+
+        def rounded(j, c):
+            return pairs[c][:, j // 2, :, j % 2], window[j][:, CHUNKS[c]]
+
+        for j in range(LANES - 1):
             for c, cols in enumerate(CHUNKS):
-                rounded, plane = pairs[c][:, j // 2, :, j % 2], window[j][:, cols]
-                if j < 2 and c == 1:
-                    nc.gpsimd.tensor_scalar(rounded, plane, 1.0, 0.0, MULT, ADD)
-                elif j < 2 or c == 0:
-                    nc.vector.tensor_copy(rounded, plane)
-        for c, cols in enumerate(CHUNKS[1:], 1):
-            for j in range(2, LANES):
-                nc.scalar.copy(pairs[c][:, j // 2, :, j % 2], window[j][:, cols])
+                nc.vector.tensor_copy(*rounded(j, c))
+                if j == 2 and c > 0:
+                    both = window[j][:, cols.stop - 1 : cols.stop].unsqueeze(2).to_broadcast([P, 1, 2])
+                    nc.vector.tensor_copy(pairs[c][:, 1, cols.stop - cols.start - 1 :, :], both)
+        nc.vector.tensor_copy(*rounded(LANES - 1, 0))
+        for c in range(1, len(CHUNKS)):
+            nc.scalar.copy(*rounded(LANES - 1, c))
 
         words_out = out_1[0].rearrange("p c l -> p (c l)").bitcast(I32)
         y_scales = sb.tile([P, GROUP], U8, name="y_scales", align_bytes=64)

@@ -14,7 +14,6 @@ E5M2 = mybir.dt.float8_e5m2_x4
 COPY = mybir.ActivationFunctionType.Copy
 MULT = mybir.AluOpType.mult
 SUB = mybir.AluOpType.subtract
-ADD = mybir.AluOpType.add
 
 P = 128
 LANES = 4
@@ -23,7 +22,6 @@ SLOTS = 512
 TOKENS = 2048
 SLOT_TILES = SLOTS // P
 HALF = SLOTS // 2
-PAD = SLOTS - P
 RUN = 4
 PER_COLUMN = 16
 ROW = P - 1
@@ -31,10 +29,12 @@ ROW = P - 1
 GROUPS = 4
 GROUP = TOKENS // GROUPS
 
-CHUNKS = [slice(0, 512), slice(512, 1024), slice(1024, 1536), slice(1536, 2048)]
-STORES = [slice(0, 1024), slice(1024, 1536), slice(1536, 2048)]
+PIECE = 256
+PLANE_BYTES = 4 * TOKENS
+
+CHUNKS = [slice(first, first + GROUP) for first in range(0, TOKENS, GROUP)]
+STORES = [slice(0, 768), slice(768, 1280), slice(1280, 1792), slice(1792, 2048)]
 VECTOR_WEAVES = 1536
-SCALAR_ROUNDS = 1536
 
 FLOPS = 2 * 2 * D * D * SLOTS
 BYTES = 4 * (3 * D * TOKENS + D * D + 2 * TOKENS + D) + 2 * P * SLOTS // PER_COLUMN + D * TOKENS + D // 32 * TOKENS
@@ -42,6 +42,14 @@ BYTES = 4 * (3 * D * TOKENS + D * D + 2 * TOKENS + D) + 2 * P * SLOTS // PER_COL
 
 def half(h, per=1):
     return slice(HALF // per * h, HALF // per * (h + 1))
+
+
+def slot_tile(m):
+    return slice(P * m, P * (m + 1))
+
+
+def walk(planes):
+    return planes.rearrange("p t (c i) -> p c t i", i=RUN)
 
 
 def quantize(nc, codes, scales, grouped, fmt):
@@ -74,7 +82,7 @@ def tile_attend_gttt_k_pl_kernel(tc, kT, vT, W, ts, tk, cf, offs, out_0, out_1, 
         nc.sync.dma_start(w_raw[:], W.rearrange("(p j) f -> p j f", j=LANES))
         nc.sync.dma_start(offsets[:], offs)
         k_pool = [sb.tile([P, TOKENS], F32, name="k_pool%d" % j, tag="k_pool%d" % j, align_bytes=64) for j in range(LANES)]
-        v_pool = [placed.tile([P, TOKENS], F32, name="v_pool%d" % t, offset=4 * TOKENS * t, align_bytes=64) for t in range(LANES)]
+        v_pool = [placed.tile([P, TOKENS], F32, name="v_pool%d" % t, offset=PLANE_BYTES * t, align_bytes=64) for t in range(LANES)]
         for j in range(LANES):
             nc.sync.dma_start(k_pool[j][:], kT.rearrange("(p j) c -> p j c", j=LANES)[:, j, :])
         for t in range(LANES):
@@ -148,7 +156,6 @@ def tile_attend_gttt_k_pl_kernel(tc, kT, vT, W, ts, tk, cf, offs, out_0, out_1, 
         for h in range(2):
             quantize(nc, k_codes[:, half(h)], k_scales[:, half(h)], k_bf[:, half(h), :], E4M3)
 
-        inner, outer = slice(0, 2), slice(2, SLOT_TILES)
         u_scaled = {}
         for m in range(SLOT_TILES):
             cols = slice(P * m, P * (m + 1))
@@ -160,7 +167,9 @@ def tile_attend_gttt_k_pl_kernel(tc, kT, vT, W, ts, tk, cf, offs, out_0, out_1, 
             u_scaled[m] = sb.tile([P, LANES, P], F32, name="u_scaled%d" % m, tag="from_psum%d" % m)
             nc.scalar.activation(u_scaled[m][:].rearrange("p t s -> p (t s)"), u_psum[:], COPY, scale=tstk2_col[:, m : m + 1])
         u_term = sb.tile([P, LANES, SLOT_TILES, P], F32, name="u_term")
-        for b, (u, tiles) in enumerate([(0, inner), (0, outer), (1, inner), (1, outer)]):
+        for b in range(4):
+            h, u = divmod(b, 2)
+            tiles = half(h, P)
             u_turned = bank(SLOT_TILES + b, "u_turned%d" % b, [P, 2, 2, P])
             for i in range(2):
                 for n, m in enumerate(range(SLOT_TILES)[tiles]):
@@ -179,87 +188,69 @@ def tile_attend_gttt_k_pl_kernel(tc, kT, vT, W, ts, tk, cf, offs, out_0, out_1, 
         v_term = sb.tile([P, LANES, SLOTS], F32, name="v_term", align_bytes=64)
         u_flat = u_term[:].rearrange("p t m s -> p t (m s)")
 
-        def slot_tile(m):
-            return slice(P * m, P * (m + 1))
-
-        def listed_v(t, cols):
-            return v_pool[t][:].indirect(offsets[:, cols.start // PER_COLUMN : cols.stop // PER_COLUMN])
-
         def look_up_v(t, cols):
-            nc.vector.tensor_tensor(v_term[:, t, cols], listed_v(t, cols), v_factor[:, t, cols], MULT)
+            values = v_pool[t][:].indirect(offsets[:, cols.start // PER_COLUMN : cols.stop // PER_COLUMN])
+            nc.vector.tensor_tensor(v_term[:, t, cols], values, v_factor[:, t, cols], MULT)
 
-        def walk(planes):
-            return planes.rearrange("p t (c i) -> p c t i", i=RUN)
-
-        e_pairs = [
-            placed.tile([P, 2, HALF, 2], BF16, name="e_pairs%d" % h, offset=4 * TOKENS * (h + 1), align_bytes=64) for h in range(2)
-        ]
+        e_pairs = placed.tile([P, 2, HALF, 2], BF16, name="e_pairs", offset=PLANE_BYTES * 2, align_bytes=64)
 
         def subtract_pair(u, cols):
-            h, first = divmod(cols.start, HALF)
-            out = e_pairs[h][:, u, first : first + cols.stop - cols.start].rearrange("p (c i) t -> p c t i", i=RUN)
+            out = e_pairs[:, u, cols].rearrange("p (c i) t -> p c t i", i=RUN)
             planes = slice(2 * u, 2 * u + 2)
             nc.vector.tensor_tensor(out, walk(u_flat[:, planes, cols]), walk(v_term[:, planes, cols]), SUB)
 
         def weave_e(m):
             e_words = e_bf[m].rearrange("p c t -> p (c t)").bitcast(F32).rearrange("p (c i u) -> p c u i", i=RUN, u=2)
-            pair_words = e_pairs[m // 2][:].rearrange("p u c e -> p u (c e)").bitcast(F32)
-            nc.vector.tensor_copy(e_words, walk(pair_words[:, :, slot_tile(m % 2)]))
+            pair_words = e_pairs[:].rearrange("p u c e -> p u (c e)").bitcast(F32)
+            nc.vector.tensor_copy(e_words, walk(pair_words[:, :, slot_tile(m)]))
+
+        def subtract(m):
+            out = e_bf[m].rearrange("p (c i) t -> p c t i", i=RUN)
+            nc.vector.tensor_tensor(out, walk(u_flat[:, :, slot_tile(m)]), walk(v_term[:, :, slot_tile(m)]), SUB)
 
         def quantize_e(m):
             quantize(nc, e_codes[:, slot_tile(m)], e_scales[:, slot_tile(m)], e_bf[m], E5M2)
 
-        whole = slice(0, SLOTS)
-        look_up_v(0, whole)
-        look_up_v(1, whole)
+        for t in range(LANES - 1):
+            look_up_v(t, slice(0, SLOTS))
         subtract_pair(0, half(0))
-        look_up_v(2, whole)
-        subtract_pair(0, half(1))
         for m in range(2):
             look_up_v(LANES - 1, slot_tile(m))
-        v_plain = sb.tile([P, SLOTS], F32, name="v_plain")
-        nc.scalar.activation(v_plain[:, half(1)], listed_v(LANES - 1, half(1)), COPY)
-
-        def scale_v(cols):
-            nc.vector.tensor_tensor(v_term[:, LANES - 1, cols], v_plain[:, cols], v_factor[:, LANES - 1, cols], MULT)
-
-        e_bf = [e_pairs[1][:, 1].rearrange("p c e -> p (c e)").rearrange("p (c t) -> p c t", t=LANES)]
+        e_bf = [v_term[:, LANES - 1, half(1)].bitcast(BF16).rearrange("p (c t) -> p c t", t=LANES)]
         for m in range(1, SLOT_TILES):
             e_bf.append(sb.tile([P, P, LANES], BF16, name="e_bf%d" % m, tag="e_bf%d" % m, align_bytes=64)[:])
-        for h in range(2):
-            tiles = range(2 * h, 2 * h + 2)
-            if h:
-                scale_v(half(1))
-            for m in tiles:
-                subtract_pair(1, slot_tile(m))
-            for m in tiles:
-                weave_e(m)
-            for m in tiles:
-                quantize_e(m)
-
-        def dk_passes(b, h, planes):
-            dk_psum = bank(b, "dk_psum%d" % b, [P, len(planes), HALF])
-            for n, j in enumerate(planes):
-                cols = slice(P * j, P * (j + 1))
-                nc.tensor.matmul_mx(
-                    dk_psum[:, n, :], lhsT=wf_codes[:, cols].bitcast(E4M3), lhsT_scale=wf_scales[:, cols],
-                    rhs=e_codes[:, half(h)].bitcast(E5M2), rhs_scale=e_scales[:, half(h)], start=True, stop=True,
-                )
-            return dk_psum
-
-        groups = [(0, (0,)), (0, (1,)), (0, (2, 3)), (1, (0,)), (1, (1,)), (1, (2, 3))]
-        first_psum = [bank(7 * m, "first_psum%d" % m, [P, P]) for m in range(2)]
         for m in range(2):
-            nc.tensor.matmul_mx(
-                first_psum[m][:], lhsT=wf_codes[:, :P].bitcast(E4M3), lhsT_scale=wf_scales[:, :P],
-                rhs=e_codes[:, slot_tile(m)].bitcast(E5M2), rhs_scale=e_scales[:, slot_tile(m)], start=True, stop=True,
-            )
-        dk_psum = [dk_passes(b, h, planes) if b else None for b, (h, planes) in enumerate(groups)]
-        dk_first = sb.tile([P, 1, HALF], F32, name="dk_first", tag="from_psum0")
-        dk_low = sb.tile([P, LANES - 1, HALF], F32, name="dk_low", tag="e_bf3", align_bytes=64)
-        dk_high = sb.tile([P, LANES, HALF], F32, name="dk_high")
-        dk_sb = [dk_first[:], dk_low[:, 0:1], dk_low[:, 1:3], dk_high[:, 0:1], dk_high[:, 1:2], dk_high[:, 2:4]]
-        dk = {(j, h): dk_sb[b][:, n, :] for b, (h, planes) in enumerate(groups) for n, j in enumerate(planes)}
+            subtract_pair(1, slot_tile(m))
+        for m in range(2):
+            weave_e(m)
+        for m in range(2):
+            quantize_e(m)
+        for m in range(2, SLOT_TILES):
+            look_up_v(LANES - 1, slot_tile(m))
+        for m in range(2, SLOT_TILES):
+            subtract(m)
+        for m in range(2, SLOT_TILES):
+            quantize_e(m)
+
+        def dk_passes(b, planes, cols):
+            products = bank(b, "dk_psum%d" % b, [P, len(planes), cols.stop - cols.start])
+            for n, j in enumerate(planes):
+                nc.tensor.matmul_mx(
+                    products[:, n, :], lhsT=wf_codes[:, P * j : P * (j + 1)].bitcast(E4M3), lhsT_scale=wf_scales[:, P * j : P * (j + 1)],
+                    rhs=e_codes[:, cols].bitcast(E5M2), rhs_scale=e_scales[:, cols], start=True, stop=True,
+                )
+            return products
+
+        first_psum = [dk_passes(b, [0], slot_tile(m)) for m, b in enumerate((0, 7))]
+        first1_psum = dk_passes(1, [1], half(0))
+        first23_psum = dk_passes(2, [2, 3], half(0))
+        second0_psum = dk_passes(3, [0], half(1))
+        second1_psum = dk_passes(4, [1], half(1))
+        second23_psum = dk_passes(5, [2, 3], half(1))
+        first01 = sb.tile([P, 2, HALF], F32, name="first01", tag="from_psum0")
+        first23 = sb.tile([P, 2, HALF], F32, name="first23", tag="e_bf3", align_bytes=64)
+        second = sb.tile([P, LANES, HALF], F32, name="second")
+        dk = [[first01[:, 0], first01[:, 1], first23[:, 0], first23[:, 1]], [second[:, j] for j in range(LANES)]]
 
         def listed(j, h):
             return window[j][:].indirect(offsets[:, half(h, PER_COLUMN)])
@@ -268,59 +259,60 @@ def tile_attend_gttt_k_pl_kernel(tc, kT, vT, W, ts, tk, cf, offs, out_0, out_1, 
             nc.sync.dma_start(out_0.rearrange("(p j) c -> p j c", j=LANES)[:, j, :], window[j][:])
 
         for m in range(2):
-            nc.scalar.copy(dk_first[:, 0, slot_tile(m)], first_psum[m][:])
-        nc.scalar.activation(listed(0, 0), dk[0, 0], COPY)
-        for b in (1, 3, 2, 4):
-            nc.vector.tensor_copy(dk_sb[b], dk_psum[b][:])
-        nc.vector.tensor_copy(listed(0, 1), dk[0, 1])
+            nc.scalar.copy(first01[:, 0:1, slot_tile(m)], first_psum[m][:])
+        nc.scalar.activation(listed(0, 0), dk[0][0], COPY)
+        nc.vector.tensor_copy(first23[:], first23_psum[:])
+        nc.vector.tensor_copy(second[:, 0:1], second0_psum[:])
+        nc.vector.tensor_copy(second[:, 1:2], second1_psum[:])
+        nc.vector.tensor_copy(listed(0, 1), dk[1][0])
         store(0)
+        nc.scalar.copy(first01[:, 1:2], first1_psum[:])
         for j in range(1, LANES):
             if j == LANES - 1:
-                nc.scalar.copy(dk_sb[5], dk_psum[5][:])
-            nc.scalar.activation(listed(j, 0), dk[j, 0], COPY)
-        nc.vector.tensor_copy(listed(1, 1), dk[1, 1])
+                nc.scalar.copy(second[:, 2:], second23_psum[:])
+            nc.scalar.activation(listed(j, 0), dk[0][j], COPY)
+        nc.vector.tensor_copy(listed(1, 1), dk[1][1])
         store(1)
         for j in range(2, LANES):
-            nc.scalar.activation(listed(j, 1), dk[j, 1], COPY)
+            nc.scalar.activation(listed(j, 1), dk[1][j], COPY)
             store(j)
 
-        pairs = [sb.tile([P, 2, c.stop - c.start, 2], BF16, name="pairs%d" % c.start, align_bytes=64) for c in CHUNKS]
-
-        def rounded(j, c):
-            return pairs[c][:, j // 2, :, j % 2], window[j][:, CHUNKS[c]]
-
+        pairs = [sb.tile([P, 2, GROUP, 2], BF16, name="pairs%d" % c.start, align_bytes=64) for c in CHUNKS]
         for j in range(LANES - 1):
             for c, cols in enumerate(CHUNKS):
-                nc.vector.tensor_copy(*rounded(j, c))
-                if j == 2 and c > 0:
-                    both = window[j][:, cols.stop - 1 : cols.stop].unsqueeze(2).to_broadcast([P, 1, 2])
-                    nc.vector.tensor_copy(pairs[c][:, 1, cols.stop - cols.start - 1 :, :], both)
-        nc.vector.tensor_copy(*rounded(LANES - 1, 0))
-        for c in range(1, len(CHUNKS)):
-            nc.scalar.copy(*rounded(LANES - 1, c))
+                if j < 2 or c == 0:
+                    nc.vector.tensor_copy(pairs[c][:, j // 2, :, j % 2], window[j][:, cols])
+                else:
+                    nc.vector.tensor_copy(pairs[c][:, 1, : GROUP - 2, 0], window[j][:, cols][:, : GROUP - 2])
+                    both = window[j][:, cols][:, GROUP - 4 :].unsqueeze(2).to_broadcast([P, 4, 2])
+                    nc.vector.tensor_copy(pairs[c][:, 1, GROUP - 4 :, :], both)
+        for c, cols in enumerate(CHUNKS):
+            if c == 0:
+                nc.vector.tensor_copy(pairs[c][:, 1, :, 1], window[LANES - 1][:, cols])
+            else:
+                nc.scalar.copy(pairs[c][:, 1, :, 1], window[LANES - 1][:, cols])
 
         words_out = out_1[0].rearrange("p c l -> p (c l)").bitcast(I32)
         y_scales = sb.tile([P, GROUP], U8, name="y_scales", align_bytes=64)
         y_codes = sb.tile([P, TOKENS], U32, name="y_codes", align_bytes=64)
-        y_bf = [sb.tile([P, HALF, LANES], BF16, name="y_bf%d" % b, align_bytes=64) for b in range(TOKENS // HALF)]
+        y_bf = [sb.tile([P, PIECE, LANES], BF16, name="y_bf%d" % b, align_bytes=64) for b in range(TOKENS // PIECE)]
 
         def weave(b):
-            c = max(n for n, cols in enumerate(CHUNKS) if cols.start <= HALF * b)
-            first = HALF * b - CHUNKS[c].start
+            c, first = divmod(PIECE * b, GROUP)
             y_words = y_bf[b][:].rearrange("p c t -> p (c t)").bitcast(F32).rearrange("p (c i u) -> p c u i", i=RUN, u=2)
-            pair_words = walk(pairs[c][:].rearrange("p u c e -> p u (c e)").bitcast(F32)[:, :, first : first + HALF])
-            if HALF * b < VECTOR_WEAVES:
+            pair_words = walk(pairs[c][:].rearrange("p u c e -> p u (c e)").bitcast(F32)[:, :, first : first + PIECE])
+            if PIECE * b < VECTOR_WEAVES:
                 nc.vector.tensor_copy(y_words, pair_words)
             else:
                 nc.scalar.copy(y_words, pair_words)
 
         def hand_on(b):
-            g, first = divmod(HALF * b, GROUP)
-            done = HALF * (b + 1)
-            quantize(nc, y_codes[:, done - HALF : done], y_scales[4 * g : P, first : first + HALF], y_bf[b][:], E4M3)
-            for store in STORES:
-                if store.stop == done:
-                    nc.sync.dma_start(words_out[:, store], y_codes[:, store].bitcast(I32))
+            g, first = divmod(PIECE * b, GROUP)
+            done = PIECE * (b + 1)
+            quantize(nc, y_codes[:, done - PIECE : done], y_scales[4 * g : P, first : first + PIECE], y_bf[b][:], E4M3)
+            for cols in STORES:
+                if cols.stop == done:
+                    nc.sync.dma_start(words_out[:, cols], y_codes[:, cols].bitcast(I32))
 
         for g in range(GROUPS):
             for b in (2 * g, 2 * g + 1):

@@ -24,13 +24,15 @@ SLOT_TILES = SLOTS // P
 HALF = SLOTS // 2
 RUN = 4
 PER_COLUMN = 16
-ROW = P - 1
+TK_ROW = P - 1
+TS_ROW = P // 2 - 1
 
 GROUPS = 4
 GROUP = TOKENS // GROUPS
 
 PIECE = 256
 PLANE_BYTES = 4 * TOKENS
+KEYS_AT = 5 * PLANE_BYTES - 2048
 
 CHUNKS = [slice(first, first + GROUP) for first in range(0, TOKENS, GROUP)]
 STORES = [slice(0, 768), slice(768, 1280), slice(1280, 1792), slice(1792, 2048)]
@@ -75,8 +77,8 @@ def tile_attend_gttt_k_pl_kernel(tc, kT, vT, W, ts, tk, cf, offs, out_0, out_1, 
         tk_pool = sb.tile([P, TOKENS], F32, name="tk_pool", tag="then_window0", align_bytes=64)
         ts_pool = sb.tile([P, TOKENS], F32, name="ts_pool")
         cf_sb = sb.tile([P, LANES], F32, name="cf_sb")
-        nc.scalar.dma_start(tk_pool[ROW:P, :], tk[0:1, :])
-        nc.scalar.dma_start(ts_pool[ROW:P, :], ts[0:1, :])
+        nc.scalar.dma_start(tk_pool[TK_ROW : TK_ROW + 1, :], tk[0:1, :])
+        nc.scalar.dma_start(ts_pool[TS_ROW : TS_ROW + 1, :], ts[0:1, :])
         nc.scalar.dma_start(cf_sb[:], cf.rearrange("(p t) o -> p (t o)", t=LANES))
         w_raw = sb.tile([P, LANES, D], F32, name="w_raw")
         nc.sync.dma_start(w_raw[:], W.rearrange("(p j) f -> p j f", j=LANES))
@@ -91,10 +93,13 @@ def tile_attend_gttt_k_pl_kernel(tc, kT, vT, W, ts, tk, cf, offs, out_0, out_1, 
         ident = sb.tile([P, P], F32, name="ident")
         make_identity(nc, ident[:])
 
-        nc.vector.memset(tk_pool[0:ROW, :], 0.0)
-        nc.vector.memset(ts_pool[0:ROW, :], 0.0)
+        nc.vector.memset(tk_pool[0:TK_ROW, :], 0.0)
+        nc.vector.memset(ts_pool[0:TS_ROW, :], 0.0)
+        nc.gpsimd.memset(ts_pool[TS_ROW + 1 : P, :], 0.0)
+        window1 = sb.tile([P, TOKENS], F32, name="window1", align_bytes=64)
+        nc.gpsimd.memset(window1[:], 0.0)
 
-        w_d = sb.tile([P, D, LANES], BF16, name="w_d", tag="then_window1", align_bytes=64)
+        w_d = placed.tile([P, D, LANES], BF16, name="w_d", offset=KEYS_AT, align_bytes=64)
         nc.scalar.activation(
             w_d[:].rearrange("p (t s) j -> p s t j", t=LANES), w_raw[:].rearrange("p j (s t) -> p s t j", t=LANES), COPY
         )
@@ -117,8 +122,8 @@ def tile_attend_gttt_k_pl_kernel(tc, kT, vT, W, ts, tk, cf, offs, out_0, out_1, 
         tstk_col = sb.tile([P, SLOT_TILES], F32, name="tstk_col")
         tstk2_col = sb.tile([P, SLOT_TILES], F32, name="tstk2_col")
         cf2 = sb.tile([P, LANES], F32, name="cf2")
-        nc.scalar.copy(tk_col[:], tk_turned[:, :, ROW])
-        nc.scalar.copy(ts_col[:], ts_turned[:, :, ROW])
+        nc.scalar.copy(tk_col[:], tk_turned[:, :, TK_ROW])
+        nc.scalar.copy(ts_col[:], ts_turned[:, :, TS_ROW])
         nc.gpsimd.tensor_tensor(cf2[:], cf_sb[:], cf_sb[:], MULT)
         nc.gpsimd.tensor_tensor(tstk_col[:], ts_col[:], tk_col[:], MULT)
         nc.gpsimd.tensor_tensor(tstk2_col[:], tstk_col[:], tk_col[:], MULT)
@@ -132,11 +137,11 @@ def tile_attend_gttt_k_pl_kernel(tc, kT, vT, W, ts, tk, cf, offs, out_0, out_1, 
             unpacked = w_turned[:].rearrange("p t s -> p (t s)").bitcast(BF16).rearrange("p (t s i) -> p i s t", t=LANES, i=2)
             nc.scalar.copy(w_f[:, 2 * u : 2 * u + 2, :, :], unpacked)
 
-        k_bf = sb.tile([P, SLOTS, LANES], BF16, name="k_bf", tag="then_window1", align_bytes=64)
+        k_bf = placed.tile([P, SLOTS, LANES], BF16, name="k_bf", offset=KEYS_AT, align_bytes=64)
         k_low = sb.tile([P, 2, SLOTS], BF16, name="k_low", tag="k_low")
         nc.vector.tensor_copy(k_low[:, 0, :], k_pool[0][:].indirect(offsets[:]))
 
-        wd_codes, wd_scales = operand("wd", "then_window3")
+        wd_codes, wd_scales = operand("wd", "wd_codes")
         quantize(nc, wd_codes[:], wd_scales[:], w_d[:], E4M3)
 
         tstk_row = bank(6, "tstk_row", [P, SLOTS])
@@ -152,7 +157,7 @@ def tile_attend_gttt_k_pl_kernel(tc, kT, vT, W, ts, tk, cf, offs, out_0, out_1, 
         quantize(nc, wf_codes[:], wf_scales[:], w_f[:].rearrange("p j s t -> p (j s) t"), E4M3)
         for h in range(2):
             nc.vector.tensor_copy(k_bf[:, half(h), LANES - 1], k_pool[LANES - 1][:].indirect(offsets[:, half(h, PER_COLUMN)]))
-        k_codes, k_scales = operand("k", "then_window2")
+        k_codes, k_scales = operand("k", "k_codes")
         for h in range(2):
             quantize(nc, k_codes[:, half(h)], k_scales[:, half(h)], k_bf[:, half(h), :], E4M3)
 
@@ -178,8 +183,9 @@ def tile_attend_gttt_k_pl_kernel(tc, kT, vT, W, ts, tk, cf, offs, out_0, out_1, 
                 t = 2 * u + i
                 nc.scalar.activation(u_term[:, t, tiles, :], u_turned[:, i], COPY, scale=cf2[:, t : t + 1])
 
-        for j in range(1, LANES):
-            window.append(sb.tile([P, TOKENS], F32, name="window%d" % j, tag="then_window%d" % j, align_bytes=64))
+        window.append(window1)
+        for j in range(2, LANES):
+            window.append(placed.tile([P, TOKENS], F32, name="window%d" % j, offset=PLANE_BYTES * (2 + j), align_bytes=64))
             nc.gpsimd.memset(window[j][:], 0.0)
 
         e_codes = sb.tile([P, SLOTS], U32, name="e_codes", align_bytes=64)

@@ -222,6 +222,8 @@ def tile_attend_gttt_k_pl_kernel(tc, kT, vT, W, ts, tk, cf, offs, out_0, out_1, 
         subtract_pair(0, half(0))
         for m in range(2):
             look_up_v(LANES - 1, slot_tile(m))
+        v_late = v_factor[:, LANES - 1, half(0)]
+        nc.scalar.activation(v_late, v_pool[LANES - 1][:].indirect(offsets[:, half(1, PER_COLUMN)]), COPY)
         e_bf = [v_term[:, LANES - 1, half(1)].bitcast(BF16).rearrange("p (c t) -> p c t", t=LANES)]
         for m in range(1, SLOT_TILES):
             e_bf.append(sb.tile([P, P, LANES], BF16, name="e_bf%d" % m, tag="e_bf%d" % m, align_bytes=64)[:])
@@ -232,7 +234,8 @@ def tile_attend_gttt_k_pl_kernel(tc, kT, vT, W, ts, tk, cf, offs, out_0, out_1, 
         for m in range(2):
             quantize_e(m)
         for m in range(2, SLOT_TILES):
-            look_up_v(LANES - 1, slot_tile(m))
+            late = v_late[:, slot_tile(m - 2)]
+            nc.vector.tensor_tensor(v_term[:, LANES - 1, slot_tile(m)], late, v_factor[:, LANES - 1, slot_tile(m)], MULT)
         for m in range(2, SLOT_TILES):
             subtract(m)
         for m in range(2, SLOT_TILES):
@@ -252,7 +255,8 @@ def tile_attend_gttt_k_pl_kernel(tc, kT, vT, W, ts, tk, cf, offs, out_0, out_1, 
         first23_psum = dk_passes(2, [2, 3], half(0))
         second0_psum = dk_passes(3, [0], half(1))
         second1_psum = dk_passes(4, [1], half(1))
-        second23_psum = dk_passes(5, [2, 3], half(1))
+        second2_psum = dk_passes(5, [2], half(1))
+        second3_psum = dk_passes(6, [3], half(1))
         first01 = sb.tile([P, 2, HALF], F32, name="first01", tag="from_psum0")
         first23 = sb.tile([P, 2, HALF], F32, name="first23", tag="e_bf3", align_bytes=64)
         second = sb.tile([P, LANES, HALF], F32, name="second")
@@ -275,10 +279,11 @@ def tile_attend_gttt_k_pl_kernel(tc, kT, vT, W, ts, tk, cf, offs, out_0, out_1, 
         nc.scalar.copy(first01[:, 1:2], first1_psum[:])
         for j in range(1, LANES):
             if j == LANES - 1:
-                nc.scalar.copy(second[:, 2:], second23_psum[:])
+                nc.scalar.copy(second[:, 2:3], second2_psum[:])
             nc.scalar.activation(listed(j, 0), dk[0][j], COPY)
         nc.vector.tensor_copy(listed(1, 1), dk[1][1])
         store(1)
+        nc.vector.tensor_copy(second[:, 3:4], second3_psum[:])
         for j in range(2, LANES):
             nc.scalar.activation(listed(j, 1), dk[1][j], COPY)
             store(j)

@@ -14,6 +14,7 @@ E5M2 = mybir.dt.float8_e5m2_x4
 COPY = mybir.ActivationFunctionType.Copy
 MULT = mybir.AluOpType.mult
 SUB = mybir.AluOpType.subtract
+ADD = mybir.AluOpType.add
 
 P = 128
 LANES = 4
@@ -34,9 +35,10 @@ PIECE = 256
 PLANE_BYTES = 4 * TOKENS
 KEYS_AT = 5 * PLANE_BYTES - 2048
 
-CHUNKS = [slice(first, first + GROUP) for first in range(0, TOKENS, GROUP)]
-STORES = [slice(0, 768), slice(768, 1280), slice(1280, 1792), slice(1792, 2048)]
-VECTOR_WEAVES = 1536
+STORES = [slice(first, first + GROUP) for first in range(0, TOKENS, GROUP)]
+GPSIMD_ROUNDS = 1024
+SPLIT = 1152
+VECTOR_WEAVES = 1024
 
 FLOPS = 2 * 2 * D * D * SLOTS
 BYTES = 4 * (3 * D * TOKENS + D * D + 2 * TOKENS + D) + 2 * P * SLOTS // PER_COLUMN + D * TOKENS + D // 32 * TOKENS
@@ -253,14 +255,15 @@ def tile_attend_gttt_k_pl_kernel(tc, kT, vT, W, ts, tk, cf, offs, out_0, out_1, 
         first_psum = [dk_passes(b, [0], slot_tile(m)) for m, b in enumerate((0, 7))]
         first1_psum = dk_passes(1, [1], half(0))
         first23_psum = dk_passes(2, [2, 3], half(0))
-        second0_psum = dk_passes(3, [0], half(1))
-        second1_psum = dk_passes(4, [1], half(1))
-        second2_psum = dk_passes(5, [2], half(1))
-        second3_psum = dk_passes(6, [3], half(1))
+        second_psum = [dk_passes(3 + j, [j], half(1)) for j in range(LANES)]
         first01 = sb.tile([P, 2, HALF], F32, name="first01", tag="from_psum0")
         first23 = sb.tile([P, 2, HALF], F32, name="first23", tag="e_bf3", align_bytes=64)
-        second = sb.tile([P, LANES, HALF], F32, name="second")
-        dk = [[first01[:, 0], first01[:, 1], first23[:, 0], first23[:, 1]], [second[:, j] for j in range(LANES)]]
+        pairs = sb.tile([P, 2, TOKENS, 2], BF16, name="pairs", align_bytes=64)
+        pair_words = pairs[:].rearrange("p u c e -> p u (c e)").bitcast(F32)
+        second0 = sb.tile([P, HALF], F32, name="second0")
+        for_scalar = pair_words[:, 1, SPLIT : SPLIT + HALF]
+        second = [second0[:], for_scalar, pair_words[:, 0, GPSIMD_ROUNDS : GPSIMD_ROUNDS + HALF], for_scalar]
+        dk = [[first01[:, 0], first01[:, 1], first23[:, 0], first23[:, 1]], second]
 
         def listed(j, h):
             return window[j][:].indirect(offsets[:, half(h, PER_COLUMN)])
@@ -268,40 +271,45 @@ def tile_attend_gttt_k_pl_kernel(tc, kT, vT, W, ts, tk, cf, offs, out_0, out_1, 
         def store(j):
             nc.sync.dma_start(out_0.rearrange("(p j) c -> p j c", j=LANES)[:, j, :], window[j][:])
 
+        def copy_second(j):
+            nc.vector.tensor_copy(second[j], second_psum[j][:, 0])
+
         for m in range(2):
             nc.scalar.copy(first01[:, 0:1, slot_tile(m)], first_psum[m][:])
         nc.scalar.activation(listed(0, 0), dk[0][0], COPY)
         nc.vector.tensor_copy(first23[:], first23_psum[:])
-        nc.vector.tensor_copy(second[:, 0:1], second0_psum[:])
-        nc.vector.tensor_copy(second[:, 1:2], second1_psum[:])
+        copy_second(0)
+        copy_second(1)
         nc.vector.tensor_copy(listed(0, 1), dk[1][0])
         store(0)
         nc.scalar.copy(first01[:, 1:2], first1_psum[:])
         for j in range(1, LANES):
-            if j == LANES - 1:
-                nc.scalar.copy(second[:, 2:3], second2_psum[:])
             nc.scalar.activation(listed(j, 0), dk[0][j], COPY)
         nc.vector.tensor_copy(listed(1, 1), dk[1][1])
         store(1)
-        nc.vector.tensor_copy(second[:, 3:4], second3_psum[:])
-        for j in range(2, LANES):
-            nc.scalar.activation(listed(j, 1), dk[1][j], COPY)
-            store(j)
+        copy_second(2)
+        nc.scalar.copy(second[3], second_psum[3][:, 0])
+        nc.vector.tensor_copy(listed(2, 1), dk[1][2])
+        store(2)
+        nc.scalar.activation(listed(3, 1), dk[1][3], COPY)
+        store(3)
 
-        pairs = [sb.tile([P, 2, GROUP, 2], BF16, name="pairs%d" % c.start, align_bytes=64) for c in CHUNKS]
-        for j in range(LANES - 1):
-            for c, cols in enumerate(CHUNKS):
-                if j < 2 or c == 0:
-                    nc.vector.tensor_copy(pairs[c][:, j // 2, :, j % 2], window[j][:, cols])
-                else:
-                    nc.vector.tensor_copy(pairs[c][:, 1, : GROUP - 2, 0], window[j][:, cols][:, : GROUP - 2])
-                    both = window[j][:, cols][:, GROUP - 4 :].unsqueeze(2).to_broadcast([P, 4, 2])
-                    nc.vector.tensor_copy(pairs[c][:, 1, GROUP - 4 :, :], both)
-        for c, cols in enumerate(CHUNKS):
-            if c == 0:
-                nc.vector.tensor_copy(pairs[c][:, 1, :, 1], window[LANES - 1][:, cols])
-            else:
-                nc.scalar.copy(pairs[c][:, 1, :, 1], window[LANES - 1][:, cols])
+        def round_plane(copy, j, cols):
+            copy(pairs[:, j // 2, cols, j % 2], window[j][:, cols])
+
+        def gpsimd_round(out, in_):
+            nc.gpsimd.tensor_scalar(out, in_, 1.0, 0.0, MULT, ADD)
+
+        for j in range(2):
+            round_plane(gpsimd_round, j, slice(0, GPSIMD_ROUNDS))
+        for j in range(2):
+            round_plane(nc.vector.tensor_copy, j, slice(GPSIMD_ROUNDS, TOKENS))
+        round_plane(nc.vector.tensor_copy, 2, slice(0, SPLIT))
+        round_plane(nc.scalar.copy, 2, slice(SPLIT, TOKENS))
+        for cols in (slice(0, GROUP), slice(GROUP, SPLIT)):
+            round_plane(nc.vector.tensor_copy, 3, cols)
+        for cols in (slice(SPLIT, TOKENS - GROUP), slice(TOKENS - GROUP, TOKENS)):
+            round_plane(nc.scalar.copy, 3, cols)
 
         words_out = out_1[0].rearrange("p c l -> p (c l)").bitcast(I32)
         y_scales = sb.tile([P, GROUP], U8, name="y_scales", align_bytes=64)
@@ -309,13 +317,9 @@ def tile_attend_gttt_k_pl_kernel(tc, kT, vT, W, ts, tk, cf, offs, out_0, out_1, 
         y_bf = [sb.tile([P, PIECE, LANES], BF16, name="y_bf%d" % b, align_bytes=64) for b in range(TOKENS // PIECE)]
 
         def weave(b):
-            c, first = divmod(PIECE * b, GROUP)
             y_words = y_bf[b][:].rearrange("p c t -> p (c t)").bitcast(F32).rearrange("p (c i u) -> p c u i", i=RUN, u=2)
-            pair_words = walk(pairs[c][:].rearrange("p u c e -> p u (c e)").bitcast(F32)[:, :, first : first + PIECE])
-            if PIECE * b < VECTOR_WEAVES:
-                nc.vector.tensor_copy(y_words, pair_words)
-            else:
-                nc.scalar.copy(y_words, pair_words)
+            copy = nc.vector.tensor_copy if PIECE * b < VECTOR_WEAVES else nc.scalar.copy
+            copy(y_words, walk(pair_words[:, :, PIECE * b : PIECE * (b + 1)]))
 
         def hand_on(b):
             g, first = divmod(PIECE * b, GROUP)
@@ -325,12 +329,12 @@ def tile_attend_gttt_k_pl_kernel(tc, kT, vT, W, ts, tk, cf, offs, out_0, out_1, 
                 if cols.stop == done:
                     nc.sync.dma_start(words_out[:, cols], y_codes[:, cols].bitcast(I32))
 
-        for g in range(GROUPS):
-            for b in (2 * g, 2 * g + 1):
+        pieces = TOKENS // PIECE
+        for b in range(pieces + 1):
+            if b < pieces:
                 weave(b)
-            for b in (2 * g, 2 * g + 1):
-                hand_on(b)
+            if b > 0:
+                hand_on(b - 1)
         for q in range(4):
             rows = out_2[0].bitcast(I32)[4 * q : 4 * q + 4, :].rearrange("r (g x) -> g r x", g=GROUPS)
-            queue = nc.scalar if q < 2 else nc.sync
-            queue.dma_start(rows, y_scales[32 * q : 32 * q + 16, :].bitcast(I32))
+            nc.sync.dma_start(rows, y_scales[32 * q : 32 * q + 16, :].bitcast(I32))

@@ -224,8 +224,8 @@ def tile_attend_gttt_k_pl_kernel(tc, kT, vT, W, ts, tk, cf, offs, out_0, out_1, 
         subtract_pair(0, half(0))
         for m in range(2):
             look_up_v(LANES - 1, slot_tile(m))
-        v_late = v_factor[:, LANES - 1, half(0)]
-        nc.scalar.activation(v_late, v_pool[LANES - 1][:].indirect(offsets[:, half(1, PER_COLUMN)]), COPY)
+        v_late = sb.tile([P, HALF], F32, name="v_late")
+        nc.scalar.activation(v_late[:], v_pool[LANES - 1][:].indirect(offsets[:, half(1, PER_COLUMN)]), COPY)
         e_bf = [v_term[:, LANES - 1, half(1)].bitcast(BF16).rearrange("p (c t) -> p c t", t=LANES)]
         for m in range(1, SLOT_TILES):
             e_bf.append(sb.tile([P, P, LANES], BF16, name="e_bf%d" % m, tag="e_bf%d" % m, align_bytes=64)[:])

@@ -200,7 +200,7 @@ def tile_attend_gttt_k_pl_kernel(tc, kT, vT, W, ts, tk, cf, offs, out_0, out_1, 
             values = v_pool[t][:].indirect(offsets[:, cols.start // PER_COLUMN : cols.stop // PER_COLUMN])
             nc.vector.tensor_tensor(v_term[:, t, cols], values, v_factor[:, t, cols], MULT)
 
-        e_pairs = placed.tile([P, 2, HALF, 2], BF16, name="e_pairs", offset=PLANE_BYTES * 2, align_bytes=64)
+        e_pairs = v_factor[:, 2, :].bitcast(BF16).rearrange("p (u c i) -> p u c i", u=2, i=2)
 
         def subtract_pair(u, cols):
             out = e_pairs[:, u, cols].rearrange("p (c i) t -> p c t i", i=RUN)
@@ -209,7 +209,7 @@ def tile_attend_gttt_k_pl_kernel(tc, kT, vT, W, ts, tk, cf, offs, out_0, out_1, 
 
         def weave_e(m):
             e_words = e_bf[m].rearrange("p c t -> p (c t)").bitcast(F32).rearrange("p (c i u) -> p c u i", i=RUN, u=2)
-            pair_words = e_pairs[:].rearrange("p u c e -> p u (c e)").bitcast(F32)
+            pair_words = e_pairs.rearrange("p u c e -> p u (c e)").bitcast(F32)
             nc.vector.tensor_copy(e_words, walk(pair_words[:, :, slot_tile(m)]))
 
         def subtract(m):
@@ -219,8 +219,10 @@ def tile_attend_gttt_k_pl_kernel(tc, kT, vT, W, ts, tk, cf, offs, out_0, out_1, 
         def quantize_e(m):
             quantize(nc, e_codes[:, slot_tile(m)], e_scales[:, slot_tile(m)], e_bf[m], E5M2)
 
-        for t in range(LANES - 1):
+        for t in range(2):
             look_up_v(t, slice(0, SLOTS))
+        for h in range(2):
+            look_up_v(2, half(h))
         subtract_pair(0, half(0))
         for m in range(2):
             look_up_v(LANES - 1, slot_tile(m))

@@ -37,7 +37,7 @@ KEYS_AT = 5 * PLANE_BYTES - 2048
 
 STORES = [slice(first, first + GROUP) for first in range(0, TOKENS, GROUP)]
 GPSIMD_ROUNDS = 1024
-SPLIT = 1152
+SPLIT = 1216
 VECTOR_WEAVES = 1024
 
 FLOPS = 2 * 2 * D * D * SLOTS
@@ -173,7 +173,10 @@ def tile_attend_gttt_k_pl_kernel(tc, kT, vT, W, ts, tk, cf, offs, out_0, out_1, 
             )
             u_scaled[m] = sb.tile([P, LANES, P], F32, name="u_scaled%d" % m, tag="from_psum%d" % m)
             nc.scalar.activation(u_scaled[m][:].rearrange("p t s -> p (t s)"), u_psum[:], COPY, scale=tstk2_col[:, m : m + 1])
-        u_term = sb.tile([P, LANES, SLOT_TILES, P], F32, name="u_term")
+        u_term = sb.tile([P, LANES, SLOTS], F32, name="u_term")
+        terms = sb.tile([P, HALF + LANES * SLOTS], F32, name="terms", align_bytes=64)
+        v_term = terms[:, HALF:].rearrange("p (t c) -> p t c", t=LANES)
+        u_late = terms[:].rearrange("p (i c) -> p i c", c=HALF)[:, 0 : 2 * LANES + 1 : 2 * LANES, :]
         for b in range(4):
             h, u = divmod(b, 2)
             tiles = half(h, P)
@@ -183,7 +186,8 @@ def tile_attend_gttt_k_pl_kernel(tc, kT, vT, W, ts, tk, cf, offs, out_0, out_1, 
                     nc.tensor.transpose(u_turned[:, i, n, :], u_scaled[m][:, 2 * u + i, :], ident[:])
             for i in range(2):
                 t = 2 * u + i
-                nc.scalar.activation(u_term[:, t, tiles, :], u_turned[:, i], COPY, scale=cf2[:, t : t + 1])
+                out = u_late[:, i] if b == 1 else u_term[:, t, half(h)]
+                nc.scalar.activation(out, u_turned[:, i].rearrange("p n s -> p (n s)"), COPY, scale=cf2[:, t : t + 1])
 
         window.append(window1)
         for j in range(2, LANES):
@@ -193,8 +197,6 @@ def tile_attend_gttt_k_pl_kernel(tc, kT, vT, W, ts, tk, cf, offs, out_0, out_1, 
         e_codes = sb.tile([P, SLOTS], U32, name="e_codes", align_bytes=64)
         e_scales = sb.tile([P, SLOTS], U8, name="e_scales", align_bytes=64)
 
-        v_term = sb.tile([P, LANES, SLOTS], F32, name="v_term", align_bytes=64)
-        u_flat = u_term[:].rearrange("p t m s -> p t (m s)")
 
         def look_up_v(t, cols):
             values = v_pool[t][:].indirect(offsets[:, cols.start // PER_COLUMN : cols.stop // PER_COLUMN])
@@ -204,8 +206,8 @@ def tile_attend_gttt_k_pl_kernel(tc, kT, vT, W, ts, tk, cf, offs, out_0, out_1, 
 
         def subtract_pair(u, cols):
             out = e_pairs[:, u, cols].rearrange("p (c i) t -> p c t i", i=RUN)
-            planes = slice(2 * u, 2 * u + 2)
-            nc.vector.tensor_tensor(out, walk(u_flat[:, planes, cols]), walk(v_term[:, planes, cols]), SUB)
+            u_pair = u_late if u == 1 else u_term[:, 0:2]
+            nc.vector.tensor_tensor(out, walk(u_pair[:, :, cols]), walk(v_term[:, 2 * u : 2 * u + 2, cols]), SUB)
 
         def weave_e(m):
             e_words = e_bf[m].rearrange("p c t -> p (c t)").bitcast(F32).rearrange("p (c i u) -> p c u i", i=RUN, u=2)
@@ -214,7 +216,7 @@ def tile_attend_gttt_k_pl_kernel(tc, kT, vT, W, ts, tk, cf, offs, out_0, out_1, 
 
         def subtract(m):
             out = e_bf[m].rearrange("p (c i) t -> p c t i", i=RUN)
-            nc.vector.tensor_tensor(out, walk(u_flat[:, :, slot_tile(m)]), walk(v_term[:, :, slot_tile(m)]), SUB)
+            nc.vector.tensor_tensor(out, walk(u_term[:, :, slot_tile(m)]), walk(v_term[:, :, slot_tile(m)]), SUB)
 
         def quantize_e(m):
             quantize(nc, e_codes[:, slot_tile(m)], e_scales[:, slot_tile(m)], e_bf[m], E5M2)
@@ -228,18 +230,15 @@ def tile_attend_gttt_k_pl_kernel(tc, kT, vT, W, ts, tk, cf, offs, out_0, out_1, 
             look_up_v(LANES - 1, slot_tile(m))
         v_late = sb.tile([P, HALF], F32, name="v_late")
         nc.scalar.activation(v_late[:], v_pool[LANES - 1][:].indirect(offsets[:, half(1, PER_COLUMN)]), COPY)
-        e_bf = [v_term[:, LANES - 1, half(1)].bitcast(BF16).rearrange("p (c t) -> p c t", t=LANES)]
-        for m in range(1, SLOT_TILES):
-            e_bf.append(sb.tile([P, P, LANES], BF16, name="e_bf%d" % m, tag="e_bf%d" % m, align_bytes=64)[:])
+        e_bf = [sb.tile([P, P, LANES], BF16, name="e_bf%d" % m, tag="e_bf%d" % m, align_bytes=64)[:] for m in range(SLOT_TILES)]
         for m in range(2):
             subtract_pair(1, slot_tile(m))
         for m in range(2):
             weave_e(m)
+            cols = slot_tile(2 + m)
+            nc.vector.tensor_tensor(v_term[:, LANES - 1, cols], v_late[:, slot_tile(m)], v_factor[:, LANES - 1, cols], MULT)
         for m in range(2):
             quantize_e(m)
-        for m in range(2, SLOT_TILES):
-            late = v_late[:, slot_tile(m - 2)]
-            nc.vector.tensor_tensor(v_term[:, LANES - 1, slot_tile(m)], late, v_factor[:, LANES - 1, slot_tile(m)], MULT)
         for m in range(2, SLOT_TILES):
             subtract(m)
         for m in range(2, SLOT_TILES):

@@ -140,7 +140,7 @@ def tile_attend_gttt_k_pl_kernel(tc, kT, vT, W, ts, tk, cf, offs, out_0, out_1, 
             nc.scalar.copy(w_f[:, 2 * u : 2 * u + 2, :, :], unpacked)
 
         k_bf = placed.tile([P, SLOTS, LANES], BF16, name="k_bf", offset=KEYS_AT, align_bytes=64)
-        k_low = sb.tile([P, 2, SLOTS], BF16, name="k_low", tag="k_low")
+        k_low = sb.tile([P, 2, SLOTS], BF16, name="k_low", tag="k_low", align_bytes=64)
         nc.vector.tensor_copy(k_low[:, 0, :], k_pool[0][:].indirect(offsets[:]))
 
         wd_codes, wd_scales = operand("wd", "wd_codes")
@@ -151,7 +151,7 @@ def tile_attend_gttt_k_pl_kernel(tc, kT, vT, W, ts, tk, cf, offs, out_0, out_1, 
             nc.tensor.transpose(tstk_row[:, P * m : P * (m + 1)], tstk_col[:, m : m + 1].to_broadcast([P, P]), ident[:])
         nc.vector.tensor_copy(k_low[:, 1, :], k_pool[1][:].indirect(offsets[:]))
         nc.scalar.copy(k_bf[:, :, 0:2], k_low[:].rearrange("p i c -> p c i"))
-        v_factor = sb.tile([P, LANES, SLOTS], F32, name="v_factor", tag="k_low")
+        v_factor = sb.tile([P, LANES, SLOTS], F32, name="v_factor", tag="k_low", align_bytes=64)
         for t in range(LANES):
             nc.scalar.activation(v_factor[:, t, :], tstk_row[:], COPY, scale=cf_sb[:, t : t + 1])
         nc.vector.tensor_copy(k_bf[:, :, 2], k_pool[2][:].indirect(offsets[:]))
@@ -202,17 +202,12 @@ def tile_attend_gttt_k_pl_kernel(tc, kT, vT, W, ts, tk, cf, offs, out_0, out_1, 
             values = v_pool[t][:].indirect(offsets[:, cols.start // PER_COLUMN : cols.stop // PER_COLUMN])
             nc.vector.tensor_tensor(v_term[:, t, cols], values, v_factor[:, t, cols], MULT)
 
-        e_pairs = v_factor[:, 2, :].bitcast(BF16).rearrange("p (u c i) -> p u c i", u=2, i=2)
+        e_first = v_factor[:].rearrange("p t c -> p (t c)")[:, 3 * HALF : 5 * HALF].bitcast(BF16).rearrange("p (c t) -> p c t", t=LANES)
 
         def subtract_pair(u, cols):
-            out = e_pairs[:, u, cols].rearrange("p (c i) t -> p c t i", i=RUN)
+            out = e_first[:, cols, 2 * u : 2 * u + 2].rearrange("p (c i) t -> p c t i", i=RUN)
             u_pair = u_late if u == 1 else u_term[:, 0:2]
             nc.vector.tensor_tensor(out, walk(u_pair[:, :, cols]), walk(v_term[:, 2 * u : 2 * u + 2, cols]), SUB)
-
-        def weave_e(m):
-            e_words = e_bf[m].rearrange("p c t -> p (c t)").bitcast(F32).rearrange("p (c i u) -> p c u i", i=RUN, u=2)
-            pair_words = e_pairs.rearrange("p u c e -> p u (c e)").bitcast(F32)
-            nc.vector.tensor_copy(e_words, walk(pair_words[:, :, slot_tile(m)]))
 
         def subtract(m):
             out = e_bf[m].rearrange("p (c i) t -> p c t i", i=RUN)
@@ -230,15 +225,15 @@ def tile_attend_gttt_k_pl_kernel(tc, kT, vT, W, ts, tk, cf, offs, out_0, out_1, 
             look_up_v(LANES - 1, slot_tile(m))
         v_late = sb.tile([P, HALF], F32, name="v_late")
         nc.scalar.activation(v_late[:], v_pool[LANES - 1][:].indirect(offsets[:, half(1, PER_COLUMN)]), COPY)
-        e_bf = [sb.tile([P, P, LANES], BF16, name="e_bf%d" % m, tag="e_bf%d" % m, align_bytes=64)[:] for m in range(SLOT_TILES)]
+        e_bf = [e_first[:, slot_tile(m)] for m in range(2)]
+        e_bf.extend(sb.tile([P, P, LANES], BF16, name="e_bf%d" % m, tag="e_bf%d" % m, align_bytes=64)[:] for m in range(2, SLOT_TILES))
         for m in range(2):
             subtract_pair(1, slot_tile(m))
         for m in range(2):
-            weave_e(m)
+            quantize_e(m)
+        for m in range(2):
             cols = slot_tile(2 + m)
             nc.vector.tensor_tensor(v_term[:, LANES - 1, cols], v_late[:, slot_tile(m)], v_factor[:, LANES - 1, cols], MULT)
-        for m in range(2):
-            quantize_e(m)
         for m in range(2, SLOT_TILES):
             subtract(m)
         for m in range(2, SLOT_TILES):

@@ -35,7 +35,6 @@ PIECE = 256
 PLANE_BYTES = 4 * TOKENS
 KEYS_AT = 5 * PLANE_BYTES - 2048
 
-STORES = [slice(first, first + GROUP) for first in range(0, TOKENS, GROUP)]
 GPSIMD_ROUNDS = 1024
 SPLIT = 1216
 VECTOR_WEAVES = 1024
@@ -309,7 +308,8 @@ def tile_attend_gttt_k_pl_kernel(tc, kT, vT, W, ts, tk, cf, offs, out_0, out_1, 
 
         words_out = out_1[0].rearrange("p c l -> p (c l)").bitcast(I32)
         y_scales = sb.tile([P, GROUP], U8, name="y_scales", align_bytes=64)
-        y_codes = sb.tile([P, TOKENS], U32, name="y_codes", align_bytes=64)
+        y_codes = [sb.tile([P, GROUP], U32, name="y_codes%d" % g, align_bytes=64) for g in range(GROUPS - 1)]
+        y_codes.append(placed.tile([P, GROUP], U32, name="y_codes_last", offset=PLANE_BYTES * 4, align_bytes=64))
         y_bf = [sb.tile([P, PIECE, LANES], BF16, name="y_bf%d" % b, align_bytes=64) for b in range(TOKENS // PIECE)]
 
         def weave(b):
@@ -319,11 +319,9 @@ def tile_attend_gttt_k_pl_kernel(tc, kT, vT, W, ts, tk, cf, offs, out_0, out_1, 
 
         def hand_on(b):
             g, first = divmod(PIECE * b, GROUP)
-            done = PIECE * (b + 1)
-            quantize(nc, y_codes[:, done - PIECE : done], y_scales[4 * g : P, first : first + PIECE], y_bf[b][:], E4M3)
-            for cols in STORES:
-                if cols.stop == done:
-                    nc.sync.dma_start(words_out[:, cols], y_codes[:, cols].bitcast(I32))
+            quantize(nc, y_codes[g][:, first : first + PIECE], y_scales[4 * g : P, first : first + PIECE], y_bf[b][:], E4M3)
+            if first + PIECE == GROUP:
+                nc.sync.dma_start(words_out[:, GROUP * g : GROUP * (g + 1)], y_codes[g][:].bitcast(I32))
 
         pieces = TOKENS // PIECE
         for b in range(pieces + 1):
@@ -333,4 +331,5 @@ def tile_attend_gttt_k_pl_kernel(tc, kT, vT, W, ts, tk, cf, offs, out_0, out_1, 
                 hand_on(b - 1)
         for q in range(4):
             rows = out_2[0].bitcast(I32)[4 * q : 4 * q + 4, :].rearrange("r (g x) -> g r x", g=GROUPS)
-            nc.sync.dma_start(rows, y_scales[32 * q : 32 * q + 16, :].bitcast(I32))
+            queue = nc.scalar if q < 2 else nc.sync
+            queue.dma_start(rows, y_scales[32 * q : 32 * q + 16, :].bitcast(I32))

from contextlib import ExitStack

import concourse.mybir as mybir
from concourse.masks import make_identity

F32 = mybir.dt.float32
BF16 = mybir.dt.bfloat16
I32 = mybir.dt.int32
U32 = mybir.dt.uint32
U16 = mybir.dt.uint16
U8 = mybir.dt.uint8
E4M3 = mybir.dt.float8_e4m3fn_x4
E5M2 = mybir.dt.float8_e5m2_x4
COPY = mybir.ActivationFunctionType.Copy
MULT = mybir.AluOpType.mult
SUB = mybir.AluOpType.subtract
ADD = mybir.AluOpType.add

P = 128
LANES = 4
D = 512
SLOTS = 512
TOKENS = 2048
SLOT_TILES = SLOTS // P
HALF = SLOTS // 2
RUN = 4
PER_COLUMN = 16
TK_ROW = P - 1
TS_ROW = P // 2 - 1

GROUPS = 4
GROUP = TOKENS // GROUPS

PIECE = 256
PLANE_BYTES = 4 * TOKENS
KEYS_AT = 5 * PLANE_BYTES - 2048

GPSIMD_ROUNDS = 1024
SPLIT = 1216
VECTOR_WEAVES = 1024

FLOPS = 2 * 2 * D * D * SLOTS
BYTES = 4 * (3 * D * TOKENS + D * D + 2 * TOKENS + D) + 2 * P * SLOTS // PER_COLUMN + D * TOKENS + D // 32 * TOKENS


def half(h, per=1):
    return slice(HALF // per * h, HALF // per * (h + 1))


def slot_tile(m):
    return slice(P * m, P * (m + 1))


def walk(planes):
    return planes.rearrange("p t (c i) -> p c t i", i=RUN)


def quantize(nc, codes, scales, grouped, fmt):
    nc.vector.quantize_mx(out=codes.bitcast(fmt), scales=scales, in_=grouped.rearrange("p c t -> p (c t)"))


def tile_attend_gttt_k_pl_kernel(tc, kT, vT, W, ts, tk, cf, offs, out_0, out_1, out_2):
    nc = tc.nc
    with ExitStack() as ctx:
        sb = ctx.enter_context(tc.tile_pool(name="sb", bufs=1))
        ps = ctx.enter_context(tc.psum_pool(name="ps", bufs=1))
        placed = ctx.enter_context(tc.tile_pool(name="placed", bufs=1))

        def bank(b, name, shape):
            return ps.tile(shape, F32, name=name, tag="bank%d" % b)

        def operand(name, tag):
            codes = sb.tile([P, 512], U32, name=name + "_codes", tag=tag, align_bytes=64)
            scales = sb.tile([P, 512], U8, name=name + "_scales", align_bytes=64)
            return codes, scales

        offsets = sb.tile([P, SLOTS // PER_COLUMN], U16, name="offsets")
        tk_pool = sb.tile([P, TOKENS], F32, name="tk_pool", tag="then_window0", align_bytes=64)
        ts_pool = sb.tile([P, TOKENS], F32, name="ts_pool")
        cf_sb = sb.tile([P, LANES], F32, name="cf_sb")
        nc.scalar.dma_start(tk_pool[TK_ROW : TK_ROW + 1, :], tk[0:1, :])
        nc.scalar.dma_start(ts_pool[TS_ROW : TS_ROW + 1, :], ts[0:1, :])
        nc.scalar.dma_start(cf_sb[:], cf.rearrange("(p t) o -> p (t o)", t=LANES))
        w_raw = sb.tile([P, LANES, D], F32, name="w_raw")
        nc.sync.dma_start(w_raw[:], W.rearrange("(p j) f -> p j f", j=LANES))
        nc.sync.dma_start(offsets[:], offs)
        k_pool = [sb.tile([P, TOKENS], F32, name="k_pool%d" % j, tag="k_pool%d" % j, align_bytes=64) for j in range(LANES)]
        v_pool = [placed.tile([P, TOKENS], F32, name="v_pool%d" % t, offset=PLANE_BYTES * t, align_bytes=64) for t in range(LANES)]
        for j in range(LANES):
            nc.sync.dma_start(k_pool[j][:], kT.rearrange("(p j) c -> p j c", j=LANES)[:, j, :])
        for t in range(LANES):
            nc.sync.dma_start(v_pool[t][:], vT.rearrange("(p t) c -> p t c", t=LANES)[:, t, :])

        ident = sb.tile([P, P], F32, name="ident")
        make_identity(nc, ident[:])

        nc.vector.memset(tk_pool[0:TK_ROW, :], 0.0)
        nc.vector.memset(ts_pool[0:TS_ROW, :], 0.0)
        nc.gpsimd.memset(ts_pool[TS_ROW + 1 : P, :], 0.0)
        window1 = sb.tile([P, TOKENS], F32, name="window1", align_bytes=64)
        nc.gpsimd.memset(window1[:], 0.0)

        w_d = placed.tile([P, D, LANES], BF16, name="w_d", offset=KEYS_AT, align_bytes=64)
        nc.scalar.activation(
            w_d[:].rearrange("p (t s) j -> p s t j", t=LANES), w_raw[:].rearrange("p j (s t) -> p s t j", t=LANES), COPY
        )

        tk_g = sb.tile([P, SLOTS], F32, name="tk_g")
        ts_g = sb.tile([P, SLOTS], F32, name="ts_g")
        nc.vector.tensor_copy(tk_g[:], tk_pool[:].indirect(offsets[:]))
        nc.vector.tensor_copy(ts_g[:], ts_pool[:].indirect(offsets[:]))
        window = [sb.tile([P, TOKENS], F32, name="window0", tag="then_window0", align_bytes=64)]
        nc.gpsimd.memset(window[0][:], 0.0)
        tk_turned = bank(4, "tk_turned", [P, SLOT_TILES, P])
        ts_turned = bank(5, "ts_turned", [P, SLOT_TILES, P])
        for m in range(SLOT_TILES):
            nc.tensor.transpose(tk_turned[:, m, :], tk_g[:, P * m : P * (m + 1)], ident[:])
        for m in range(SLOT_TILES):
            nc.tensor.transpose(ts_turned[:, m, :], ts_g[:, P * m : P * (m + 1)], ident[:])

        tk_col = sb.tile([P, SLOT_TILES], F32, name="tk_col")
        ts_col = sb.tile([P, SLOT_TILES], F32, name="ts_col")
        tstk_col = sb.tile([P, SLOT_TILES], F32, name="tstk_col")
        tstk2_col = sb.tile([P, SLOT_TILES], F32, name="tstk2_col")
        cf2 = sb.tile([P, LANES], F32, name="cf2")
        nc.scalar.copy(tk_col[:], tk_turned[:, :, TK_ROW])
        nc.scalar.copy(ts_col[:], ts_turned[:, :, TS_ROW])
        nc.gpsimd.tensor_tensor(cf2[:], cf_sb[:], cf_sb[:], MULT)
        nc.gpsimd.tensor_tensor(tstk_col[:], ts_col[:], tk_col[:], MULT)
        nc.gpsimd.tensor_tensor(tstk2_col[:], tstk_col[:], tk_col[:], MULT)

        w_f = sb.tile([P, LANES, P, LANES], BF16, name="w_f", align_bytes=64)
        w_words = w_d[:].rearrange("p c j -> p (c j)").bitcast(F32).rearrange("p (t s u) -> p t u s", t=LANES, u=2)
        for u in range(2):
            w_turned = bank(u, "w_turned%d" % u, [P, LANES, P])
            for t in range(LANES):
                nc.tensor.transpose(w_turned[:, t, :], w_words[:, t, u, :], ident[:])
            unpacked = w_turned[:].rearrange("p t s -> p (t s)").bitcast(BF16).rearrange("p (t s i) -> p i s t", t=LANES, i=2)
            nc.scalar.copy(w_f[:, 2 * u : 2 * u + 2, :, :], unpacked)

        k_bf = placed.tile([P, SLOTS, LANES], BF16, name="k_bf", offset=KEYS_AT, align_bytes=64)
        k_low = sb.tile([P, 2, SLOTS], BF16, name="k_low", tag="k_low", align_bytes=64)
        nc.vector.tensor_copy(k_low[:, 0, :], k_pool[0][:].indirect(offsets[:]))

        wd_codes, wd_scales = operand("wd", "wd_codes")
        quantize(nc, wd_codes[:], wd_scales[:], w_d[:], E4M3)

        tstk_row = bank(6, "tstk_row", [P, SLOTS])
        for m in range(SLOT_TILES):
            nc.tensor.transpose(tstk_row[:, P * m : P * (m + 1)], tstk_col[:, m : m + 1].to_broadcast([P, P]), ident[:])
        nc.vector.tensor_copy(k_low[:, 1, :], k_pool[1][:].indirect(offsets[:]))
        nc.scalar.copy(k_bf[:, :, 0:2], k_low[:].rearrange("p i c -> p c i"))
        v_factor = sb.tile([P, LANES, SLOTS], F32, name="v_factor", tag="k_low", align_bytes=64)
        for t in range(LANES):
            nc.scalar.activation(v_factor[:, t, :], tstk_row[:], COPY, scale=cf_sb[:, t : t + 1])
        nc.vector.tensor_copy(k_bf[:, :, 2], k_pool[2][:].indirect(offsets[:]))
        wf_codes, wf_scales = operand("wf", "k_pool2")
        quantize(nc, wf_codes[:], wf_scales[:], w_f[:].rearrange("p j s t -> p (j s) t"), E4M3)
        for h in range(2):
            nc.vector.tensor_copy(k_bf[:, half(h), LANES - 1], k_pool[LANES - 1][:].indirect(offsets[:, half(h, PER_COLUMN)]))
        k_codes, k_scales = operand("k", "k_codes")
        for h in range(2):
            quantize(nc, k_codes[:, half(h)], k_scales[:, half(h)], k_bf[:, half(h), :], E4M3)

        u_scaled = {}
        for m in range(SLOT_TILES):
            cols = slice(P * m, P * (m + 1))
            u_psum = bank(m, "u_psum%d" % m, [P, D])
            nc.tensor.matmul_mx(
                u_psum[:], lhsT=k_codes[:, cols].bitcast(E4M3), lhsT_scale=k_scales[:, cols],
                rhs=wd_codes[:].bitcast(E4M3), rhs_scale=wd_scales[:], start=True, stop=True,
            )
            u_scaled[m] = sb.tile([P, LANES, P], F32, name="u_scaled%d" % m, tag="from_psum%d" % m)
            nc.scalar.activation(u_scaled[m][:].rearrange("p t s -> p (t s)"), u_psum[:], COPY, scale=tstk2_col[:, m : m + 1])
        u_term = sb.tile([P, LANES, SLOTS], F32, name="u_term")
        terms = sb.tile([P, HALF + LANES * SLOTS], F32, name="terms", align_bytes=64)
        v_term = terms[:, HALF:].rearrange("p (t c) -> p t c", t=LANES)
        u_late = terms[:].rearrange("p (i c) -> p i c", c=HALF)[:, 0 : 2 * LANES + 1 : 2 * LANES, :]
        for b in range(4):
            h, u = divmod(b, 2)
            tiles = half(h, P)
            u_turned = bank(SLOT_TILES + b, "u_turned%d" % b, [P, 2, 2, P])
            for i in range(2):
                for n, m in enumerate(range(SLOT_TILES)[tiles]):
                    nc.tensor.transpose(u_turned[:, i, n, :], u_scaled[m][:, 2 * u + i, :], ident[:])
            for i in range(2):
                t = 2 * u + i
                out = u_late[:, i] if b == 1 else u_term[:, t, half(h)]
                nc.scalar.activation(out, u_turned[:, i].rearrange("p n s -> p (n s)"), COPY, scale=cf2[:, t : t + 1])

        window.append(window1)
        for j in range(2, LANES):
            window.append(placed.tile([P, TOKENS], F32, name="window%d" % j, offset=PLANE_BYTES * (2 + j), align_bytes=64))
            nc.gpsimd.memset(window[j][:], 0.0)

        e_codes = sb.tile([P, SLOTS], U32, name="e_codes", align_bytes=64)
        e_scales = sb.tile([P, SLOTS], U8, name="e_scales", align_bytes=64)


        def look_up_v(t, cols):
            values = v_pool[t][:].indirect(offsets[:, cols.start // PER_COLUMN : cols.stop // PER_COLUMN])
            nc.vector.tensor_tensor(v_term[:, t, cols], values, v_factor[:, t, cols], MULT)

        e_first = v_factor[:].rearrange("p t c -> p (t c)")[:, 3 * HALF : 5 * HALF].bitcast(BF16).rearrange("p (c t) -> p c t", t=LANES)

        def subtract_pair(u, cols):
            out = e_first[:, cols, 2 * u : 2 * u + 2].rearrange("p (c i) t -> p c t i", i=RUN)
            u_pair = u_late if u == 1 else u_term[:, 0:2]
            nc.vector.tensor_tensor(out, walk(u_pair[:, :, cols]), walk(v_term[:, 2 * u : 2 * u + 2, cols]), SUB)

        def subtract(m):
            out = e_bf[m].rearrange("p (c i) t -> p c t i", i=RUN)
            nc.vector.tensor_tensor(out, walk(u_term[:, :, slot_tile(m)]), walk(v_term[:, :, slot_tile(m)]), SUB)

        def quantize_e(m):
            quantize(nc, e_codes[:, slot_tile(m)], e_scales[:, slot_tile(m)], e_bf[m], E5M2)

        for t in range(2):
            look_up_v(t, slice(0, SLOTS))
        for h in range(2):
            look_up_v(2, half(h))
        subtract_pair(0, half(0))
        for m in range(2):
            look_up_v(LANES - 1, slot_tile(m))
        v_late = sb.tile([P, HALF], F32, name="v_late")
        nc.scalar.activation(v_late[:], v_pool[LANES - 1][:].indirect(offsets[:, half(1, PER_COLUMN)]), COPY)
        e_bf = [e_first[:, slot_tile(m)] for m in range(2)]
        e_bf.extend(sb.tile([P, P, LANES], BF16, name="e_bf%d" % m, tag="e_bf%d" % m, align_bytes=64)[:] for m in range(2, SLOT_TILES))
        for m in range(2):
            subtract_pair(1, slot_tile(m))
        for m in range(2):
            quantize_e(m)
        for m in range(2):
            cols = slot_tile(2 + m)
            nc.vector.tensor_tensor(v_term[:, LANES - 1, cols], v_late[:, slot_tile(m)], v_factor[:, LANES - 1, cols], MULT)
        for m in range(2, SLOT_TILES):
            subtract(m)
        for m in range(2, SLOT_TILES):
            quantize_e(m)

        def dk_passes(b, planes, cols):
            products = bank(b, "dk_psum%d" % b, [P, len(planes), cols.stop - cols.start])
            for n, j in enumerate(planes):
                nc.tensor.matmul_mx(
                    products[:, n, :], lhsT=wf_codes[:, P * j : P * (j + 1)].bitcast(E4M3), lhsT_scale=wf_scales[:, P * j : P * (j + 1)],
                    rhs=e_codes[:, cols].bitcast(E5M2), rhs_scale=e_scales[:, cols], start=True, stop=True,
                )
            return products

        first_psum = [dk_passes(b, [0], slot_tile(m)) for m, b in enumerate((0, 7))]
        first1_psum = dk_passes(1, [1], half(0))
        first23_psum = dk_passes(2, [2, 3], half(0))
        second_psum = [dk_passes(3 + j, [j], half(1)) for j in range(LANES)]
        first01 = sb.tile([P, 2, HALF], F32, name="first01", tag="from_psum0")
        first23 = sb.tile([P, 2, HALF], F32, name="first23", tag="e_bf3", align_bytes=64)
        pairs = sb.tile([P, 2, TOKENS, 2], BF16, name="pairs", align_bytes=64)
        pair_words = pairs[:].rearrange("p u c e -> p u (c e)").bitcast(F32)
        second0 = sb.tile([P, HALF], F32, name="second0")
        for_scalar = pair_words[:, 1, SPLIT : SPLIT + HALF]
        second = [second0[:], for_scalar, pair_words[:, 0, GPSIMD_ROUNDS : GPSIMD_ROUNDS + HALF], for_scalar]
        dk = [[first01[:, 0], first01[:, 1], first23[:, 0], first23[:, 1]], second]

        def listed(j, h):
            return window[j][:].indirect(offsets[:, half(h, PER_COLUMN)])

        def store(j):
            nc.sync.dma_start(out_0.rearrange("(p j) c -> p j c", j=LANES)[:, j, :], window[j][:])

        def copy_second(j):
            nc.vector.tensor_copy(second[j], second_psum[j][:, 0])

        for m in range(2):
            nc.scalar.copy(first01[:, 0:1, slot_tile(m)], first_psum[m][:])
        nc.scalar.activation(listed(0, 0), dk[0][0], COPY)
        nc.vector.tensor_copy(first23[:], first23_psum[:])
        copy_second(0)
        copy_second(1)
        nc.vector.tensor_copy(listed(0, 1), dk[1][0])
        store(0)
        nc.scalar.copy(first01[:, 1:2], first1_psum[:])
        for j in range(1, LANES):
            nc.scalar.activation(listed(j, 0), dk[0][j], COPY)
        nc.vector.tensor_copy(listed(1, 1), dk[1][1])
        store(1)
        copy_second(2)
        nc.scalar.copy(second[3], second_psum[3][:, 0])
        nc.vector.tensor_copy(listed(2, 1), dk[1][2])
        store(2)
        nc.scalar.activation(listed(3, 1), dk[1][3], COPY)
        store(3)

        def round_plane(copy, j, cols):
            copy(pairs[:, j // 2, cols, j % 2], window[j][:, cols])

        def gpsimd_round(out, in_):
            nc.gpsimd.tensor_scalar(out, in_, 1.0, 0.0, MULT, ADD)

        for j in range(2):
            round_plane(gpsimd_round, j, slice(0, GPSIMD_ROUNDS))
        for j in range(2):
            round_plane(nc.vector.tensor_copy, j, slice(GPSIMD_ROUNDS, TOKENS))
        round_plane(nc.vector.tensor_copy, 2, slice(0, SPLIT))
        round_plane(nc.scalar.copy, 2, slice(SPLIT, TOKENS))
        for cols in (slice(0, GROUP), slice(GROUP, SPLIT)):
            round_plane(nc.vector.tensor_copy, 3, cols)
        for cols in (slice(SPLIT, TOKENS - GROUP), slice(TOKENS - GROUP, TOKENS)):
            round_plane(nc.scalar.copy, 3, cols)

        words_out = out_1[0].rearrange("p c l -> p (c l)").bitcast(I32)
        y_scales = sb.tile([P, GROUP], U8, name="y_scales", align_bytes=64)
        y_codes = [sb.tile([P, GROUP], U32, name="y_codes%d" % g, align_bytes=64) for g in range(GROUPS - 1)]
        y_codes.append(placed.tile([P, GROUP], U32, name="y_codes_last", offset=PLANE_BYTES * 4, align_bytes=64))
        y_bf = [sb.tile([P, PIECE, LANES], BF16, name="y_bf%d" % b, align_bytes=64) for b in range(TOKENS // PIECE)]

        def weave(b):
            y_words = y_bf[b][:].rearrange("p c t -> p (c t)").bitcast(F32).rearrange("p (c i u) -> p c u i", i=RUN, u=2)
            copy = nc.vector.tensor_copy if PIECE * b < VECTOR_WEAVES else nc.scalar.copy
            copy(y_words, walk(pair_words[:, :, PIECE * b : PIECE * (b + 1)]))

        def hand_on(b):
            g, first = divmod(PIECE * b, GROUP)
            quantize(nc, y_codes[g][:, first : first + PIECE], y_scales[4 * g : P, first : first + PIECE], y_bf[b][:], E4M3)
            if first + PIECE == GROUP:
                nc.sync.dma_start(words_out[:, GROUP * g : GROUP * (g + 1)], y_codes[g][:].bitcast(I32))

        pieces = TOKENS // PIECE
        for b in range(pieces + 1):
            if b < pieces:
                weave(b)
            if b > 0:
                hand_on(b - 1)
        for q in range(4):
            rows = out_2[0].bitcast(I32)[4 * q : 4 * q + 4, :].rearrange("r (g x) -> g r x", g=GROUPS)
            queue = nc.scalar if q < 2 else nc.sync
            queue.dma_start(rows, y_scales[32 * q : 32 * q + 16, :].bitcast(I32))
